import numpy as np
import ml_dtypes


def mxq(x, axis, fmt="e4m3"):
    dtype, down = {"e4m3": (ml_dtypes.float8_e4m3fn, 7), "e5m2": (ml_dtypes.float8_e5m2, 14)}[fmt]
    v = np.moveaxis(np.asarray(x, np.float32).astype(ml_dtypes.bfloat16).astype(np.float64), axis, -1)
    blocks = v.reshape(v.shape[:-1] + (-1, 32))
    amax = np.abs(blocks).max(-1, keepdims=True)
    byte = np.maximum(np.where(amax > 0, np.frexp(amax)[1] - 1 + 127, 0) - down, 1)
    scale = np.exp2(byte - 127.0)
    codes = (blocks / scale).astype(np.float32).astype(dtype).astype(np.float64)
    return np.moveaxis((codes * scale).reshape(v.shape), -1, axis)


WIDE = False


def mx_kscale(k):
    if not WIDE:
        return np.ones(k)
    levels = np.array([10, -10, 5, -5, 0])
    if k % 512:
        return np.exp2(np.random.permutation(np.resize(levels, k // 32))).repeat(32)
    a = np.empty((k // 512, 16))
    for p in range(k // 512):
        a[p, :8] = np.random.permutation(np.resize(levels, 8))
        for g in range(8):
            far = levels[np.abs(levels - a[p, g]) >= 10]
            a[p, g + 8] = far[np.random.randint(len(far))]
    return np.exp2(a.ravel()).repeat(32)


BF16 = ml_dtypes.bfloat16


def bf(x):
    return np.asarray(x, np.float32).astype(BF16)


def f64(x):
    return np.asarray(x).astype(np.float64)

E4M3FN = np.array([(-1.0 if i & 128 else 1.0) * ((1.0 + (i & 7) / 8.0) * 2.0 ** (((i >> 3) & 15) - 7) if i & 120 else (i & 7) * 2.0 ** -9) for i in range(256)])


def e4m3fn_bytes(y):
    return np.clip(np.asarray(y, np.float64), -448.0, 448.0).astype(np.float32).astype(ml_dtypes.float8_e4m3fn).view(np.uint8)


def e4m3fn_values(b):
    return E4M3FN[b]


T, K, N, R, G = 1024, 2048, 1536, 512, 128


def setup_inputs():
    s, t = mx_kscale(K), mx_kscale(R)
    x = np.random.standard_normal((T, K)) * np.random.uniform(0.5, 1.5, (T, 1)) * s
    c = np.random.uniform(0.5, 1.5, (K // G, N // G))
    w0 = np.random.standard_normal((K, N)) / np.sqrt(K) * np.repeat(np.repeat(c, G, 0), G, 1) * np.random.uniform(0.5, 1.5, N)
    b0 = 0.5 * np.random.standard_normal((R, N)) / np.sqrt(R)
    lam = 1 + 0.2 * np.random.standard_normal(R)
    norm = np.sqrt((w0 ** 2).sum(0) + ((lam[:, None] * b0) ** 2).sum(0))
    w = w0 / s[:, None]
    x_scale = (np.abs(x).reshape(T, K // G, G).max(2) / 448).astype(np.float32)
    w_scale = (np.abs(w).reshape(K // G, G, N // G, G).max((1, 3)) / 448).astype(np.float32)
    return {"x_bytes": e4m3fn_bytes(x / np.repeat(f64(x_scale), G, 1)),
            "x_scale": x_scale,
            "w_bytes": e4m3fn_bytes(w / np.repeat(np.repeat(f64(w_scale), G, 0), G, 1)),
            "w_scale": w_scale,
            "a": bf(np.random.standard_normal((K, R)) / np.sqrt(K) / s[:, None] * t),
            "lam": bf(lam),
            "b": bf(b0 / t[:, None]),
            "mag": bf(norm * np.random.uniform(0.6, 1.4, N)),
            "norm": bf(norm)}


def reference(x_bytes, x_scale, w_bytes, w_scale, a, lam, b, mag, norm):
    x = e4m3fn_values(x_bytes) * np.repeat(f64(x_scale), G, 1)
    w = e4m3fn_values(w_bytes) * np.repeat(np.repeat(f64(w_scale), G, 0), G, 1)
    xq = mxq(x, 1, "e4m3")
    base = xq @ mxq(w, 0, "e4m3")
    h = (xq @ mxq(f64(a), 0, "e4m3")) * f64(lam)
    delta = mxq(h, 1, "e4m3") @ mxq(f64(b), 0, "e4m3")
    return (base + delta) * (f64(mag) / f64(norm))

@@ -1,0 +1,392 @@
+from contextlib import ExitStack
+
+import concourse.mybir as mybir
+from concourse.masks import make_identity
+
+T, K, N, R = 1024, 2048, 1536, 512
+FLOPS = 2 * T * (K * N + K * R + R * N)
+
+F32 = mybir.dt.float32
+BF16 = mybir.dt.bfloat16
+U32 = mybir.dt.uint32
+U8 = mybir.dt.uint8
+E4M3 = mybir.dt.float8_e4m3fn
+MX = mybir.dt.float8_e4m3fn_x4
+MULT = mybir.AluOpType.mult
+COPY = mybir.ActivationFunctionType.Copy
+
+P = 128
+G = K // 512
+TILES = T // P
+PAIRS = TILES // 2
+CW = 512
+C = N // CW
+
+
+def tile_dora_fp8_forward_d2_kernel(tc, x_bytes, x_scale, w_bytes, w_scale, a, lam, b, mag, norm, out):
+    nc = tc.nc
+    with ExitStack() as ctx:
+        keep = ctx.enter_context(tc.tile_pool(name="keep", bufs=1))
+        agp = ctx.enter_context(tc.tile_pool(name="agp", bufs=2))
+        xwp = ctx.enter_context(tc.tile_pool(name="xwp", bufs=4))
+        xgp = ctx.enter_context(tc.tile_pool(name="xgp", bufs=4))
+        wwp = ctx.enter_context(tc.tile_pool(name="wwp", bufs=4))
+        wgp = ctx.enter_context(tc.tile_pool(name="wgp", bufs=4))
+        hp = ctx.enter_context(tc.tile_pool(name="hp", bufs=2))
+        resp = ctx.enter_context(tc.tile_pool(name="resp", bufs=8))
+        psum = ctx.enter_context(tc.psum_pool(name="psum", bufs=4))
+
+        def kept(shape, dtype, name):
+            return keep.tile(shape, dtype, name=name, align_bytes=64)
+
+        ident = kept([P, P], F32, "ident")
+        xs = kept([P, TILES, K // 128], F32, "xs")
+        wsall = kept([P, G, 4, N // 128], F32, "wsall")
+        ws = kept([P, G, N // 128], F32, "ws")
+        lamb = kept([P, 4], BF16, "lamb")
+        lamf = kept([P, 4], F32, "lamf")
+        magb = kept([P, N // P], BF16, "magb")
+        normb = kept([P, N // P], BF16, "normb")
+        rec = kept([P, N // P], F32, "rec")
+        s1 = kept([P, N // P], F32, "s1")
+        sb = kept([P, N], F32, "sb")
+        xb = [kept([P, 2, K], U8, f"xb{j}") for j in range(PAIRS)]
+        araw = [kept([P, 4, R], BF16, f"araw{g}") for g in range(G)]
+        wb = [kept([P, 4, CW], U8, f"wb{v}") for v in range(C * G)]
+        braw = [kept([P, 4, CW], BF16, f"braw{c}") for c in range(C)]
+        xq = kept([P, G, T], U32, "xq")
+        xqs = kept([P, G, T], U8, "xqs")
+        aq = kept([P, G, R], U32, "aq")
+        aqs = kept([P, G, R], U8, "aqs")
+        wq = [kept([P, CW], U32, f"wq{v}") for v in range(C * G)]
+        wqs = [kept([P, CW], U8, f"wqs{v}") for v in range(C * G)]
+        bq = [kept([P, CW], U32, f"bq{c}") for c in range(C)]
+        bqs = [kept([P, CW], U8, f"bqs{c}") for c in range(C)]
+        hq = kept([P, T], U32, "hq")
+        hqs = kept([P, T], U8, "hqs")
+
+        x_view = x_bytes.rearrange("(p i) k -> p i k", i=TILES)
+        a_view = a.rearrange("(g p t) r -> g p t r", p=P, t=4)
+        w_view = w_bytes.rearrange("(g p t) n -> g p t n", p=P, t=4)
+        b_view = b.rearrange("(p t) n -> p t n", t=4)
+        out_view = out.rearrange("(p i) n -> p i n", i=TILES)
+
+        nc.scalar.dma_start(out=xs[:], in_=x_scale.rearrange("(p i) k -> p i k", i=TILES))
+        make_identity(nc, ident[:])
+        nc.gpsimd.dma_start(out=lamb[:], in_=lam.rearrange("(p t) -> p t", t=4))
+        nc.gpsimd.dma_start(out=magb[:], in_=mag.rearrange("(p j) -> p j", j=N // P))
+        nc.gpsimd.dma_start(out=normb[:], in_=norm.rearrange("(p j) -> p j", j=N // P))
+        nc.gpsimd.dma_start(
+            out=wsall[:].rearrange("p g q n -> p (g q n)"),
+            in_=w_scale.rearrange("k n -> (k n)").partition_broadcast(P),
+        )
+        nc.gpsimd.tensor_copy(out=lamf[:], in_=lamb[:])
+        for q in range(4):
+            rows = slice(32 * q, 32 * q + 32)
+            nc.gpsimd.tensor_copy(out=ws[rows, :, :], in_=wsall[rows, :, q, :])
+
+        half = K // 2
+        nc.sync.dma_start(out=xb[0][:, :, 0:half], in_=x_view[:, 0:2, 0:half])
+        nc.sync.dma_start(out=araw[0][:], in_=a_view[0])
+        nc.sync.dma_start(out=xb[0][:, :, half:K], in_=x_view[:, 0:2, half:K])
+        nc.sync.dma_start(out=araw[1][:], in_=a_view[1])
+        nc.sync.dma_start(out=xb[1][:], in_=x_view[:, 2:4, :])
+        nc.sync.dma_start(out=araw[2][:], in_=a_view[2])
+        nc.sync.dma_start(out=araw[3][:], in_=a_view[3])
+        nc.sync.dma_start(out=xb[2][:], in_=x_view[:, 4:6, :])
+        nc.sync.dma_start(out=xb[3][:], in_=x_view[:, 6:8, :])
+        for c in range(C):
+            cols = slice(CW * c, CW * (c + 1))
+            for g in range(G):
+                nc.sync.dma_start(out=wb[G * c + g][:], in_=w_view[g][:, :, cols])
+                if g == 3:
+                    nc.sync.dma_start(out=braw[c][:], in_=b_view[:, :, cols])
+
+        xw, xbank, xg = {}, {}, {}
+
+        def x_widen(u):
+            j, g = divmod(u, G)
+            xw[u] = xwp.tile([P, 2, 512], BF16, name="xw", align_bytes=64)
+            for i in range(2):
+                for q in range(4):
+                    k = 512 * g + 128 * q
+                    nc.vector.tensor_scalar(
+                        out=xw[u][:, i, 128 * q : 128 * (q + 1)],
+                        in0=xb[j][:, i, k : k + 128].bitcast(E4M3),
+                        scalar1=xs[:, 2 * j + i, 4 * g + q : 4 * g + q + 1],
+                        scalar2=None,
+                        op0=MULT,
+                    )
+
+        def x_turn(u):
+            xbank[u] = psum.tile([P, 2, 2, P], F32, name="bank", tag="bank")
+            for i in range(2):
+                words = xw[u][:, i, :].bitcast(F32)
+                for h in range(2):
+                    nc.tensor.transpose(xbank[u][:, i, h, :], words[:, h:256:2], ident[:])
+
+        def x_out(u):
+            xg[u] = xgp.tile([P, 2, P, 4], BF16, name="xg", align_bytes=64)
+            nc.scalar.copy(
+                out=xg[u][:].rearrange("p i r t -> p (i r t)").bitcast(F32).rearrange("p (i r h) -> p i r h", i=2, h=2),
+                in_=xbank[u][:].rearrange("p i h r -> p i r h"),
+            )
+
+        def x_quant(u):
+            j, g = divmod(u, G)
+            cols = slice(256 * j, 256 * (j + 1))
+            nc.vector.quantize_mx(
+                out=xq[:, g, cols].bitcast(MX),
+                scales=xqs[:, g, cols],
+                in_=xg[u][:].rearrange("p i r t -> p (i r t)"),
+            )
+
+        ag = {}
+
+        def a_inter(g, t, engine):
+            if t == 0:
+                ag[g] = agp.tile([P, 4, P, 4], BF16, name="ag", align_bytes=64)
+            dst = ag[g][:, t, :, :]
+            src = araw[g][:].rearrange("p j (m t) -> p t m j", t=4)[:, t, :, :]
+            if engine == "v":
+                nc.vector.tensor_copy(out=dst, in_=src)
+            else:
+                nc.scalar.copy(out=dst, in_=src)
+
+        def a_quant(g):
+            nc.vector.quantize_mx(
+                out=aq[:, g, :].bitcast(MX), scales=aqs[:, g, :], in_=ag[g][:].rearrange("p t m j -> p (t m j)")
+            )
+
+        hbank, hb, hg = {}, {}, {}
+
+        def h_mm(j):
+            cols = slice(256 * j, 256 * (j + 1))
+            for t in range(4):
+                if t % 2 == 0:
+                    tag = "acc" if j < 2 else "bank"
+                    hbank[j, t // 2] = psum.tile([P, 2, 256], F32, name=tag, tag=tag)
+                for g in range(G):
+                    nc.tensor.matmul_mx(
+                        out=hbank[j, t // 2][:, t % 2, :],
+                        lhsT=aq[:, g, P * t : P * (t + 1)].bitcast(MX),
+                        lhsT_scale=aqs[:, g, P * t : P * (t + 1)],
+                        rhs=xq[:, g, cols].bitcast(MX),
+                        rhs_scale=xqs[:, g, cols],
+                        start=(g == 0),
+                        stop=(g == G - 1),
+                    )
+
+        def h_out(j):
+            hb[j] = hp.tile([P, 4, 256], BF16, name="hb", align_bytes=64)
+            for t in range(4):
+                nc.scalar.activation(
+                    out=hb[j][:, t, :], in_=hbank[j, t // 2][:, t % 2, :], func=COPY, scale=lamf[:, t : t + 1]
+                )
+
+        def h_inter(j):
+            hg[j] = hp.tile([P, 256, 4], BF16, name="hg", align_bytes=64)
+            nc.vector.tensor_copy(out=hg[j][:], in_=hb[j][:].rearrange("p t n -> p n t"))
+
+        def h_quant(j):
+            cols = slice(256 * j, 256 * (j + 1))
+            nc.vector.quantize_mx(
+                out=hq[:, cols].bitcast(MX), scales=hqs[:, cols], in_=hg[j][:].rearrange("p n t -> p (n t)")
+            )
+
+        bg = {}
+
+        def b_inter(c, engine):
+            bg[c] = wgp.tile([P, CW, 4], BF16, name="wg", tag="wg", align_bytes=64)
+            for e in range(2):
+                n = slice(256 * e, 256 * (e + 1))
+                if engine == "v":
+                    nc.vector.tensor_copy(out=bg[c][:, n, :], in_=braw[c][:, :, n].rearrange("p t n -> p n t"))
+                else:
+                    nc.scalar.copy(out=bg[c][:, n, :], in_=braw[c][:, :, n].rearrange("p t n -> p n t"))
+
+        def b_quant(c):
+            nc.vector.quantize_mx(out=bq[c][:].bitcast(MX), scales=bqs[c][:], in_=bg[c][:].rearrange("p n t -> p (n t)"))
+
+        subs = [(0, 512), (512, 512), (1024, 256), (1280, 256)]
+        ww, wg, acc = {}, {}, {}
+
+        def w_widen(v, halves=(0, 1)):
+            for e in halves:
+                if e == 0:
+                    ww[v] = wwp.tile([P, 4, CW], BF16, name="ww", align_bytes=64)
+                nc.scalar.copy(
+                    out=ww[v][:, 2 * e : 2 * e + 2, :].rearrange("p t n -> p (t n)"),
+                    in_=wb[v][:, 2 * e : 2 * e + 2, :].rearrange("p t n -> p (t n)").bitcast(E4M3),
+                )
+
+        def w_inter(u, g, engine, blocks):
+            n0, width = subs[u]
+            if (u, g) not in wg:
+                wg[u, g] = wgp.tile([P, CW, 4], BF16, name="wg", tag="wg", align_bytes=64)
+            for e in blocks:
+                src = ww[G * (n0 // CW) + g][:, :, n0 % CW + 128 * e : n0 % CW + 128 * (e + 1)].rearrange("p t n -> p n t")
+                dst = wg[u, g][:, 128 * e : 128 * (e + 1), :]
+                block = n0 // 128 + e
+                scale = ws[:, g, block : block + 1]
+                if engine == "v":
+                    nc.vector.tensor_scalar(out=dst, in0=src, scalar1=scale, scalar2=None, op0=MULT)
+                else:
+                    nc.scalar.activation(out=dst, in_=src, func=COPY, scale=scale)
+
+        def w_cols(u, g):
+            n0, width = subs[u]
+            return G * (n0 // CW) + g, slice(n0 % CW, n0 % CW + width)
+
+        def w_quant(u, g):
+            v, cols = w_cols(u, g)
+            width = subs[u][1]
+            nc.vector.quantize_mx(
+                out=wq[v][:, cols].bitcast(MX),
+                scales=wqs[v][:, cols],
+                in_=wg[u, g][:, 0:width, :].rearrange("p n t -> p (n t)"),
+            )
+
+        def mm(u, g, i):
+            n0, width = subs[u]
+            v, cols = w_cols(u, g)
+            rows = slice(P * i, P * (i + 1))
+            if g == 0:
+                tag = "acc" if i < 4 else "bank"
+                acc[u, i] = psum.tile([P, CW], F32, name=tag, tag=tag)
+            if g == (3, 2, 0, 0)[u]:
+                nc.tensor.matmul_mx(
+                    out=acc[u, i][:, 0:width],
+                    lhsT=hq[:, rows].bitcast(MX),
+                    lhsT_scale=hqs[:, rows],
+                    rhs=bq[n0 // CW][:, cols].bitcast(MX),
+                    rhs_scale=bqs[n0 // CW][:, cols],
+                    start=(u > 1),
+                    stop=False,
+                )
+            nc.tensor.matmul_mx(
+                out=acc[u, i][:, 0:width],
+                lhsT=xq[:, g, rows].bitcast(MX),
+                lhsT_scale=xqs[:, g, rows],
+                rhs=wq[v][:, cols].bitcast(MX),
+                rhs_scale=wqs[v][:, cols],
+                start=(g == 0 and u < 2),
+                stop=(g == G - 1),
+            )
+
+        def y_out(u, i):
+            n0, width = subs[u]
+            cols = slice(n0, n0 + width)
+            res = resp.tile([P, CW], F32, name="res")
+            nc.vector.tensor_tensor(out=res[:, 0:width], in0=acc[u, i][:, 0:width], in1=sb[:, cols], op=MULT)
+            nc.sync.dma_start(out=out_view[:, i, cols], in_=res[:, 0:width])
+
+        with tc.manual_schedule(
+            engines={mybir.EngineType.PE, mybir.EngineType.DVE, mybir.EngineType.Activation, mybir.EngineType.SP}
+        ):
+            units = PAIRS * G
+            for s in range(units + 3):
+                if s < units:
+                    x_widen(s)
+                    x_turn(s)
+                if s == 9:
+                    nc.vector.reciprocal(out=rec[:], in_=normb[:])
+                    nc.vector.tensor_tensor(out=s1[:], in0=magb[:], in1=rec[:], op=MULT)
+                if 1 <= s <= units:
+                    x_out(s - 1)
+                if s < 8:
+                    for t in range(2 * (s % 2), 2 * (s % 2) + 2):
+                        a_inter(s // 2, t, "v" if t == 3 or (s == 6 and t == 1) else "s")
+                if s >= 3:
+                    x_quant(s - 3)
+                if s >= 3 and s % 2 == 1 and s <= 9:
+                    a_quant((s - 3) // 2)
+                if s == 10:
+                    nc.sync.dma_start(out=out[0].rearrange("(p j) -> p j", j=N // P), in_=s1[:])
+                    nc.sync.dma_start(out=sb[:], in_=out[0].partition_broadcast(P))
+                if s in (10, 12, 15):
+                    h_mm({10: 0, 12: 1, 15: 2}[s])
+                if s in (11, 13, 16):
+                    h_out({11: 0, 13: 1, 16: 2}[s])
+                if s in (13, 15, 18):
+                    h_inter({13: 0, 15: 1, 18: 2}[s])
+                if s in (14, 16):
+                    h_quant({14: 0, 16: 1}[s])
+                if s in (8, 9, 10, 11, 12, 14, 15, 16, 17, 18):
+                    n = (8, 9, 10, 11, 12, 14, 15, 16, 17, 18).index(s)
+                    w_widen(n // 2, (n % 2,))
+                if s in (11, 12, 13, 14, 16, 17):
+                    n = (11, 12, 13, 14, 16, 17).index(s)
+                    w_inter(0, n // 2, "v", range(2 * (n % 2), 2 * (n % 2) + 2))
+                if s == 13:
+                    w_quant(0, 0)
+                if s == 15:
+                    w_quant(0, 1)
+                if s == 18:
+                    w_quant(0, 2)
+                if s == 14:
+                    for i in range(4):
+                        mm(0, 0, i)
+                if s == 16:
+                    for i in range(4):
+                        mm(0, 1, i)
+                if s == 17:
+                    b_inter(0, "v")
+            h_mm(3)
+            for i in range(4):
+                mm(0, 2, i)
+            h_quant(2)
+            b_quant(0)
+            w_inter(0, 3, "v", range(4))
+            w_widen(5)
+            h_out(3)
+            for g in range(3):
+                for i in range(4, TILES):
+                    mm(0, g, i)
+            todo = [(u, g) for u in range(1, len(subs)) for g in range(G)]
+
+            def s_ahead(n):
+                if n < len(todo):
+                    u, g = todo[n]
+                    v = w_cols(u, g)[0]
+                    if u < 3 and v + 1 < C * G:
+                        w_widen(v + 1)
+                    w_inter(u, g, "s", range(own(u, g), subs[u][1] // 128))
+
+            def own(u, g):
+                n = subs[u][1] // 128
+                return n - 1
+
+            s_ahead(0)
+            w_inter(1, 0, "v", range(own(1, 0)))
+            h_inter(3)
+            w_quant(0, 3)
+            h_quant(3)
+            for i in range(TILES):
+                mm(0, 3, i)
+            for n, (u, g) in enumerate(todo):
+                if n > 0:
+                    w_inter(u, g, "v", range(own(u, g)))
+                s_ahead(n + 1)
+                if (u, g) == (1, 0):
+                    b_inter(1, "s")
+                if (u, g) == (1, 2):
+                    b_quant(1)
+                    b_inter(2, "s")
+                if (u, g) == (2, 0):
+                    b_quant(2)
+                if n == 0:
+                    continue
+                pu, pg = todo[n - 1]
+                w_quant(pu, pg)
+                if g == 1:
+                    for i in range(TILES):
+                        y_out(u - 1, i)
+                        mm(pu, pg, i)
+                else:
+                    for i in range(TILES):
+                        mm(pu, pg, i)
+            w_quant(3, 3)
+            for i in range(TILES):
+                mm(3, 3, i)
+                y_out(3, i)

@@ -21,23 +21,26 @@ TILES = T // P
 PAIRS = TILES // 2
 CW = 512
 C = N // CW
+SUBS = [(0, 512), (512, 512), (1024, 512)]
 
 
 def tile_dora_fp8_forward_d2_kernel(tc, x_bytes, x_scale, w_bytes, w_scale, a, lam, b, mag, norm, out):
     nc = tc.nc
     with ExitStack() as ctx:
         keep = ctx.enter_context(tc.tile_pool(name="keep", bufs=1))
-        agp = ctx.enter_context(tc.tile_pool(name="agp", bufs=2))
+        big = ctx.enter_context(tc.tile_pool(name="big", bufs=14))
         xwp = ctx.enter_context(tc.tile_pool(name="xwp", bufs=4))
-        xgp = ctx.enter_context(tc.tile_pool(name="xgp", bufs=4))
-        wwp = ctx.enter_context(tc.tile_pool(name="wwp", bufs=4))
+        xgp = ctx.enter_context(tc.tile_pool(name="xgp", bufs=3))
+        wwp = ctx.enter_context(tc.tile_pool(name="wwp", bufs=3))
         wgp = ctx.enter_context(tc.tile_pool(name="wgp", bufs=4))
         hp = ctx.enter_context(tc.tile_pool(name="hp", bufs=2))
-        resp = ctx.enter_context(tc.tile_pool(name="resp", bufs=8))
-        psum = ctx.enter_context(tc.psum_pool(name="psum", bufs=4))
+        psum = ctx.enter_context(tc.psum_pool(name="psum", bufs=1))
 
         def kept(shape, dtype, name):
             return keep.tile(shape, dtype, name=name, align_bytes=64)
+
+        def bank(n, shape):
+            return psum.tile(shape, F32, name=f"bank{n}", tag=f"bank{n}")
 
         ident = kept([P, P], F32, "ident")
         xs = kept([P, TILES, K // 128], F32, "xs")
@@ -45,17 +48,17 @@ def tile_dora_fp8_forward_d2_kernel(tc, x_bytes, x_scale, w_bytes, w_scale, a, l
         ws = kept([P, G, N // 128], F32, "ws")
         lamb = kept([P, 4], BF16, "lamb")
         lamf = kept([P, 4], F32, "lamf")
-        magb = kept([P, N // P], BF16, "magb")
-        normb = kept([P, N // P], BF16, "normb")
-        rec = kept([P, N // P], F32, "rec")
-        s1 = kept([P, N // P], F32, "s1")
+        magb = kept([64, N // 64], BF16, "magb")
+        normb = kept([64, N // 64], BF16, "normb")
+        rec = kept([64, N // 64], F32, "rec")
+        s1 = kept([64, N // 64], F32, "s1")
         sb = kept([P, N], F32, "sb")
-        xb = [kept([P, 2, K], U8, f"xb{j}") for j in range(PAIRS)]
-        araw = [kept([P, 4, R], BF16, f"araw{g}") for g in range(G)]
+        xb = [big.tile([P, 2, K], U8, name=f"xb{j}", tag="big", align_bytes=64) for j in range(PAIRS)]
+        araw = [big.tile([P, 4, R], BF16, name=f"araw{g}", tag="big", align_bytes=64) for g in range(G)]
         wb = [kept([P, 4, CW], U8, f"wb{v}") for v in range(C * G)]
         braw = [kept([P, 4, CW], BF16, f"braw{c}") for c in range(C)]
-        xq = kept([P, G, T], U32, "xq")
-        xqs = kept([P, G, T], U8, "xqs")
+        xq = kept([P, PAIRS, G, 256], U32, "xq")
+        xqs = kept([P, PAIRS, G, 256], U8, "xqs")
         aq = kept([P, G, R], U32, "aq")
         aqs = kept([P, G, R], U8, "aqs")
         wq = [kept([P, CW], U32, f"wq{v}") for v in range(C * G)]
@@ -71,36 +74,14 @@ def tile_dora_fp8_forward_d2_kernel(tc, x_bytes, x_scale, w_bytes, w_scale, a, l
         b_view = b.rearrange("(p t) n -> p t n", t=4)
         out_view = out.rearrange("(p i) n -> p i n", i=TILES)
 
-        nc.scalar.dma_start(out=xs[:], in_=x_scale.rearrange("(p i) k -> p i k", i=TILES))
         make_identity(nc, ident[:])
-        nc.gpsimd.dma_start(out=lamb[:], in_=lam.rearrange("(p t) -> p t", t=4))
-        nc.gpsimd.dma_start(out=magb[:], in_=mag.rearrange("(p j) -> p j", j=N // P))
-        nc.gpsimd.dma_start(out=normb[:], in_=norm.rearrange("(p j) -> p j", j=N // P))
-        nc.gpsimd.dma_start(
-            out=wsall[:].rearrange("p g q n -> p (g q n)"),
-            in_=w_scale.rearrange("k n -> (k n)").partition_broadcast(P),
-        )
-        nc.gpsimd.tensor_copy(out=lamf[:], in_=lamb[:])
-        for q in range(4):
-            rows = slice(32 * q, 32 * q + 32)
-            nc.gpsimd.tensor_copy(out=ws[rows, :, :], in_=wsall[rows, :, q, :])
 
-        half = K // 2
-        nc.sync.dma_start(out=xb[0][:, :, 0:half], in_=x_view[:, 0:2, 0:half])
-        nc.sync.dma_start(out=araw[0][:], in_=a_view[0])
-        nc.sync.dma_start(out=xb[0][:, :, half:K], in_=x_view[:, 0:2, half:K])
-        nc.sync.dma_start(out=araw[1][:], in_=a_view[1])
-        nc.sync.dma_start(out=xb[1][:], in_=x_view[:, 2:4, :])
-        nc.sync.dma_start(out=araw[2][:], in_=a_view[2])
-        nc.sync.dma_start(out=araw[3][:], in_=a_view[3])
-        nc.sync.dma_start(out=xb[2][:], in_=x_view[:, 4:6, :])
-        nc.sync.dma_start(out=xb[3][:], in_=x_view[:, 6:8, :])
-        for c in range(C):
-            cols = slice(CW * c, CW * (c + 1))
-            for g in range(G):
-                nc.sync.dma_start(out=wb[G * c + g][:], in_=w_view[g][:, :, cols])
-                if g == 3:
-                    nc.sync.dma_start(out=braw[c][:], in_=b_view[:, :, cols])
+        def load_w(v):
+            c, g = divmod(v, G)
+            nc.sync.dma_start(out=wb[v][:], in_=w_view[g][:, :, CW * c : CW * (c + 1)])
+
+        def load_b(c):
+            nc.sync.dma_start(out=braw[c][:], in_=b_view[:, :, CW * c : CW * (c + 1)])
 
         xw, xbank, xg = {}, {}, {}
 
@@ -108,10 +89,11 @@ def tile_dora_fp8_forward_d2_kernel(tc, x_bytes, x_scale, w_bytes, w_scale, a, l
             j, g = divmod(u, G)
             xw[u] = xwp.tile([P, 2, 512], BF16, name="xw", align_bytes=64)
             for i in range(2):
+                dst = xw[u][:, i, :].rearrange("p (h m e) -> p m h e", h=2, e=2)
                 for q in range(4):
                     k = 512 * g + 128 * q
                     nc.vector.tensor_scalar(
-                        out=xw[u][:, i, 128 * q : 128 * (q + 1)],
+                        out=dst[:, 32 * q : 32 * (q + 1), :, :],
                         in0=xb[j][:, i, k : k + 128].bitcast(E4M3),
                         scalar1=xs[:, 2 * j + i, 4 * g + q : 4 * g + q + 1],
                         scalar2=None,
@@ -119,39 +101,46 @@ def tile_dora_fp8_forward_d2_kernel(tc, x_bytes, x_scale, w_bytes, w_scale, a, l
                     )
 
         def x_turn(u):
-            xbank[u] = psum.tile([P, 2, 2, P], F32, name="bank", tag="bank")
+            xbank[u] = bank(u % 4, [P, 2, 2, P])
             for i in range(2):
                 words = xw[u][:, i, :].bitcast(F32)
                 for h in range(2):
-                    nc.tensor.transpose(xbank[u][:, i, h, :], words[:, h:256:2], ident[:])
+                    nc.tensor.transpose(xbank[u][:, i, h, :], words[:, P * h : P * (h + 1)], ident[:])
 
         def x_out(u):
-            xg[u] = xgp.tile([P, 2, P, 4], BF16, name="xg", align_bytes=64)
+            if u % 2 == 0:
+                xg[u // 2] = xgp.tile([P, 2, 2, P, 4], BF16, name="xg", align_bytes=64)
+            words = xg[u // 2][:, u % 2].rearrange("p i r t -> p (i r t)").bitcast(F32)
             nc.scalar.copy(
-                out=xg[u][:].rearrange("p i r t -> p (i r t)").bitcast(F32).rearrange("p (i r h) -> p i r h", i=2, h=2),
+                out=words.rearrange("p (i r h) -> p i r h", i=2, h=2),
                 in_=xbank[u][:].rearrange("p i h r -> p i r h"),
             )
 
-        def x_quant(u):
-            j, g = divmod(u, G)
-            cols = slice(256 * j, 256 * (j + 1))
+        def x_quant(d):
+            j, e = divmod(d, 2)
             nc.vector.quantize_mx(
-                out=xq[:, g, cols].bitcast(MX),
-                scales=xqs[:, g, cols],
-                in_=xg[u][:].rearrange("p i r t -> p (i r t)"),
+                out=xq[:, j, 2 * e : 2 * e + 2, :].rearrange("p g n -> p (g n)").bitcast(MX),
+                scales=xqs[:, j, 2 * e : 2 * e + 2, :].rearrange("p g n -> p (g n)"),
+                in_=xg[d][:].rearrange("p g i r t -> p (g i r t)"),
             )
 
-        ag = {}
-
-        def a_inter(g, t, engine):
-            if t == 0:
-                ag[g] = agp.tile([P, 4, P, 4], BF16, name="ag", align_bytes=64)
-            dst = ag[g][:, t, :, :]
-            src = araw[g][:].rearrange("p j (m t) -> p t m j", t=4)[:, t, :, :]
+        def copy_on(engine, dst, src):
             if engine == "v":
                 nc.vector.tensor_copy(out=dst, in_=src)
             else:
                 nc.scalar.copy(out=dst, in_=src)
+
+        def fours(dst, src):
+            return dst.rearrange("p (c i) t -> p c t i", i=4), src.rearrange("p t (c i) -> p c t i", i=4)
+
+        ag = {}
+
+        def a_inter(g, e, engine):
+            if g not in ag:
+                ag[g] = wgp.tile([P, 4, P, 4], BF16, name="wg", tag="wg", align_bytes=64)
+            dst = ag[g][:, 2 * e : 2 * e + 2].rearrange("p t m j -> p m j t")
+            src = araw[g][:].rearrange("p j (m t) -> p m j t", t=4)[:, :, :, 2 * e : 2 * e + 2]
+            copy_on(engine, dst, src)
 
         def a_quant(g):
             nc.vector.quantize_mx(
@@ -160,33 +149,31 @@ def tile_dora_fp8_forward_d2_kernel(tc, x_bytes, x_scale, w_bytes, w_scale, a, l
 
         hbank, hb, hg = {}, {}, {}
 
-        def h_mm(j):
-            cols = slice(256 * j, 256 * (j + 1))
-            for t in range(4):
-                if t % 2 == 0:
-                    tag = "acc" if j < 2 else "bank"
-                    hbank[j, t // 2] = psum.tile([P, 2, 256], F32, name=tag, tag=tag)
+        def h_mm(n):
+            j, e = divmod(n, 2)
+            hbank[n] = bank(4 + n % 4, [P, 2, 256])
+            for t in (2 * e, 2 * e + 1):
                 for g in range(G):
                     nc.tensor.matmul_mx(
-                        out=hbank[j, t // 2][:, t % 2, :],
+                        out=hbank[n][:, t % 2, :],
                         lhsT=aq[:, g, P * t : P * (t + 1)].bitcast(MX),
                         lhsT_scale=aqs[:, g, P * t : P * (t + 1)],
-                        rhs=xq[:, g, cols].bitcast(MX),
-                        rhs_scale=xqs[:, g, cols],
+                        rhs=xq[:, j, g, :].bitcast(MX),
+                        rhs_scale=xqs[:, j, g, :],
                         start=(g == 0),
                         stop=(g == G - 1),
                     )
 
-        def h_out(j):
-            hb[j] = hp.tile([P, 4, 256], BF16, name="hb", align_bytes=64)
-            for t in range(4):
-                nc.scalar.activation(
-                    out=hb[j][:, t, :], in_=hbank[j, t // 2][:, t % 2, :], func=COPY, scale=lamf[:, t : t + 1]
-                )
+        def h_out(n):
+            j, e = divmod(n, 2)
+            if e == 0:
+                hb[j] = hp.tile([P, 4, 256], BF16, name="hb", bufs=4, align_bytes=64)
+            for t in (2 * e, 2 * e + 1):
+                nc.scalar.activation(out=hb[j][:, t, :], in_=hbank[n][:, t % 2, :], func=COPY, scale=lamf[:, t : t + 1])
 
         def h_inter(j):
             hg[j] = hp.tile([P, 256, 4], BF16, name="hg", align_bytes=64)
-            nc.vector.tensor_copy(out=hg[j][:], in_=hb[j][:].rearrange("p t n -> p n t"))
+            copy_on("v", *fours(hg[j][:], hb[j][:]))
 
         def h_quant(j):
             cols = slice(256 * j, 256 * (j + 1))
@@ -196,197 +183,213 @@ def tile_dora_fp8_forward_d2_kernel(tc, x_bytes, x_scale, w_bytes, w_scale, a, l
 
         bg = {}
 
-        def b_inter(c, engine):
-            bg[c] = wgp.tile([P, CW, 4], BF16, name="wg", tag="wg", align_bytes=64)
-            for e in range(2):
-                n = slice(256 * e, 256 * (e + 1))
-                if engine == "v":
-                    nc.vector.tensor_copy(out=bg[c][:, n, :], in_=braw[c][:, :, n].rearrange("p t n -> p n t"))
-                else:
-                    nc.scalar.copy(out=bg[c][:, n, :], in_=braw[c][:, :, n].rearrange("p t n -> p n t"))
+        def b_inter(c, e, engine):
+            if c not in bg:
+                bg[c] = wgp.tile([P, CW, 4], BF16, name="wg", tag="wg", align_bytes=64)
+            n = slice(256 * e, 256 * (e + 1))
+            copy_on(engine, *fours(bg[c][:, n, :], braw[c][:, :, n]))
 
         def b_quant(c):
             nc.vector.quantize_mx(out=bq[c][:].bitcast(MX), scales=bqs[c][:], in_=bg[c][:].rearrange("p n t -> p (n t)"))
 
-        subs = [(0, 512), (512, 512), (1024, 256), (1280, 256)]
-        ww, wg, acc = {}, {}, {}
+        ww, wg, acc, res = {}, {}, {}, {}
 
-        def w_widen(v, halves=(0, 1)):
-            for e in halves:
-                if e == 0:
-                    ww[v] = wwp.tile([P, 4, CW], BF16, name="ww", align_bytes=64)
-                nc.scalar.copy(
-                    out=ww[v][:, 2 * e : 2 * e + 2, :].rearrange("p t n -> p (t n)"),
-                    in_=wb[v][:, 2 * e : 2 * e + 2, :].rearrange("p t n -> p (t n)").bitcast(E4M3),
-                )
+        def w_widen(v):
+            ww[v] = wwp.tile([P, 4, CW], BF16, name="ww", align_bytes=64)
+            nc.scalar.copy(
+                out=ww[v][:].rearrange("p t n -> p (t n)"), in_=wb[v][:].rearrange("p t n -> p (t n)").bitcast(E4M3)
+            )
+
+        def w_cols(u, g):
+            n0, width = SUBS[u]
+            return G * (n0 // CW) + g, slice(n0 % CW, n0 % CW + width)
 
         def w_inter(u, g, engine, blocks):
-            n0, width = subs[u]
+            n0, width = SUBS[u]
             if (u, g) not in wg:
-                wg[u, g] = wgp.tile([P, CW, 4], BF16, name="wg", tag="wg", align_bytes=64)
+                wg[u, g] = wgp.tile([P, width, 4], BF16, name="wg", tag="wg", align_bytes=64)
             for e in blocks:
-                src = ww[G * (n0 // CW) + g][:, :, n0 % CW + 128 * e : n0 % CW + 128 * (e + 1)].rearrange("p t n -> p n t")
-                dst = wg[u, g][:, 128 * e : 128 * (e + 1), :]
-                block = n0 // 128 + e
-                scale = ws[:, g, block : block + 1]
+                c0 = n0 % CW + 128 * e
+                dst, src = fours(wg[u, g][:, 128 * e : 128 * (e + 1), :], ww[w_cols(u, g)[0]][:, :, c0 : c0 + 128])
+                scale = ws[:, g, n0 // 128 + e : n0 // 128 + e + 1]
                 if engine == "v":
                     nc.vector.tensor_scalar(out=dst, in0=src, scalar1=scale, scalar2=None, op0=MULT)
                 else:
                     nc.scalar.activation(out=dst, in_=src, func=COPY, scale=scale)
 
-        def w_cols(u, g):
-            n0, width = subs[u]
-            return G * (n0 // CW) + g, slice(n0 % CW, n0 % CW + width)
-
         def w_quant(u, g):
             v, cols = w_cols(u, g)
-            width = subs[u][1]
             nc.vector.quantize_mx(
-                out=wq[v][:, cols].bitcast(MX),
-                scales=wqs[v][:, cols],
-                in_=wg[u, g][:, 0:width, :].rearrange("p n t -> p (n t)"),
+                out=wq[v][:, cols].bitcast(MX), scales=wqs[v][:, cols], in_=wg[u, g][:].rearrange("p n t -> p (n t)")
             )
 
-        def mm(u, g, i):
-            n0, width = subs[u]
-            v, cols = w_cols(u, g)
-            rows = slice(P * i, P * (i + 1))
-            if g == 0:
-                tag = "acc" if i < 4 else "bank"
-                acc[u, i] = psum.tile([P, CW], F32, name=tag, tag=tag)
-            if g == (3, 2, 0, 0)[u]:
+        def mm(u, g, tiles):
+            n0, width = SUBS[u]
+            for i in tiles:
+                if g == 0:
+                    acc[u, i] = bank(i, [P, width])
+                if g == G:
+                    cols = w_cols(u, 0)[1]
+                    lhs, lhs_s = hq[:, P * i : P * (i + 1)], hqs[:, P * i : P * (i + 1)]
+                    rhs, rhs_s = bq[n0 // CW][:, cols], bqs[n0 // CW][:, cols]
+                else:
+                    v, cols = w_cols(u, g)
+                    rows = slice(P * (i % 2), P * (i % 2 + 1))
+                    lhs, lhs_s = xq[:, i // 2, g, rows], xqs[:, i // 2, g, rows]
+                    rhs, rhs_s = wq[v][:, cols], wqs[v][:, cols]
                 nc.tensor.matmul_mx(
-                    out=acc[u, i][:, 0:width],
-                    lhsT=hq[:, rows].bitcast(MX),
-                    lhsT_scale=hqs[:, rows],
-                    rhs=bq[n0 // CW][:, cols].bitcast(MX),
-                    rhs_scale=bqs[n0 // CW][:, cols],
-                    start=(u > 1),
-                    stop=False,
+                    out=acc[u, i][:],
+                    lhsT=lhs.bitcast(MX),
+                    lhsT_scale=lhs_s,
+                    rhs=rhs.bitcast(MX),
+                    rhs_scale=rhs_s,
+                    start=(g == 0),
+                    stop=(g == (G if u == 0 else G - 1)),
                 )
-            nc.tensor.matmul_mx(
-                out=acc[u, i][:, 0:width],
-                lhsT=xq[:, g, rows].bitcast(MX),
-                lhsT_scale=xqs[:, g, rows],
-                rhs=wq[v][:, cols].bitcast(MX),
-                rhs_scale=wqs[v][:, cols],
-                start=(g == 0 and u < 2),
-                stop=(g == G - 1),
-            )
 
-        def y_out(u, i):
-            n0, width = subs[u]
+        def y_out(u, tiles, per_store):
+            n0, width = SUBS[u]
             cols = slice(n0, n0 + width)
-            res = resp.tile([P, CW], F32, name="res")
-            nc.vector.tensor_tensor(out=res[:, 0:width], in0=acc[u, i][:, 0:width], in1=sb[:, cols], op=MULT)
-            nc.sync.dma_start(out=out_view[:, i, cols], in_=res[:, 0:width])
+            rows = 2 * CW // width
+            for n, i in enumerate(tiles):
+                if (u, i // rows) not in res:
+                    res[u, i // rows] = big.tile([P, rows, width], F32, name="res", tag="big", align_bytes=64)
+                tile = res[u, i // rows]
+                nc.vector.tensor_tensor(out=tile[:, i % rows, :], in0=acc[u, i][:], in1=sb[:, cols], op=MULT)
+                if (n + 1) % per_store == 0:
+                    i0 = min(tiles[n + 1 - per_store : n + 1])
+                    nc.sync.dma_start(
+                        out=out_view[:, i0 : i0 + per_store, cols], in_=tile[:, i0 % rows : i0 % rows + per_store, :]
+                    )
+
+        A, B = [0, 1, 2, 3], [4, 5, 6, 7]
+        units = [(u, g) for u in range(len(SUBS)) for g in range(G)]
+
+        def vector_blocks(u, g):
+            return (4 - g % 2, 3 - g % 2, 2)[u]
 
         with tc.manual_schedule(
             engines={mybir.EngineType.PE, mybir.EngineType.DVE, mybir.EngineType.Activation, mybir.EngineType.SP}
         ):
-            units = PAIRS * G
-            for s in range(units + 3):
-                if s < units:
-                    x_widen(s)
-                    x_turn(s)
-                if s == 9:
+            half = K // 2
+            nc.scalar.dma_start(out=xs[:], in_=x_scale.rearrange("(p i) k -> p i k", i=TILES))
+            nc.sync.dma_start(out=xb[0][:, :, 0:half], in_=x_view[:, 0:2, 0:half])
+            load_w(0)
+            nc.sync.dma_start(out=araw[0][:], in_=a_view[0])
+            nc.sync.dma_start(out=xb[0][:, :, half:K], in_=x_view[:, 0:2, half:K])
+            nc.scalar.dma_start(
+                out=wsall[:].rearrange("p g q n -> p (g q n)"),
+                in_=w_scale.rearrange("k n -> (k n)").partition_broadcast(P),
+            )
+            nc.scalar.dma_start(out=lamb[:], in_=lam.rearrange("(p t) -> p t", t=4))
+            for g in range(1, G):
+                nc.sync.dma_start(out=araw[g][:], in_=a_view[g])
+            nc.sync.dma_start(out=magb[:], in_=mag.rearrange("(p j) -> p j", p=64))
+            nc.sync.dma_start(out=normb[:], in_=norm.rearrange("(p j) -> p j", p=64))
+            for j in range(1, PAIRS):
+                nc.sync.dma_start(out=xb[j][:], in_=x_view[:, 2 * j : 2 * j + 2, :])
+                load_w(j)
+            load_b(0)
+
+            w_widen(0)
+            for d in range(2 * PAIRS):
+                for u in (2 * d, 2 * d + 1):
+                    x_widen(u)
+                    x_turn(u)
+                    if u > 0:
+                        x_out(u - 1)
+                    if u < G:
+                        a_inter(u, 1, "s")
+                        a_inter(u, 0, "v")
+                    if 1 <= u <= G:
+                        a_quant(u - 1)
+                    if u % 2 == 0 and d >= 4:
+                        h_out(d - 4)
+                if d == 2:
+                    nc.scalar.copy(out=lamf[:], in_=lamb[:])
+                    nc.scalar.copy(out=ws[0:32, :, :], in_=wsall[0:32, :, 0, :])
                     nc.vector.reciprocal(out=rec[:], in_=normb[:])
+                if 3 <= d < 6:
+                    rows = slice(32 * (d - 2), 32 * (d - 1))
+                    nc.scalar.copy(out=ws[rows, :, :], in_=wsall[rows, :, d - 2, :])
+                if d == 3:
                     nc.vector.tensor_tensor(out=s1[:], in0=magb[:], in1=rec[:], op=MULT)
-                if 1 <= s <= units:
-                    x_out(s - 1)
-                if s < 8:
-                    for t in range(2 * (s % 2), 2 * (s % 2) + 2):
-                        a_inter(s // 2, t, "v" if t == 3 or (s == 6 and t == 1) else "s")
-                if s >= 3:
-                    x_quant(s - 3)
-                if s >= 3 and s % 2 == 1 and s <= 9:
-                    a_quant((s - 3) // 2)
-                if s == 10:
-                    nc.sync.dma_start(out=out[0].rearrange("(p j) -> p j", j=N // P), in_=s1[:])
+                    nc.sync.dma_start(out=out[0].rearrange("(p j) -> p j", p=64), in_=s1[:])
+                    for v in range(G, 2 * G):
+                        load_w(v)
                     nc.sync.dma_start(out=sb[:], in_=out[0].partition_broadcast(P))
-                if s in (10, 12, 15):
-                    h_mm({10: 0, 12: 1, 15: 2}[s])
-                if s in (11, 13, 16):
-                    h_out({11: 0, 13: 1, 16: 2}[s])
-                if s in (13, 15, 18):
-                    h_inter({13: 0, 15: 1, 18: 2}[s])
-                if s in (14, 16):
-                    h_quant({14: 0, 16: 1}[s])
-                if s in (8, 9, 10, 11, 12, 14, 15, 16, 17, 18):
-                    n = (8, 9, 10, 11, 12, 14, 15, 16, 17, 18).index(s)
-                    w_widen(n // 2, (n % 2,))
-                if s in (11, 12, 13, 14, 16, 17):
-                    n = (11, 12, 13, 14, 16, 17).index(s)
-                    w_inter(0, n // 2, "v", range(2 * (n % 2), 2 * (n % 2) + 2))
-                if s == 13:
-                    w_quant(0, 0)
-                if s == 15:
-                    w_quant(0, 1)
-                if s == 18:
-                    w_quant(0, 2)
-                if s == 14:
-                    for i in range(4):
-                        mm(0, 0, i)
-                if s == 16:
-                    for i in range(4):
-                        mm(0, 1, i)
-                if s == 17:
-                    b_inter(0, "v")
-            h_mm(3)
-            for i in range(4):
-                mm(0, 2, i)
-            h_quant(2)
-            b_quant(0)
-            w_inter(0, 3, "v", range(4))
-            w_widen(5)
-            h_out(3)
-            for g in range(3):
-                for i in range(4, TILES):
-                    mm(0, g, i)
-            todo = [(u, g) for u in range(1, len(subs)) for g in range(G)]
+                    load_b(1)
+                    for v in range(2 * G, 3 * G):
+                        load_w(v)
+                    load_b(2)
+                if d in (2,):
+                    w_widen(len(ww))
+                if d in (2, 3):
+                    b_inter(0, int(0 in bg), "s")
+                if d == 2 * PAIRS - 1:
+                    w_inter(0, 0, "v", range(4))
+                if d > 0:
+                    x_quant(d - 1)
+                if d == 5:
+                    b_quant(0)
+                if d >= 3:
+                    h_mm(d - 3)
+            x_out(4 * PAIRS - 1)
+            h_out(4)
+            h_inter(0)
+            x_quant(2 * PAIRS - 1)
+            h_mm(5)
+            h_mm(6)
+            h_out(5)
 
-            def s_ahead(n):
-                if n < len(todo):
-                    u, g = todo[n]
-                    v = w_cols(u, g)[0]
-                    if u < 3 and v + 1 < C * G:
-                        w_widen(v + 1)
-                    w_inter(u, g, "s", range(own(u, g), subs[u][1] // 128))
-
-            def own(u, g):
-                n = subs[u][1] // 128
-                return n - 1
-
-            s_ahead(0)
-            w_inter(1, 0, "v", range(own(1, 0)))
-            h_inter(3)
-            w_quant(0, 3)
-            h_quant(3)
-            for i in range(TILES):
-                mm(0, 3, i)
-            for n, (u, g) in enumerate(todo):
-                if n > 0:
-                    w_inter(u, g, "v", range(own(u, g)))
-                s_ahead(n + 1)
-                if (u, g) == (1, 0):
-                    b_inter(1, "s")
-                if (u, g) == (1, 2):
-                    b_quant(1)
-                    b_inter(2, "s")
-                if (u, g) == (2, 0):
-                    b_quant(2)
+            last = len(SUBS) - 1
+            for n, (u, g) in enumerate(units):
+                if n + 1 < len(units):
+                    nu, ng = units[n + 1]
+                    w_inter(nu, ng, "s", range(vector_blocks(nu, ng), 4))
+                if n < 2:
+                    h_out(6 + n)
+                if len(ww) < C * G:
+                    w_widen(len(ww))
+                if u > 0 and g < 2:
+                    b_inter(u, g, "s")
+                w_quant(u, g)
+                if n < PAIRS:
+                    h_quant(n)
+                if g == 1 and u > 0:
+                    y_out(u - 1, A, 2)
+                if n + 1 < len(units):
+                    w_inter(nu, ng, "v", range(vector_blocks(nu, ng)))
+                if n + 1 < PAIRS:
+                    h_inter(n + 1)
+                if g == 2 and u > 0:
+                    b_quant(u)
                 if n == 0:
-                    continue
-                pu, pg = todo[n - 1]
-                w_quant(pu, pg)
+                    mm(0, 0, A)
+                    h_mm(7)
                 if g == 1:
-                    for i in range(TILES):
-                        y_out(u - 1, i)
-                        mm(pu, pg, i)
-                else:
-                    for i in range(TILES):
-                        mm(pu, pg, i)
-            w_quant(3, 3)
-            for i in range(TILES):
-                mm(3, 3, i)
-                y_out(3, i)
+                    if u > 0:
+                        mm(u, 0, A)
+                    mm(u, 1, A)
+                    if u > 0:
+                        y_out(u - 1, B, 2)
+                    mm(u, 0, B)
+                    mm(u, 1, B)
+                if g == 2:
+                    mm(u, 2, A)
+                    if u > 0:
+                        mm(u, G, A)
+                if g == 3:
+                    mm(u, 3, A)
+                    order = (2, G, 3)
+                    if u == 0:
+                        mm(u, G, A)
+                        order = (2, 3, G)
+                    if u < last:
+                        for e in order:
+                            mm(u, e, B)
+            y_out(last, A, 2)
+            for i in B:
+                for e in (2, G, 3):
+                    mm(last, e, [i])
+                y_out(last, [i], 1)

@@ -21,7 +21,24 @@ TILES = T // P
 PAIRS = TILES // 2
 CW = 512
 C = N // CW
-SUBS = [(0, 512), (512, 512), (1024, 512)]
+XW_BUFS = 6
+XW_S = [1, 9]
+A_ENG = "svsvsvsv"
+A_LAG = 1
+XO_LAG = 2
+QA_LAG = 1
+QX_LAG = 2
+QX_LAG2 = 4
+H_LAG = 2
+SMALL_AT = 10
+HO_AT = 11
+HO_PER = 4
+W0_AT = 15
+WW_AT = [9,15]
+LOOK = 1
+HI_ENG = "vvvv"
+B0_ENG = "vs"
+REV = True
 
 
 def tile_dora_fp8_forward_d2_kernel(tc, x_bytes, x_scale, w_bytes, w_scale, a, lam, b, mag, norm, out):
@@ -29,23 +46,22 @@ def tile_dora_fp8_forward_d2_kernel(tc, x_bytes, x_scale, w_bytes, w_scale, a, l
     with ExitStack() as ctx:
         keep = ctx.enter_context(tc.tile_pool(name="keep", bufs=1))
         big = ctx.enter_context(tc.tile_pool(name="big", bufs=14))
-        xwp = ctx.enter_context(tc.tile_pool(name="xwp", bufs=4))
-        xgp = ctx.enter_context(tc.tile_pool(name="xgp", bufs=3))
-        wwp = ctx.enter_context(tc.tile_pool(name="wwp", bufs=3))
-        wgp = ctx.enter_context(tc.tile_pool(name="wgp", bufs=4))
-        hp = ctx.enter_context(tc.tile_pool(name="hp", bufs=2))
+        xwp = ctx.enter_context(tc.tile_pool(name="xwp", bufs=XW_BUFS))
+        stage = ctx.enter_context(tc.tile_pool(name="stage", bufs=14))
         psum = ctx.enter_context(tc.psum_pool(name="psum", bufs=1))
 
         def kept(shape, dtype, name):
             return keep.tile(shape, dtype, name=name, align_bytes=64)
 
-        def bank(n, shape):
-            return psum.tile(shape, F32, name=f"bank{n}", tag=f"bank{n}")
+        def staged(shape, name):
+            return stage.tile(shape, BF16, name=name, tag="stage", align_bytes=64)
+
+        def bank(n, shape, dtype=F32):
+            return psum.tile(shape, dtype, name=f"bank{n}", tag=f"bank{n}")
 
         ident = kept([P, P], F32, "ident")
         xs = kept([P, TILES, K // 128], F32, "xs")
-        wsall = kept([P, G, 4, N // 128], F32, "wsall")
-        ws = kept([P, G, N // 128], F32, "ws")
+        ws = kept([P, G, 16], F32, "ws")
         lamb = kept([P, 4], BF16, "lamb")
         lamf = kept([P, 4], F32, "lamf")
         magb = kept([64, N // 64], BF16, "magb")
@@ -53,16 +69,15 @@ def tile_dora_fp8_forward_d2_kernel(tc, x_bytes, x_scale, w_bytes, w_scale, a, l
         rec = kept([64, N // 64], F32, "rec")
         s1 = kept([64, N // 64], F32, "s1")
         sb = kept([P, N], F32, "sb")
-        xb = [big.tile([P, 2, K], U8, name=f"xb{j}", tag="big", align_bytes=64) for j in range(PAIRS)]
+        xb = [big.tile([P, 4, K // 2], U8, name=f"xb{n}", tag="big", align_bytes=64) for n in range(4)]
         araw = [big.tile([P, 4, R], BF16, name=f"araw{g}", tag="big", align_bytes=64) for g in range(G)]
         wb = [kept([P, 4, CW], U8, f"wb{v}") for v in range(C * G)]
         braw = [kept([P, 4, CW], BF16, f"braw{c}") for c in range(C)]
-        xq = kept([P, PAIRS, G, 256], U32, "xq")
-        xqs = kept([P, PAIRS, G, 256], U8, "xqs")
+        xq = kept([P, 2, G, 512], U32, "xq")
+        xqs = kept([P, 2, G, 512], U8, "xqs")
         aq = kept([P, G, R], U32, "aq")
         aqs = kept([P, G, R], U8, "aqs")
-        wq = [kept([P, CW], U32, f"wq{v}") for v in range(C * G)]
-        wqs = [kept([P, CW], U8, f"wqs{v}") for v in range(C * G)]
+        wq, wqs = {}, {}
         bq = [kept([P, CW], U32, f"bq{c}") for c in range(C)]
         bqs = [kept([P, CW], U8, f"bqs{c}") for c in range(C)]
         hq = kept([P, T], U32, "hq")
@@ -83,33 +98,38 @@ def tile_dora_fp8_forward_d2_kernel(tc, x_bytes, x_scale, w_bytes, w_scale, a, l
         def load_b(c):
             nc.sync.dma_start(out=braw[c][:], in_=b_view[:, :, CW * c : CW * (c + 1)])
 
-        xw, xbank, xg = {}, {}, {}
+        xw, xbank, xg, xstep = {}, {}, {}, {}
 
-        def x_widen(u):
-            j, g = divmod(u, G)
+        def x_widen(u, engine):
+            half, g, j = u // 8, u % 8 // 2, u % 2
+            xstep[u] = engine
             xw[u] = xwp.tile([P, 2, 512], BF16, name="xw", align_bytes=64)
             for i in range(2):
                 dst = xw[u][:, i, :].rearrange("p (h m e) -> p m h e", h=2, e=2)
                 for q in range(4):
-                    k = 512 * g + 128 * q
-                    nc.vector.tensor_scalar(
-                        out=dst[:, 32 * q : 32 * (q + 1), :, :],
-                        in0=xb[j][:, i, k : k + 128].bitcast(E4M3),
-                        scalar1=xs[:, 2 * j + i, 4 * g + q : 4 * g + q + 1],
-                        scalar2=None,
-                        op0=MULT,
-                    )
+                    k = 512 * (g % 2) + 128 * q
+                    codes = xb[2 * half + g // 2][:, 2 * j + i, k : k + 128].bitcast(E4M3)
+                    scale = xs[:, 4 * half + 2 * j + i, 4 * g + q : 4 * g + q + 1]
+                    if engine == "v":
+                        nc.vector.tensor_scalar(
+                            out=dst[:, 32 * q : 32 * (q + 1), :, :], in0=codes, scalar1=scale, scalar2=None, op0=MULT
+                        )
+                    else:
+                        nc.scalar.activation(
+                            out=xw[u][:, i, 128 * q : 128 * (q + 1)], in_=codes, func=COPY, scale=scale
+                        )
 
         def x_turn(u):
             xbank[u] = bank(u % 4, [P, 2, 2, P])
             for i in range(2):
                 words = xw[u][:, i, :].bitcast(F32)
                 for h in range(2):
-                    nc.tensor.transpose(xbank[u][:, i, h, :], words[:, P * h : P * (h + 1)], ident[:])
+                    half = words[:, P * h : P * (h + 1)] if xstep[u] == "v" else words[:, h : 2 * P : 2]
+                    nc.tensor.transpose(xbank[u][:, i, h, :], half, ident[:])
 
         def x_out(u):
             if u % 2 == 0:
-                xg[u // 2] = xgp.tile([P, 2, 2, P, 4], BF16, name="xg", align_bytes=64)
+                xg[u // 2] = staged([P, 2, 2, P, 4], "xg")
             words = xg[u // 2][:, u % 2].rearrange("p i r t -> p (i r t)").bitcast(F32)
             nc.scalar.copy(
                 out=words.rearrange("p (i r h) -> p i r h", i=2, h=2),
@@ -117,11 +137,11 @@ def tile_dora_fp8_forward_d2_kernel(tc, x_bytes, x_scale, w_bytes, w_scale, a, l
             )
 
         def x_quant(d):
-            j, e = divmod(d, 2)
+            half, g = divmod(d, G)
             nc.vector.quantize_mx(
-                out=xq[:, j, 2 * e : 2 * e + 2, :].rearrange("p g n -> p (g n)").bitcast(MX),
-                scales=xqs[:, j, 2 * e : 2 * e + 2, :].rearrange("p g n -> p (g n)"),
-                in_=xg[d][:].rearrange("p g i r t -> p (g i r t)"),
+                out=xq[:, half, g, :].bitcast(MX),
+                scales=xqs[:, half, g, :],
+                in_=xg[d][:].rearrange("p j i r t -> p (j i r t)"),
             )
 
         def copy_on(engine, dst, src):
@@ -137,7 +157,7 @@ def tile_dora_fp8_forward_d2_kernel(tc, x_bytes, x_scale, w_bytes, w_scale, a, l
 
         def a_inter(g, e, engine):
             if g not in ag:
-                ag[g] = wgp.tile([P, 4, P, 4], BF16, name="wg", tag="wg", align_bytes=64)
+                ag[g] = staged([P, 4, P, 4], "wga")
             dst = ag[g][:, 2 * e : 2 * e + 2].rearrange("p t m j -> p m j t")
             src = araw[g][:].rearrange("p j (m t) -> p m j t", t=4)[:, :, :, 2 * e : 2 * e + 2]
             copy_on(engine, dst, src)
@@ -149,43 +169,43 @@ def tile_dora_fp8_forward_d2_kernel(tc, x_bytes, x_scale, w_bytes, w_scale, a, l
 
         hbank, hb, hg = {}, {}, {}
 
-        def h_mm(n):
-            j, e = divmod(n, 2)
-            hbank[n] = bank(4 + n % 4, [P, 2, 256])
-            for t in (2 * e, 2 * e + 1):
-                for g in range(G):
-                    nc.tensor.matmul_mx(
-                        out=hbank[n][:, t % 2, :],
-                        lhsT=aq[:, g, P * t : P * (t + 1)].bitcast(MX),
-                        lhsT_scale=aqs[:, g, P * t : P * (t + 1)],
-                        rhs=xq[:, j, g, :].bitcast(MX),
-                        rhs_scale=xqs[:, j, g, :],
-                        start=(g == 0),
-                        stop=(g == G - 1),
-                    )
+        def h_mm(d):
+            half, g = divmod(d, G)
+            for t in range(4):
+                if g == 0:
+                    hbank[half, t] = bank(4 + t, [P, 512])
+                nc.tensor.matmul_mx(
+                    out=hbank[half, t][:],
+                    lhsT=aq[:, g, P * t : P * (t + 1)].bitcast(MX),
+                    lhsT_scale=aqs[:, g, P * t : P * (t + 1)],
+                    rhs=xq[:, half, g, :].bitcast(MX),
+                    rhs_scale=xqs[:, half, g, :],
+                    start=(g == 0),
+                    stop=(g == G - 1),
+                )
 
-        def h_out(n):
-            j, e = divmod(n, 2)
-            if e == 0:
-                hb[j] = hp.tile([P, 4, 256], BF16, name="hb", bufs=4, align_bytes=64)
-            for t in (2 * e, 2 * e + 1):
-                nc.scalar.activation(out=hb[j][:, t, :], in_=hbank[n][:, t % 2, :], func=COPY, scale=lamf[:, t : t + 1])
+        def h_out(half, t):
+            if half not in hb:
+                hb[half] = staged([P, 4, 512], "hb")
+            nc.scalar.activation(out=hb[half][:, t, :], in_=hbank[half, t][:], func=COPY, scale=lamf[:, t : t + 1])
 
-        def h_inter(j):
-            hg[j] = hp.tile([P, 256, 4], BF16, name="hg", align_bytes=64)
-            copy_on("v", *fours(hg[j][:], hb[j][:]))
+        def h_inter(half, e, engine):
+            if half not in hg:
+                hg[half] = staged([P, 512, 4], "hg")
+            n = slice(256 * e, 256 * (e + 1))
+            copy_on(engine, *fours(hg[half][:, n, :], hb[half][:, :, n]))
 
-        def h_quant(j):
-            cols = slice(256 * j, 256 * (j + 1))
+        def h_quant(half):
+            cols = slice(512 * half, 512 * (half + 1))
             nc.vector.quantize_mx(
-                out=hq[:, cols].bitcast(MX), scales=hqs[:, cols], in_=hg[j][:].rearrange("p n t -> p (n t)")
+                out=hq[:, cols].bitcast(MX), scales=hqs[:, cols], in_=hg[half][:].rearrange("p n t -> p (n t)")
             )
 
         bg = {}
 
         def b_inter(c, e, engine):
             if c not in bg:
-                bg[c] = wgp.tile([P, CW, 4], BF16, name="wg", tag="wg", align_bytes=64)
+                bg[c] = staged([P, CW, 4], "wgb")
             n = slice(256 * e, 256 * (e + 1))
             copy_on(engine, *fours(bg[c][:, n, :], braw[c][:, :, n]))
 
@@ -195,124 +215,126 @@ def tile_dora_fp8_forward_d2_kernel(tc, x_bytes, x_scale, w_bytes, w_scale, a, l
         ww, wg, acc, res = {}, {}, {}, {}
 
         def w_widen(v):
-            ww[v] = wwp.tile([P, 4, CW], BF16, name="ww", align_bytes=64)
+            ww[v] = staged([P, 4, CW], "ww")
             nc.scalar.copy(
                 out=ww[v][:].rearrange("p t n -> p (t n)"), in_=wb[v][:].rearrange("p t n -> p (t n)").bitcast(E4M3)
             )
 
-        def w_cols(u, g):
-            n0, width = SUBS[u]
-            return G * (n0 // CW) + g, slice(n0 % CW, n0 % CW + width)
-
-        def w_inter(u, g, engine, blocks):
-            n0, width = SUBS[u]
-            if (u, g) not in wg:
-                wg[u, g] = wgp.tile([P, width, 4], BF16, name="wg", tag="wg", align_bytes=64)
+        def w_inter(v, engine, blocks):
+            c, g = divmod(v, G)
+            if v not in wg:
+                wg[v] = staged([P, CW, 4], "wg")
             for e in blocks:
-                c0 = n0 % CW + 128 * e
-                dst, src = fours(wg[u, g][:, 128 * e : 128 * (e + 1), :], ww[w_cols(u, g)[0]][:, :, c0 : c0 + 128])
-                scale = ws[:, g, n0 // 128 + e : n0 // 128 + e + 1]
+                cols = slice(128 * e, 128 * (e + 1))
+                dst, src = fours(wg[v][:, cols, :], ww[v][:, :, cols])
+                scale = ws[:, g, 4 * c + e : 4 * c + e + 1]
                 if engine == "v":
                     nc.vector.tensor_scalar(out=dst, in0=src, scalar1=scale, scalar2=None, op0=MULT)
                 else:
                     nc.scalar.activation(out=dst, in_=src, func=COPY, scale=scale)
 
-        def w_quant(u, g):
-            v, cols = w_cols(u, g)
-            nc.vector.quantize_mx(
-                out=wq[v][:, cols].bitcast(MX), scales=wqs[v][:, cols], in_=wg[u, g][:].rearrange("p n t -> p (n t)")
-            )
+        def w_quant(v):
+            wq[v] = keep.tile([P, CW], U32, name=f"wq{v}", tag="wq", bufs=2 * G, align_bytes=64)
+            wqs[v] = keep.tile([P, CW], U8, name=f"wqs{v}", tag="wqs", bufs=2 * G, align_bytes=64)
+            nc.vector.quantize_mx(out=wq[v][:].bitcast(MX), scales=wqs[v][:], in_=wg[v][:].rearrange("p n t -> p (n t)"))
 
-        def mm(u, g, tiles):
-            n0, width = SUBS[u]
+        passes = {}
+
+        def mm(c, g, tiles):
             for i in tiles:
-                if g == 0:
-                    acc[u, i] = bank(i, [P, width])
+                if (c, i) not in acc:
+                    acc[c, i] = bank(i, [P, CW])
+                    passes[c, i] = 0
                 if g == G:
-                    cols = w_cols(u, 0)[1]
                     lhs, lhs_s = hq[:, P * i : P * (i + 1)], hqs[:, P * i : P * (i + 1)]
-                    rhs, rhs_s = bq[n0 // CW][:, cols], bqs[n0 // CW][:, cols]
+                    rhs, rhs_s = bq[c][:], bqs[c][:]
                 else:
-                    v, cols = w_cols(u, g)
-                    rows = slice(P * (i % 2), P * (i % 2 + 1))
-                    lhs, lhs_s = xq[:, i // 2, g, rows], xqs[:, i // 2, g, rows]
-                    rhs, rhs_s = wq[v][:, cols], wqs[v][:, cols]
+                    rows = slice(P * (i % 4), P * (i % 4 + 1))
+                    lhs, lhs_s = xq[:, i // 4, g, rows], xqs[:, i // 4, g, rows]
+                    rhs, rhs_s = wq[G * c + g][:], wqs[G * c + g][:]
                 nc.tensor.matmul_mx(
-                    out=acc[u, i][:],
+                    out=acc[c, i][:],
                     lhsT=lhs.bitcast(MX),
                     lhsT_scale=lhs_s,
                     rhs=rhs.bitcast(MX),
                     rhs_scale=rhs_s,
-                    start=(g == 0),
-                    stop=(g == (G if u == 0 else G - 1)),
+                    start=(passes[c, i] == 0),
+                    stop=(passes[c, i] == G),
                 )
+                passes[c, i] = passes[c, i] + 1
 
-        def y_out(u, tiles, per_store):
-            n0, width = SUBS[u]
-            cols = slice(n0, n0 + width)
-            rows = 2 * CW // width
+        def y_out(c, tiles, per_store):
+            cols = slice(CW * c, CW * (c + 1))
             for n, i in enumerate(tiles):
-                if (u, i // rows) not in res:
-                    res[u, i // rows] = big.tile([P, rows, width], F32, name="res", tag="big", align_bytes=64)
-                tile = res[u, i // rows]
-                nc.vector.tensor_tensor(out=tile[:, i % rows, :], in0=acc[u, i][:], in1=sb[:, cols], op=MULT)
+                if (c, i // 2) not in res:
+                    res[c, i // 2] = big.tile([P, 2, CW], F32, name="res", tag="big", align_bytes=64)
+                tile = res[c, i // 2]
+                nc.vector.tensor_tensor(out=tile[:, i % 2, :], in0=acc[c, i][:], in1=sb[:, cols], op=MULT)
                 if (n + 1) % per_store == 0:
                     i0 = min(tiles[n + 1 - per_store : n + 1])
                     nc.sync.dma_start(
-                        out=out_view[:, i0 : i0 + per_store, cols], in_=tile[:, i0 % rows : i0 % rows + per_store, :]
+                        out=out_view[:, i0 : i0 + per_store, cols], in_=tile[:, i0 % 2 : i0 % 2 + per_store, :]
                     )
 
         A, B = [0, 1, 2, 3], [4, 5, 6, 7]
-        units = [(u, g) for u in range(len(SUBS)) for g in range(G)]
-
-        def vector_blocks(u, g):
-            return (4 - g % 2, 3 - g % 2, 2)[u]
+        UNITS = C * G
 
         with tc.manual_schedule(
             engines={mybir.EngineType.PE, mybir.EngineType.DVE, mybir.EngineType.Activation, mybir.EngineType.SP}
         ):
-            half = K // 2
+            def load_x(half, g, passes):
+                k = 512 * (g % 2)
+                nc.sync.dma_start(
+                    out=xb[2 * half + g // 2][:, :, k : k + 512 * passes],
+                    in_=x_view[:, 4 * half : 4 * half + 4, 512 * g : 512 * (g + passes)],
+                )
+
             nc.scalar.dma_start(out=xs[:], in_=x_scale.rearrange("(p i) k -> p i k", i=TILES))
-            nc.sync.dma_start(out=xb[0][:, :, 0:half], in_=x_view[:, 0:2, 0:half])
-            load_w(0)
+            load_x(0, 0, 1)
             nc.sync.dma_start(out=araw[0][:], in_=a_view[0])
-            nc.sync.dma_start(out=xb[0][:, :, half:K], in_=x_view[:, 0:2, half:K])
-            nc.scalar.dma_start(
-                out=wsall[:].rearrange("p g q n -> p (g q n)"),
-                in_=w_scale.rearrange("k n -> (k n)").partition_broadcast(P),
-            )
+            load_x(0, 1, 1)
+            nc.sync.dma_start(out=araw[1][:], in_=a_view[1])
+            load_x(0, 2, 2)
+            nc.sync.dma_start(out=araw[2][:], in_=a_view[2])
+            nc.sync.dma_start(out=araw[3][:], in_=a_view[3])
             nc.scalar.dma_start(out=lamb[:], in_=lam.rearrange("(p t) -> p t", t=4))
-            for g in range(1, G):
-                nc.sync.dma_start(out=araw[g][:], in_=a_view[g])
+            load_x(1, 0, 2)
+            load_x(1, 2, 2)
+            ws_view = w_scale.rearrange("(g q) n -> q g n", q=4)
+            for q in range(4):
+                nc.sync.dma_start(out=ws[32 * q : 32 * (q + 1), :, 0 : N // 128], in_=ws_view[q].partition_broadcast(32))
             nc.sync.dma_start(out=magb[:], in_=mag.rearrange("(p j) -> p j", p=64))
             nc.sync.dma_start(out=normb[:], in_=norm.rearrange("(p j) -> p j", p=64))
-            for j in range(1, PAIRS):
-                nc.sync.dma_start(out=xb[j][:], in_=x_view[:, 2 * j : 2 * j + 2, :])
-                load_w(j)
+            for v in range(G):
+                load_w(v)
             load_b(0)
 
-            w_widen(0)
-            for d in range(2 * PAIRS):
-                for u in (2 * d, 2 * d + 1):
-                    x_widen(u)
-                    x_turn(u)
-                    if u > 0:
-                        x_out(u - 1)
-                    if u < G:
-                        a_inter(u, 1, "s")
-                        a_inter(u, 0, "v")
-                    if 1 <= u <= G:
-                        a_quant(u - 1)
-                    if u % 2 == 0 and d >= 4:
-                        h_out(d - 4)
-                if d == 2:
+            def w_shares(v):
+                while len(ww) <= min(v + LOOK, UNITS - 1):
+                    w_widen(len(ww))
+                w_inter(v, "s", range(4 - v // G, 4))
+                w_inter(v, "v", range(4 - v // G))
+
+            nq, nh, nho = 0, 0, 0
+            for u in range(4 * G):
+                x_widen(u, "s" if u in XW_S else "v")
+                x_turn(u)
+                if u >= XO_LAG:
+                    x_out(u - XO_LAG)
+                if 0 <= u - A_LAG < 2 * G:
+                    g, e = divmod(u - A_LAG, 2)
+                    a_inter(g, 1 - e, A_ENG[2 * g + e])
+                if nh >= G and u >= HO_AT:
+                    for t in range(nho, min(nho + HO_PER, 4)):
+                        h_out(0, t)
+                        nho = nho + 1
+                if u in WW_AT:
+                    w_widen(len(ww))
+                if u == G:
                     nc.scalar.copy(out=lamf[:], in_=lamb[:])
-                    nc.scalar.copy(out=ws[0:32, :, :], in_=wsall[0:32, :, 0, :])
+                if u == SMALL_AT:
                     nc.vector.reciprocal(out=rec[:], in_=normb[:])
-                if 3 <= d < 6:
-                    rows = slice(32 * (d - 2), 32 * (d - 1))
-                    nc.scalar.copy(out=ws[rows, :, :], in_=wsall[rows, :, d - 2, :])
-                if d == 3:
+                if u == SMALL_AT + 1:
                     nc.vector.tensor_tensor(out=s1[:], in0=magb[:], in1=rec[:], op=MULT)
                     nc.sync.dma_start(out=out[0].rearrange("(p j) -> p j", p=64), in_=s1[:])
                     for v in range(G, 2 * G):
@@ -322,74 +344,82 @@ def tile_dora_fp8_forward_d2_kernel(tc, x_bytes, x_scale, w_bytes, w_scale, a, l
                     for v in range(2 * G, 3 * G):
                         load_w(v)
                     load_b(2)
-                if d in (2,):
-                    w_widen(len(ww))
-                if d in (2, 3):
-                    b_inter(0, int(0 in bg), "s")
-                if d == 2 * PAIRS - 1:
-                    w_inter(0, 0, "v", range(4))
-                if d > 0:
-                    x_quant(d - 1)
-                if d == 5:
-                    b_quant(0)
-                if d >= 3:
-                    h_mm(d - 3)
-            x_out(4 * PAIRS - 1)
-            h_out(4)
-            h_inter(0)
-            x_quant(2 * PAIRS - 1)
-            h_mm(5)
-            h_mm(6)
-            h_out(5)
+                if u == W0_AT:
+                    w_shares(0)
+                g, e = divmod(u - A_LAG - QA_LAG - 1, 2)
+                if e == 0 and 0 <= g < G:
+                    a_quant(g)
+                if u >= 2 * nq + 1 + (QX_LAG if nq < G else QX_LAG2):
+                    x_quant(nq)
+                    nq = nq + 1
+                if nh < nq and u >= 2 * nh + 1 + A_LAG + QA_LAG and (nh < G or nho == 4) and u >= 2 * nh + 1 + H_LAG:
+                    h_mm(nh)
+                    nh = nh + 1
+            for u in range(4 * G - XO_LAG, 4 * G):
+                x_out(u)
+            for d in range(nq, 2 * G - 1):
+                x_quant(d)
+            for d in range(nh, 2 * G - 1):
+                h_mm(d)
+            w_shares(1)
+            w_quant(0)
+            x_quant(2 * G - 1)
+            mm(0, 0, A)
+            h_mm(2 * G - 1)
+            h_inter(0, 0, HI_ENG[0])
+            w_quant(1)
+            mm(0, 1, A)
+            w_shares(2)
+            for t in range(4):
+                h_out(1, t)
+            h_inter(0, 1, HI_ENG[1])
+            w_quant(2)
+            mm(0, 2, A)
+            mm(0, 0, B)
+            mm(0, 1, B)
+            b_inter(0, 0, B0_ENG[0])
+            b_inter(0, 1, B0_ENG[1])
+            w_shares(3)
+            h_quant(0)
+            h_inter(1, 0, HI_ENG[2])
+            b_quant(0)
+            mm(0, G, A)
 
-            last = len(SUBS) - 1
-            for n, (u, g) in enumerate(units):
-                if n + 1 < len(units):
-                    nu, ng = units[n + 1]
-                    w_inter(nu, ng, "s", range(vector_blocks(nu, ng), 4))
-                if n < 2:
-                    h_out(6 + n)
-                if len(ww) < C * G:
-                    w_widen(len(ww))
-                if u > 0 and g < 2:
-                    b_inter(u, g, "s")
-                w_quant(u, g)
-                if n < PAIRS:
-                    h_quant(n)
-                if g == 1 and u > 0:
-                    y_out(u - 1, A, 2)
-                if n + 1 < len(units):
-                    w_inter(nu, ng, "v", range(vector_blocks(nu, ng)))
-                if n + 1 < PAIRS:
-                    h_inter(n + 1)
-                if g == 2 and u > 0:
-                    b_quant(u)
-                if n == 0:
-                    mm(0, 0, A)
-                    h_mm(7)
-                if g == 1:
-                    if u > 0:
-                        mm(u, 0, A)
-                    mm(u, 1, A)
-                    if u > 0:
-                        y_out(u - 1, B, 2)
-                    mm(u, 0, B)
-                    mm(u, 1, B)
-                if g == 2:
-                    mm(u, 2, A)
-                    if u > 0:
-                        mm(u, G, A)
-                if g == 3:
-                    mm(u, 3, A)
-                    order = (2, G, 3)
-                    if u == 0:
-                        mm(u, G, A)
-                        order = (2, 3, G)
-                    if u < last:
-                        for e in order:
-                            mm(u, e, B)
-            y_out(last, A, 2)
-            for i in B:
-                for e in (2, G, 3):
-                    mm(last, e, [i])
-                y_out(last, [i], 1)
+            a_t, b_t = A, B
+            for c in range(C - 1):
+                v = G * (c + 1)
+                w_shares(v)
+                w_quant(v - 1)
+                mm(c, 3, a_t)
+                mm(c, 2, b_t)
+                mm(c, 3, b_t)
+                if c == 0:
+                    h_inter(1, 1, HI_ENG[3])
+                w_shares(v + 1)
+                if c == 0:
+                    h_quant(1)
+                mm(c, G, b_t)
+                w_quant(v)
+                if REV:
+                    a_t, b_t = a_t[::-1], b_t[::-1]
+                y_out(c, a_t, 2)
+                mm(c + 1, 0, a_t)
+                w_quant(v + 1)
+                mm(c + 1, 1, a_t)
+                w_shares(v + 2)
+                b_inter(c + 1, 0, "s")
+                b_inter(c + 1, 1, "s")
+                y_out(c, b_t, 2)
+                mm(c + 1, 0, b_t)
+                mm(c + 1, 1, b_t)
+                w_quant(v + 2)
+                w_shares(v + 3)
+                b_quant(c + 1)
+                if c + 2 < C:
+                    mm(c + 1, 2, a_t)
+                    mm(c + 1, G, a_t)
+            w_quant(UNITS - 1)
+            for i in a_t + b_t:
+                for g in (2, G, 3):
+                    mm(C - 1, g, [i])
+                y_out(C - 1, [i], 1)

@@ -16,29 +16,23 @@ MULT = mybir.AluOpType.mult
 COPY = mybir.ActivationFunctionType.Copy
 
 P = 128
-G = K // 512
+PASSES = K // 512
+UPDATE = PASSES
 TILES = T // P
-PAIRS = TILES // 2
 CW = 512
-C = N // CW
-XW_BUFS = 6
-XW_S = [1, 9]
-A_ENG = "svsvsvsv"
-A_LAG = 1
-XO_LAG = 2
-QA_LAG = 1
-QX_LAG = 2
-QX_LAG2 = 4
-H_LAG = 2
-SMALL_AT = 10
-HO_AT = 11
-HO_PER = 4
-W0_AT = 15
-WW_AT = [9,15]
-LOOK = 1
-HI_ENG = "vvvv"
-B0_ENG = "vs"
-REV = True
+CHUNKS = N // CW
+X_UNITS = 4 * PASSES
+W_UNITS = CHUNKS * PASSES
+
+X_ON_SCALAR = (1, 3)
+A_ON_SCALAR = range(4, 7)
+W_WIDEN_FROM = 9
+
+
+def vector_blocks(v):
+    if v < PASSES:
+        return 4
+    return 3 if v < W_UNITS - 2 else 2
 
 
 def tile_dora_fp8_forward_d2_kernel(tc, x_bytes, x_scale, w_bytes, w_scale, a, lam, b, mag, norm, out):
@@ -46,7 +40,7 @@ def tile_dora_fp8_forward_d2_kernel(tc, x_bytes, x_scale, w_bytes, w_scale, a, l
     with ExitStack() as ctx:
         keep = ctx.enter_context(tc.tile_pool(name="keep", bufs=1))
         big = ctx.enter_context(tc.tile_pool(name="big", bufs=14))
-        xwp = ctx.enter_context(tc.tile_pool(name="xwp", bufs=XW_BUFS))
+        widened = ctx.enter_context(tc.tile_pool(name="widened", bufs=6))
         stage = ctx.enter_context(tc.tile_pool(name="stage", bufs=14))
         psum = ctx.enter_context(tc.psum_pool(name="psum", bufs=1))
 
@@ -61,62 +55,80 @@ def tile_dora_fp8_forward_d2_kernel(tc, x_bytes, x_scale, w_bytes, w_scale, a, l
 
         ident = kept([P, P], F32, "ident")
         xs = kept([P, TILES, K // 128], F32, "xs")
-        ws = kept([P, G, 16], F32, "ws")
-        lamb = kept([P, 4], BF16, "lamb")
-        lamf = kept([P, 4], F32, "lamf")
-        magb = kept([64, N // 64], BF16, "magb")
-        normb = kept([64, N // 64], BF16, "normb")
-        rec = kept([64, N // 64], F32, "rec")
-        s1 = kept([64, N // 64], F32, "s1")
-        sb = kept([P, N], F32, "sb")
+        ws = kept([P, PASSES, 16], F32, "ws")
+        lam_rows = kept([P, P], BF16, "lam_rows")
+        ident_bf = kept([P, P], BF16, "ident_bf")
+        lam_cols = kept([P, 4], F32, "lam_cols")
+        mag_sb = kept([64, N // 64], BF16, "mag_sb")
+        norm_sb = kept([64, N // 64], BF16, "norm_sb")
+        inv_norm = kept([64, N // 64], F32, "inv_norm")
+        gain_rows = kept([64, N // 64], F32, "gain_rows")
+        gain = kept([P, N], F32, "gain")
         xb = [big.tile([P, 4, K // 2], U8, name=f"xb{n}", tag="big", align_bytes=64) for n in range(4)]
-        araw = [big.tile([P, 4, R], BF16, name=f"araw{g}", tag="big", align_bytes=64) for g in range(G)]
-        wb = [kept([P, 4, CW], U8, f"wb{v}") for v in range(C * G)]
-        braw = [kept([P, 4, CW], BF16, f"braw{c}") for c in range(C)]
-        xq = kept([P, 2, G, 512], U32, "xq")
-        xqs = kept([P, 2, G, 512], U8, "xqs")
-        aq = kept([P, G, R], U32, "aq")
-        aqs = kept([P, G, R], U8, "aqs")
+        araw = [big.tile([P, 4, R], BF16, name=f"araw{g}", tag="big", align_bytes=64) for g in range(PASSES)]
+        wb = [kept([P, 4, CW], U8, f"wb{v}") for v in range(W_UNITS)]
+        braw = kept([P, 4, N], BF16, "braw")
+        xq = kept([P, 2, PASSES, 512], U32, "xq")
+        xqs = kept([P, 2, PASSES, 512], U8, "xqs")
+        aq = kept([P, PASSES, R], U32, "aq")
+        aqs = kept([P, PASSES, R], U8, "aqs")
         wq, wqs = {}, {}
-        bq = [kept([P, CW], U32, f"bq{c}") for c in range(C)]
-        bqs = [kept([P, CW], U8, f"bqs{c}") for c in range(C)]
+        bq = [kept([P, CW], U32, f"bq{c}") for c in range(CHUNKS)]
+        bqs = [kept([P, CW], U8, f"bqs{c}") for c in range(CHUNKS)]
         hq = kept([P, T], U32, "hq")
         hqs = kept([P, T], U8, "hqs")
 
         x_view = x_bytes.rearrange("(p i) k -> p i k", i=TILES)
         a_view = a.rearrange("(g p t) r -> g p t r", p=P, t=4)
         w_view = w_bytes.rearrange("(g p t) n -> g p t n", p=P, t=4)
-        b_view = b.rearrange("(p t) n -> p t n", t=4)
+        b_view = b.rearrange("(q t i) n -> t q i n", t=4, i=8)
         out_view = out.rearrange("(p i) n -> p i n", i=TILES)
 
+        nc.gpsimd.memset(lam_rows[:], 0.0)
         make_identity(nc, ident[:])
+        make_identity(nc, ident_bf[:])
 
-        def load_w(v):
-            c, g = divmod(v, G)
-            nc.sync.dma_start(out=wb[v][:], in_=w_view[g][:, :, CW * c : CW * (c + 1)])
+        def load_x(half, g, passes):
+            k = 512 * (g % 2)
+            nc.sync.dma_start(
+                out=xb[2 * half + g // 2][:, :, k : k + 512 * passes],
+                in_=x_view[:, 4 * half : 4 * half + 4, 512 * g : 512 * (g + passes)],
+            )
 
-        def load_b(c):
-            nc.sync.dma_start(out=braw[c][:], in_=b_view[:, :, CW * c : CW * (c + 1)])
+        def load_w(c):
+            for g in range(PASSES):
+                nc.sync.dma_start(out=wb[PASSES * c + g][:], in_=w_view[g][:, :, CW * c : CW * (c + 1)])
 
-        xw, xbank, xg, xstep = {}, {}, {}, {}
+        def copy_on(engine, dst, src):
+            if engine == "vector":
+                nc.vector.tensor_copy(out=dst, in_=src)
+            else:
+                nc.scalar.copy(out=dst, in_=src)
 
-        def x_widen(u, engine):
+        def fours(dst, src):
+            return dst.rearrange("p (c i) t -> p c t i", i=4), src.rearrange("p t (c i) -> p c t i", i=4)
+
+        def quantise(codes, scales, values):
+            nc.vector.quantize_mx(out=codes.bitcast(MX), scales=scales, in_=values)
+
+        xw, xbank, xg = {}, {}, {}
+
+        def x_widen(u):
             half, g, j = u // 8, u % 8 // 2, u % 2
-            xstep[u] = engine
-            xw[u] = xwp.tile([P, 2, 512], BF16, name="xw", align_bytes=64)
+            xw[u] = widened.tile([P, 2, 512], BF16, name="xw", align_bytes=64)
             for i in range(2):
-                dst = xw[u][:, i, :].rearrange("p (h m e) -> p m h e", h=2, e=2)
+                runs = xw[u][:, i, :].rearrange("p (h m e) -> p m h e", h=2, e=2)
                 for q in range(4):
                     k = 512 * (g % 2) + 128 * q
                     codes = xb[2 * half + g // 2][:, 2 * j + i, k : k + 128].bitcast(E4M3)
                     scale = xs[:, 4 * half + 2 * j + i, 4 * g + q : 4 * g + q + 1]
-                    if engine == "v":
-                        nc.vector.tensor_scalar(
-                            out=dst[:, 32 * q : 32 * (q + 1), :, :], in0=codes, scalar1=scale, scalar2=None, op0=MULT
-                        )
-                    else:
+                    if u in X_ON_SCALAR:
                         nc.scalar.activation(
                             out=xw[u][:, i, 128 * q : 128 * (q + 1)], in_=codes, func=COPY, scale=scale
+                        )
+                    else:
+                        nc.vector.tensor_scalar(
+                            out=runs[:, 32 * q : 32 * (q + 1), :, :], in0=codes, scalar1=scale, scalar2=None, op0=MULT
                         )
 
         def x_turn(u):
@@ -124,8 +136,8 @@ def tile_dora_fp8_forward_d2_kernel(tc, x_bytes, x_scale, w_bytes, w_scale, a, l
             for i in range(2):
                 words = xw[u][:, i, :].bitcast(F32)
                 for h in range(2):
-                    half = words[:, P * h : P * (h + 1)] if xstep[u] == "v" else words[:, h : 2 * P : 2]
-                    nc.tensor.transpose(xbank[u][:, i, h, :], half, ident[:])
+                    src = words[:, h : 2 * P : 2] if u in X_ON_SCALAR else words[:, P * h : P * (h + 1)]
+                    nc.tensor.transpose(xbank[u][:, i, h, :], src, ident[:])
 
         def x_out(u):
             if u % 2 == 0:
@@ -137,40 +149,25 @@ def tile_dora_fp8_forward_d2_kernel(tc, x_bytes, x_scale, w_bytes, w_scale, a, l
             )
 
         def x_quant(d):
-            half, g = divmod(d, G)
-            nc.vector.quantize_mx(
-                out=xq[:, half, g, :].bitcast(MX),
-                scales=xqs[:, half, g, :],
-                in_=xg[d][:].rearrange("p j i r t -> p (j i r t)"),
-            )
+            half, g = divmod(d, PASSES)
+            quantise(xq[:, half, g, :], xqs[:, half, g, :], xg[d][:].rearrange("p j i r t -> p (j i r t)"))
 
-        def copy_on(engine, dst, src):
-            if engine == "v":
-                nc.vector.tensor_copy(out=dst, in_=src)
-            else:
-                nc.scalar.copy(out=dst, in_=src)
+        ag, hbank, hb, hg = {}, {}, {}, {}
 
-        def fours(dst, src):
-            return dst.rearrange("p (c i) t -> p c t i", i=4), src.rearrange("p t (c i) -> p c t i", i=4)
-
-        ag = {}
-
-        def a_inter(g, e, engine):
+        def a_inter(n):
+            g, e = n // 2, 1 - n % 2
             if g not in ag:
                 ag[g] = staged([P, 4, P, 4], "wga")
-            dst = ag[g][:, 2 * e : 2 * e + 2].rearrange("p t m j -> p m j t")
-            src = araw[g][:].rearrange("p j (m t) -> p m j t", t=4)[:, :, :, 2 * e : 2 * e + 2]
-            copy_on(engine, dst, src)
+            for t in (2 * e, 2 * e + 1):
+                dst = ag[g][:, t].rearrange("p (q c i) j -> p q c j i", c=2, i=4)
+                src = araw[g][:].rearrange("p j (q t c i) -> p t q c j i", t=4, c=2, i=4)[:, t]
+                copy_on("scalar" if n in A_ON_SCALAR else "vector", dst, src)
 
         def a_quant(g):
-            nc.vector.quantize_mx(
-                out=aq[:, g, :].bitcast(MX), scales=aqs[:, g, :], in_=ag[g][:].rearrange("p t m j -> p (t m j)")
-            )
-
-        hbank, hb, hg = {}, {}, {}
+            quantise(aq[:, g, :], aqs[:, g, :], ag[g][:].rearrange("p t m j -> p (t m j)"))
 
         def h_mm(d):
-            half, g = divmod(d, G)
+            half, g = divmod(d, PASSES)
             for t in range(4):
                 if g == 0:
                     hbank[half, t] = bank(4 + t, [P, 512])
@@ -181,38 +178,34 @@ def tile_dora_fp8_forward_d2_kernel(tc, x_bytes, x_scale, w_bytes, w_scale, a, l
                     rhs=xq[:, half, g, :].bitcast(MX),
                     rhs_scale=xqs[:, half, g, :],
                     start=(g == 0),
-                    stop=(g == G - 1),
+                    stop=(g == PASSES - 1),
                 )
 
         def h_out(half, t):
             if half not in hb:
                 hb[half] = staged([P, 4, 512], "hb")
-            nc.scalar.activation(out=hb[half][:, t, :], in_=hbank[half, t][:], func=COPY, scale=lamf[:, t : t + 1])
+            nc.scalar.activation(out=hb[half][:, t, :], in_=hbank[half, t][:], func=COPY, scale=lam_cols[:, t : t + 1])
 
-        def h_inter(half, e, engine):
+        def h_inter(half, e):
             if half not in hg:
                 hg[half] = staged([P, 512, 4], "hg")
             n = slice(256 * e, 256 * (e + 1))
-            copy_on(engine, *fours(hg[half][:, n, :], hb[half][:, :, n]))
+            copy_on("vector", *fours(hg[half][:, n, :], hb[half][:, :, n]))
 
         def h_quant(half):
             cols = slice(512 * half, 512 * (half + 1))
-            nc.vector.quantize_mx(
-                out=hq[:, cols].bitcast(MX), scales=hqs[:, cols], in_=hg[half][:].rearrange("p n t -> p (n t)")
-            )
+            quantise(hq[:, cols], hqs[:, cols], hg[half][:].rearrange("p n t -> p (n t)"))
 
-        bg = {}
+        bg, ww, wg = {}, {}, {}
 
         def b_inter(c, e, engine):
             if c not in bg:
                 bg[c] = staged([P, CW, 4], "wgb")
-            n = slice(256 * e, 256 * (e + 1))
-            copy_on(engine, *fours(bg[c][:, n, :], braw[c][:, :, n]))
+            n0 = 256 * e
+            copy_on(engine, *fours(bg[c][:, n0 : n0 + 256, :], braw[:, :, CW * c + n0 : CW * c + n0 + 256]))
 
         def b_quant(c):
-            nc.vector.quantize_mx(out=bq[c][:].bitcast(MX), scales=bqs[c][:], in_=bg[c][:].rearrange("p n t -> p (n t)"))
-
-        ww, wg, acc, res = {}, {}, {}, {}
+            quantise(bq[c][:], bqs[c][:], bg[c][:].rearrange("p n t -> p (n t)"))
 
         def w_widen(v):
             ww[v] = staged([P, 4, CW], "ww")
@@ -220,206 +213,198 @@ def tile_dora_fp8_forward_d2_kernel(tc, x_bytes, x_scale, w_bytes, w_scale, a, l
                 out=ww[v][:].rearrange("p t n -> p (t n)"), in_=wb[v][:].rearrange("p t n -> p (t n)").bitcast(E4M3)
             )
 
-        def w_inter(v, engine, blocks):
-            c, g = divmod(v, G)
-            if v not in wg:
-                wg[v] = staged([P, CW, 4], "wg")
-            for e in blocks:
+        def w_inter(v):
+            c, g = divmod(v, PASSES)
+            if v + 1 < W_UNITS and v + 1 not in ww:
+                w_widen(v + 1)
+            wg[v] = staged([P, CW, 4], "wg")
+            for e in [*range(vector_blocks(v), 4), *range(vector_blocks(v))]:
                 cols = slice(128 * e, 128 * (e + 1))
                 dst, src = fours(wg[v][:, cols, :], ww[v][:, :, cols])
                 scale = ws[:, g, 4 * c + e : 4 * c + e + 1]
-                if engine == "v":
+                if e < vector_blocks(v):
                     nc.vector.tensor_scalar(out=dst, in0=src, scalar1=scale, scalar2=None, op0=MULT)
                 else:
                     nc.scalar.activation(out=dst, in_=src, func=COPY, scale=scale)
 
         def w_quant(v):
-            wq[v] = keep.tile([P, CW], U32, name=f"wq{v}", tag="wq", bufs=2 * G, align_bytes=64)
-            wqs[v] = keep.tile([P, CW], U8, name=f"wqs{v}", tag="wqs", bufs=2 * G, align_bytes=64)
-            nc.vector.quantize_mx(out=wq[v][:].bitcast(MX), scales=wqs[v][:], in_=wg[v][:].rearrange("p n t -> p (n t)"))
+            wq[v] = keep.tile([P, CW], U32, name=f"wq{v}", tag="wq", bufs=2 * PASSES, align_bytes=64)
+            wqs[v] = keep.tile([P, CW], U8, name=f"wqs{v}", tag="wqs", bufs=2 * PASSES, align_bytes=64)
+            quantise(wq[v][:], wqs[v][:], wg[v][:].rearrange("p n t -> p (n t)"))
 
-        passes = {}
+        acc, done, res = {}, {}, {}
 
-        def mm(c, g, tiles):
+        def y_mm(c, g, tiles):
             for i in tiles:
                 if (c, i) not in acc:
                     acc[c, i] = bank(i, [P, CW])
-                    passes[c, i] = 0
-                if g == G:
+                    done[c, i] = 0
+                if g == UPDATE:
                     lhs, lhs_s = hq[:, P * i : P * (i + 1)], hqs[:, P * i : P * (i + 1)]
                     rhs, rhs_s = bq[c][:], bqs[c][:]
                 else:
                     rows = slice(P * (i % 4), P * (i % 4 + 1))
                     lhs, lhs_s = xq[:, i // 4, g, rows], xqs[:, i // 4, g, rows]
-                    rhs, rhs_s = wq[G * c + g][:], wqs[G * c + g][:]
+                    rhs, rhs_s = wq[PASSES * c + g][:], wqs[PASSES * c + g][:]
                 nc.tensor.matmul_mx(
                     out=acc[c, i][:],
                     lhsT=lhs.bitcast(MX),
                     lhsT_scale=lhs_s,
                     rhs=rhs.bitcast(MX),
                     rhs_scale=rhs_s,
-                    start=(passes[c, i] == 0),
-                    stop=(passes[c, i] == G),
+                    start=(done[c, i] == 0),
+                    stop=(done[c, i] == PASSES),
                 )
-                passes[c, i] = passes[c, i] + 1
+                done[c, i] = done[c, i] + 1
 
-        def y_out(c, tiles, per_store):
-            cols = slice(CW * c, CW * (c + 1))
+        def y_scale(c, i, part):
+            if (c, i // 2) not in res:
+                res[c, i // 2] = big.tile([P, 2, CW], F32, name="res", tag="big", align_bytes=64)
+            cols = slice(CW * c + part.start, CW * c + part.stop)
+            nc.vector.tensor_tensor(out=res[c, i // 2][:, i % 2, part], in0=acc[c, i][:, part], in1=gain[:, cols], op=MULT)
+
+        def y_out(c, tiles):
             for n, i in enumerate(tiles):
-                if (c, i // 2) not in res:
-                    res[c, i // 2] = big.tile([P, 2, CW], F32, name="res", tag="big", align_bytes=64)
-                tile = res[c, i // 2]
-                nc.vector.tensor_tensor(out=tile[:, i % 2, :], in0=acc[c, i][:], in1=sb[:, cols], op=MULT)
-                if (n + 1) % per_store == 0:
-                    i0 = min(tiles[n + 1 - per_store : n + 1])
-                    nc.sync.dma_start(
-                        out=out_view[:, i0 : i0 + per_store, cols], in_=tile[:, i0 % 2 : i0 % 2 + per_store, :]
-                    )
+                y_scale(c, i, slice(0, CW))
+                if n % 2 == 1:
+                    i0 = i - i % 2
+                    nc.sync.dma_start(out=out_view[:, i0 : i0 + 2, CW * c : CW * (c + 1)], in_=res[c, i // 2][:])
 
-        A, B = [0, 1, 2, 3], [4, 5, 6, 7]
-        UNITS = C * G
+        group_a, group_b = [0, 1, 2, 3], [4, 5, 6, 7]
 
         with tc.manual_schedule(
             engines={mybir.EngineType.PE, mybir.EngineType.DVE, mybir.EngineType.Activation, mybir.EngineType.SP}
         ):
-            def load_x(half, g, passes):
-                k = 512 * (g % 2)
-                nc.sync.dma_start(
-                    out=xb[2 * half + g // 2][:, :, k : k + 512 * passes],
-                    in_=x_view[:, 4 * half : 4 * half + 4, 512 * g : 512 * (g + passes)],
-                )
-
             nc.scalar.dma_start(out=xs[:], in_=x_scale.rearrange("(p i) k -> p i k", i=TILES))
-            load_x(0, 0, 1)
+            for j in range(2):
+                nc.sync.dma_start(out=xb[0][:, 2 * j : 2 * j + 2, 0:512], in_=x_view[:, 2 * j : 2 * j + 2, 0:512])
             nc.sync.dma_start(out=araw[0][:], in_=a_view[0])
+            nc.scalar.dma_start(out=norm_sb[:], in_=norm.rearrange("(p j) -> p j", p=64))
+            nc.scalar.dma_start(out=mag_sb[:], in_=mag.rearrange("(p j) -> p j", p=64))
+            nc.scalar.dma_start(
+                out=lam_rows[0:4, :].rearrange("t (q i) -> t q i", i=8),
+                in_=lam.rearrange("(q t i) -> t q i", t=4, i=8),
+            )
             load_x(0, 1, 1)
             nc.sync.dma_start(out=araw[1][:], in_=a_view[1])
             load_x(0, 2, 2)
             nc.sync.dma_start(out=araw[2][:], in_=a_view[2])
             nc.sync.dma_start(out=araw[3][:], in_=a_view[3])
-            nc.scalar.dma_start(out=lamb[:], in_=lam.rearrange("(p t) -> p t", t=4))
             load_x(1, 0, 2)
             load_x(1, 2, 2)
             ws_view = w_scale.rearrange("(g q) n -> q g n", q=4)
             for q in range(4):
                 nc.sync.dma_start(out=ws[32 * q : 32 * (q + 1), :, 0 : N // 128], in_=ws_view[q].partition_broadcast(32))
-            nc.sync.dma_start(out=magb[:], in_=mag.rearrange("(p j) -> p j", p=64))
-            nc.sync.dma_start(out=normb[:], in_=norm.rearrange("(p j) -> p j", p=64))
-            for v in range(G):
-                load_w(v)
-            load_b(0)
+            load_w(0)
+            for t in range(4):
+                nc.sync.dma_start(out=braw[:, t, :], in_=b_view[t])
 
-            def w_shares(v):
-                while len(ww) <= min(v + LOOK, UNITS - 1):
-                    w_widen(len(ww))
-                w_inter(v, "s", range(4 - v // G, 4))
-                w_inter(v, "v", range(4 - v // G))
-
-            nq, nh, nho = 0, 0, 0
-            for u in range(4 * G):
-                x_widen(u, "s" if u in XW_S else "v")
+            last_h = 2 * (PASSES - 1) + 5
+            for u in range(X_UNITS):
+                x_widen(u)
                 x_turn(u)
-                if u >= XO_LAG:
-                    x_out(u - XO_LAG)
-                if 0 <= u - A_LAG < 2 * G:
-                    g, e = divmod(u - A_LAG, 2)
-                    a_inter(g, 1 - e, A_ENG[2 * g + e])
-                if nh >= G and u >= HO_AT:
-                    for t in range(nho, min(nho + HO_PER, 4)):
-                        h_out(0, t)
-                        nho = nho + 1
-                if u in WW_AT:
-                    w_widen(len(ww))
-                if u == G:
-                    nc.scalar.copy(out=lamf[:], in_=lamb[:])
-                if u == SMALL_AT:
-                    nc.vector.reciprocal(out=rec[:], in_=normb[:])
-                if u == SMALL_AT + 1:
-                    nc.vector.tensor_tensor(out=s1[:], in0=magb[:], in1=rec[:], op=MULT)
-                    nc.sync.dma_start(out=out[0].rearrange("(p j) -> p j", p=64), in_=s1[:])
-                    for v in range(G, 2 * G):
-                        load_w(v)
-                    nc.sync.dma_start(out=sb[:], in_=out[0].partition_broadcast(P))
-                    load_b(1)
-                    for v in range(2 * G, 3 * G):
-                        load_w(v)
-                    load_b(2)
-                if u == W0_AT:
-                    w_shares(0)
-                g, e = divmod(u - A_LAG - QA_LAG - 1, 2)
-                if e == 0 and 0 <= g < G:
-                    a_quant(g)
-                if u >= 2 * nq + 1 + (QX_LAG if nq < G else QX_LAG2):
-                    x_quant(nq)
-                    nq = nq + 1
-                if nh < nq and u >= 2 * nh + 1 + A_LAG + QA_LAG and (nh < G or nho == 4) and u >= 2 * nh + 1 + H_LAG:
-                    h_mm(nh)
-                    nh = nh + 1
-            for u in range(4 * G - XO_LAG, 4 * G):
-                x_out(u)
-            for d in range(nq, 2 * G - 1):
-                x_quant(d)
-            for d in range(nh, 2 * G - 1):
-                h_mm(d)
-            w_shares(1)
+                if u >= 2:
+                    x_out(u - 2)
+                if 1 <= u <= 2 * PASSES:
+                    a_inter(u - 1)
+                if u > last_h:
+                    h_out(0, u - last_h - 1)
+                if u in (W_WIDEN_FROM, W_WIDEN_FROM + 1):
+                    w_widen(u - W_WIDEN_FROM)
+                if u == 0:
+                    lam_turned = bank(7, [P, P], BF16)
+                    nc.tensor.transpose(lam_turned[:], lam_rows[:], ident_bf[:])
+                    nc.vector.reciprocal(out=inv_norm[:], in_=norm_sb[:])
+                if u == 1:
+                    nc.scalar.copy(out=lam_cols[:], in_=lam_turned[:, 0:4])
+                    nc.vector.tensor_tensor(out=gain_rows[:], in0=mag_sb[:], in1=inv_norm[:], op=MULT)
+                if u == W_WIDEN_FROM:
+                    nc.sync.dma_start(out=out[0].rearrange("(p j) -> p j", p=64), in_=gain_rows[:])
+                    load_w(1)
+                    nc.sync.dma_start(out=gain[:], in_=out[0].partition_broadcast(P))
+                    load_w(2)
+                if u == X_UNITS - 1:
+                    w_inter(0)
+                if u % 2 == 1:
+                    step = u // 2
+                    if 1 <= step <= PASSES:
+                        a_quant(step - 1)
+                        x_quant(step - 1)
+                    if step >= PASSES + 2:
+                        x_quant(step - 2)
+                    if 2 <= step <= PASSES + 1:
+                        h_mm(step - 2)
+            h_mm(PASSES)
+            x_out(X_UNITS - 2)
+            x_out(X_UNITS - 1)
+            x_quant(2 * PASSES - 2)
+            h_mm(PASSES + 1)
+            h_mm(PASSES + 2)
+
             w_quant(0)
-            x_quant(2 * G - 1)
-            mm(0, 0, A)
-            h_mm(2 * G - 1)
-            h_inter(0, 0, HI_ENG[0])
+            y_mm(0, 0, group_a)
+            w_inter(1)
+            x_quant(2 * PASSES - 1)
+            h_mm(2 * PASSES - 1)
+            h_inter(0, 0)
             w_quant(1)
-            mm(0, 1, A)
-            w_shares(2)
+            y_mm(0, 1, group_a)
+            w_inter(2)
             for t in range(4):
                 h_out(1, t)
-            h_inter(0, 1, HI_ENG[1])
+            h_inter(0, 1)
             w_quant(2)
-            mm(0, 2, A)
-            mm(0, 0, B)
-            mm(0, 1, B)
-            b_inter(0, 0, B0_ENG[0])
-            b_inter(0, 1, B0_ENG[1])
-            w_shares(3)
+            y_mm(0, 2, group_a)
+            y_mm(0, 0, group_b)
+            y_mm(0, 1, group_b)
+            b_inter(0, 0, "vector")
+            b_inter(0, 1, "scalar")
+            w_inter(3)
             h_quant(0)
-            h_inter(1, 0, HI_ENG[2])
+            h_inter(1, 0)
             b_quant(0)
-            mm(0, G, A)
+            y_mm(0, UPDATE, group_a)
+            h_inter(1, 1)
 
-            a_t, b_t = A, B
-            for c in range(C - 1):
-                v = G * (c + 1)
-                w_shares(v)
+            for c in range(CHUNKS - 1):
+                v = PASSES * (c + 1)
+                w_inter(v)
                 w_quant(v - 1)
-                mm(c, 3, a_t)
-                mm(c, 2, b_t)
-                mm(c, 3, b_t)
-                if c == 0:
-                    h_inter(1, 1, HI_ENG[3])
-                w_shares(v + 1)
+                y_mm(c, 3, group_a)
+                y_mm(c, 2, group_b)
+                y_mm(c, 3, group_b)
+                w_inter(v + 1)
                 if c == 0:
                     h_quant(1)
-                mm(c, G, b_t)
+                y_mm(c, UPDATE, group_b)
+                group_b = group_b[::-1]
                 w_quant(v)
-                if REV:
-                    a_t, b_t = a_t[::-1], b_t[::-1]
-                y_out(c, a_t, 2)
-                mm(c + 1, 0, a_t)
+                y_out(c, group_a[::-1])
+                y_mm(c + 1, 0, group_a)
                 w_quant(v + 1)
-                mm(c + 1, 1, a_t)
-                w_shares(v + 2)
-                b_inter(c + 1, 0, "s")
-                b_inter(c + 1, 1, "s")
-                y_out(c, b_t, 2)
-                mm(c + 1, 0, b_t)
-                mm(c + 1, 1, b_t)
+                y_mm(c + 1, 1, group_a)
+                w_inter(v + 2)
+                b_inter(c + 1, 0, "scalar")
+                b_inter(c + 1, 1, "scalar")
+                y_out(c, group_b)
+                y_mm(c + 1, 0, group_b)
+                y_mm(c + 1, 1, group_b)
                 w_quant(v + 2)
-                w_shares(v + 3)
+                w_inter(v + 3)
                 b_quant(c + 1)
-                if c + 2 < C:
-                    mm(c + 1, 2, a_t)
-                    mm(c + 1, G, a_t)
-            w_quant(UNITS - 1)
-            for i in a_t + b_t:
-                for g in (2, G, 3):
-                    mm(C - 1, g, [i])
-                y_out(C - 1, [i], 1)
+                if c + 2 < CHUNKS:
+                    y_mm(c + 1, 2, group_a)
+                    y_mm(c + 1, UPDATE, group_a)
+
+            c = CHUNKS - 1
+            w_quant(W_UNITS - 1)
+            for i in group_a + group_b:
+                for g in (2, UPDATE, 3):
+                    y_mm(c, g, [i])
+                parts = 2 if i == group_b[-1] else 1
+                for e in range(parts):
+                    part = slice(CW // parts * e, CW // parts * (e + 1))
+                    y_scale(c, i, part)
+                    nc.sync.dma_start(
+                        out=out_view[:, i, CW * c + part.start : CW * c + part.stop], in_=res[c, i // 2][:, i % 2, part]
+                    )

@@ -41,14 +41,14 @@ def tile_dora_fp8_forward_d2_kernel(tc, x_bytes, x_scale, w_bytes, w_scale, a, l
         keep = ctx.enter_context(tc.tile_pool(name="keep", bufs=1))
         big = ctx.enter_context(tc.tile_pool(name="big", bufs=14))
         widened = ctx.enter_context(tc.tile_pool(name="widened", bufs=6))
-        stage = ctx.enter_context(tc.tile_pool(name="stage", bufs=14))
+        stage = ctx.enter_context(tc.tile_pool(name="stage", bufs=13))
         psum = ctx.enter_context(tc.psum_pool(name="psum", bufs=1))
 
         def kept(shape, dtype, name):
-            return keep.tile(shape, dtype, name=name, align_bytes=64)
+            return keep.tile(shape, dtype, name=name, align_bytes=256)
 
         def staged(shape, name):
-            return stage.tile(shape, BF16, name=name, tag="stage", align_bytes=64)
+            return stage.tile(shape, BF16, name=name, tag="stage", align_bytes=256)
 
         def bank(n, shape, dtype=F32):
             return psum.tile(shape, dtype, name=f"bank{n}", tag=f"bank{n}")
@@ -64,8 +64,8 @@ def tile_dora_fp8_forward_d2_kernel(tc, x_bytes, x_scale, w_bytes, w_scale, a, l
         inv_norm = kept([64, N // 64], F32, "inv_norm")
         gain_rows = kept([64, N // 64], F32, "gain_rows")
         gain = kept([P, N], F32, "gain")
-        xb = [big.tile([P, 4, K // 2], U8, name=f"xb{n}", tag="big", align_bytes=64) for n in range(4)]
-        araw = [big.tile([P, 4, R], BF16, name=f"araw{g}", tag="big", align_bytes=64) for g in range(PASSES)]
+        xb = [big.tile([P, 4, K // 2], U8, name=f"xb{n}", tag="big", align_bytes=256) for n in range(4)]
+        araw = [big.tile([P, 4, R], BF16, name=f"araw{g}", tag="big", align_bytes=256) for g in range(PASSES)]
         wb = [kept([P, 4, CW], U8, f"wb{v}") for v in range(W_UNITS)]
         braw = kept([P, 4, N], BF16, "braw")
         xq = kept([P, 2, PASSES, 512], U32, "xq")
@@ -115,7 +115,7 @@ def tile_dora_fp8_forward_d2_kernel(tc, x_bytes, x_scale, w_bytes, w_scale, a, l
 
         def x_widen(u):
             half, g, j = u // 8, u % 8 // 2, u % 2
-            xw[u] = widened.tile([P, 2, 512], BF16, name="xw", align_bytes=64)
+            xw[u] = widened.tile([P, 2, 512], BF16, name="xw", align_bytes=256)
             for i in range(2):
                 runs = xw[u][:, i, :].rearrange("p (h m e) -> p m h e", h=2, e=2)
                 for q in range(4):
@@ -228,8 +228,8 @@ def tile_dora_fp8_forward_d2_kernel(tc, x_bytes, x_scale, w_bytes, w_scale, a, l
                     nc.scalar.activation(out=dst, in_=src, func=COPY, scale=scale)
 
         def w_quant(v):
-            wq[v] = keep.tile([P, CW], U32, name=f"wq{v}", tag="wq", bufs=2 * PASSES, align_bytes=64)
-            wqs[v] = keep.tile([P, CW], U8, name=f"wqs{v}", tag="wqs", bufs=2 * PASSES, align_bytes=64)
+            wq[v] = keep.tile([P, CW], U32, name=f"wq{v}", tag="wq", bufs=2 * PASSES, align_bytes=256)
+            wqs[v] = keep.tile([P, CW], U8, name=f"wqs{v}", tag="wqs", bufs=2 * PASSES, align_bytes=256)
             quantise(wq[v][:], wqs[v][:], wg[v][:].rearrange("p n t -> p (n t)"))
 
         acc, done, res = {}, {}, {}
@@ -259,7 +259,7 @@ def tile_dora_fp8_forward_d2_kernel(tc, x_bytes, x_scale, w_bytes, w_scale, a, l
 
         def y_scale(c, i, part):
             if (c, i // 2) not in res:
-                res[c, i // 2] = big.tile([P, 2, CW], F32, name="res", tag="big", align_bytes=64)
+                res[c, i // 2] = big.tile([P, 2, CW], F32, name="res", tag="big", align_bytes=256)
             cols = slice(CW * c + part.start, CW * c + part.stop)
             nc.vector.tensor_tensor(out=res[c, i // 2][:, i % 2, part], in0=acc[c, i][:, part], in1=gain[:, cols], op=MULT)
 

@@ -13,6 +13,7 @@ U8 = mybir.dt.uint8
 E4M3 = mybir.dt.float8_e4m3fn
 MX = mybir.dt.float8_e4m3fn_x4
 MULT = mybir.AluOpType.mult
+ADD = mybir.AluOpType.add
 COPY = mybir.ActivationFunctionType.Copy
 
 P = 128
@@ -31,8 +32,8 @@ W_WIDEN_FROM = 9
 
 def vector_blocks(v):
     if v < PASSES:
-        return 4
-    return 3 if v < W_UNITS - 2 else 2
+        return 3 if v == 1 else 4
+    return 3 - (v - 2) // PASSES
 
 
 def tile_dora_fp8_forward_d2_kernel(tc, x_bytes, x_scale, w_bytes, w_scale, a, lam, b, mag, norm, out):
@@ -207,6 +208,15 @@ def tile_dora_fp8_forward_d2_kernel(tc, x_bytes, x_scale, w_bytes, w_scale, a, l
         def b_quant(c):
             quantise(bq[c][:], bqs[c][:], bg[c][:].rearrange("p n t -> p (n t)"))
 
+        def b_inter_late(c, e, tile):
+            bg[c, e] = tile
+            src = braw[:, :, CW * c + 256 * e : CW * c + 256 * (e + 1)].rearrange("p t n -> p n t")
+            nc.gpsimd.tensor_scalar(out=tile[:, 0:256, :], in0=src, scalar1=1.0, scalar2=0.0, op0=MULT, op1=ADD)
+
+        def b_quant_late(c, e):
+            cols = slice(256 * e, 256 * (e + 1))
+            quantise(bq[c][:, cols], bqs[c][:, cols], bg[c, e][:, 0:256, :].rearrange("p n t -> p (n t)"))
+
         def w_widen(v):
             ww[v] = staged([P, 4, CW], "ww")
             nc.scalar.copy(
@@ -379,19 +389,20 @@ def tile_dora_fp8_forward_d2_kernel(tc, x_bytes, x_scale, w_bytes, w_scale, a, l
                 y_mm(c, UPDATE, group_b)
                 group_b = group_b[::-1]
                 w_quant(v)
+                b_inter_late(c + 1, 0, wg[v])
                 y_out(c, group_a[::-1])
                 y_mm(c + 1, 0, group_a)
+                w_inter(v + 2)
                 w_quant(v + 1)
                 y_mm(c + 1, 1, group_a)
-                w_inter(v + 2)
-                b_inter(c + 1, 0, "scalar")
-                b_inter(c + 1, 1, "scalar")
+                b_inter_late(c + 1, 1, wg[v + 1])
                 y_out(c, group_b)
                 y_mm(c + 1, 0, group_b)
                 y_mm(c + 1, 1, group_b)
                 w_quant(v + 2)
                 w_inter(v + 3)
-                b_quant(c + 1)
+                b_quant_late(c + 1, 0)
+                b_quant_late(c + 1, 1)
                 if c + 2 < CHUNKS:
                     y_mm(c + 1, 2, group_a)
                     y_mm(c + 1, UPDATE, group_a)

@@ -33,7 +33,7 @@ W_WIDEN_FROM = 9
 def vector_blocks(v):
     if v < PASSES:
         return 3 if v == 1 else 4
-    return 3 - (v - 2) // PASSES
+    return 2 if v < W_UNITS - 2 else 1
 
 
 def tile_dora_fp8_forward_d2_kernel(tc, x_bytes, x_scale, w_bytes, w_scale, a, lam, b, mag, norm, out):
@@ -167,9 +167,9 @@ def tile_dora_fp8_forward_d2_kernel(tc, x_bytes, x_scale, w_bytes, w_scale, a, l
         def a_quant(g):
             quantise(aq[:, g, :], aqs[:, g, :], ag[g][:].rearrange("p t m j -> p (t m j)"))
 
-        def h_mm(d):
+        def h_mm(d, ts=range(4)):
             half, g = divmod(d, PASSES)
-            for t in range(4):
+            for t in ts:
                 if g == 0:
                     hbank[half, t] = bank(4 + t, [P, 512])
                 nc.tensor.matmul_mx(
@@ -199,21 +199,18 @@ def tile_dora_fp8_forward_d2_kernel(tc, x_bytes, x_scale, w_bytes, w_scale, a, l
 
         bg, ww, wg = {}, {}, {}
 
-        def b_inter(c, e, engine):
-            if c not in bg:
-                bg[c] = staged([P, CW, 4], "wgb")
-            n0 = 256 * e
-            copy_on(engine, *fours(bg[c][:, n0 : n0 + 256, :], braw[:, :, CW * c + n0 : CW * c + n0 + 256]))
+        def b_first(e, engine):
+            if 0 not in bg:
+                bg[0] = staged([P, CW, 4], "wgb")
+            n = slice(256 * e, 256 * (e + 1))
+            copy_on(engine, *fours(bg[0][:, n, :], braw[:, :, n]))
 
-        def b_quant(c):
-            quantise(bq[c][:], bqs[c][:], bg[c][:].rearrange("p n t -> p (n t)"))
-
-        def b_inter_late(c, e, tile):
+        def b_later(c, e, tile):
             bg[c, e] = tile
             src = braw[:, :, CW * c + 256 * e : CW * c + 256 * (e + 1)].rearrange("p t n -> p n t")
             nc.gpsimd.tensor_scalar(out=tile[:, 0:256, :], in0=src, scalar1=1.0, scalar2=0.0, op0=MULT, op1=ADD)
 
-        def b_quant_late(c, e):
+        def b_later_quant(c, e):
             cols = slice(256 * e, 256 * (e + 1))
             quantise(bq[c][:, cols], bqs[c][:, cols], bg[c, e][:, 0:256, :].rearrange("p n t -> p (n t)"))
 
@@ -344,11 +341,12 @@ def tile_dora_fp8_forward_d2_kernel(tc, x_bytes, x_scale, w_bytes, w_scale, a, l
                         x_quant(step - 2)
                     if 2 <= step <= PASSES + 1:
                         h_mm(step - 2)
-            h_mm(PASSES)
+                    if u > last_h:
+                        h_mm(PASSES, (u - last_h - 2, u - last_h - 1))
+            h_mm(PASSES + 1)
             x_out(X_UNITS - 2)
             x_out(X_UNITS - 1)
             x_quant(2 * PASSES - 2)
-            h_mm(PASSES + 1)
             h_mm(PASSES + 2)
 
             w_quant(0)
@@ -367,12 +365,12 @@ def tile_dora_fp8_forward_d2_kernel(tc, x_bytes, x_scale, w_bytes, w_scale, a, l
             y_mm(0, 2, group_a)
             y_mm(0, 0, group_b)
             y_mm(0, 1, group_b)
-            b_inter(0, 0, "vector")
-            b_inter(0, 1, "scalar")
+            b_first(0, "vector")
+            b_first(1, "scalar")
             w_inter(3)
             h_quant(0)
             h_inter(1, 0)
-            b_quant(0)
+            quantise(bq[0][:], bqs[0][:], bg[0][:].rearrange("p n t -> p (n t)"))
             y_mm(0, UPDATE, group_a)
             h_inter(1, 1)
 
@@ -389,20 +387,20 @@ def tile_dora_fp8_forward_d2_kernel(tc, x_bytes, x_scale, w_bytes, w_scale, a, l
                 y_mm(c, UPDATE, group_b)
                 group_b = group_b[::-1]
                 w_quant(v)
-                b_inter_late(c + 1, 0, wg[v])
+                b_later(c + 1, 0, wg[v])
                 y_out(c, group_a[::-1])
                 y_mm(c + 1, 0, group_a)
                 w_inter(v + 2)
                 w_quant(v + 1)
                 y_mm(c + 1, 1, group_a)
-                b_inter_late(c + 1, 1, wg[v + 1])
+                b_later(c + 1, 1, wg[v + 1])
                 y_out(c, group_b)
                 y_mm(c + 1, 0, group_b)
                 y_mm(c + 1, 1, group_b)
                 w_quant(v + 2)
                 w_inter(v + 3)
-                b_quant_late(c + 1, 0)
-                b_quant_late(c + 1, 1)
+                b_later_quant(c + 1, 0)
+                b_later_quant(c + 1, 1)
                 if c + 2 < CHUNKS:
                     y_mm(c + 1, 2, group_a)
                     y_mm(c + 1, UPDATE, group_a)

@@ -96,9 +96,10 @@ def tile_dora_fp8_forward_d2_kernel(tc, x_bytes, x_scale, w_bytes, w_scale, a, l
                 in_=x_view[:, 4 * half : 4 * half + 4, 512 * g : 512 * (g + passes)],
             )
 
-        def load_w(c):
-            for g in range(PASSES):
-                nc.sync.dma_start(out=wb[PASSES * c + g][:], in_=w_view[g][:, :, CW * c : CW * (c + 1)])
+        def load_w(units):
+            for v in units:
+                c, g = divmod(v, PASSES)
+                nc.sync.dma_start(out=wb[v][:], in_=w_view[g][:, :, CW * c : CW * (c + 1)])
 
         def copy_on(engine, dst, src):
             if engine == "vector":
@@ -298,11 +299,12 @@ def tile_dora_fp8_forward_d2_kernel(tc, x_bytes, x_scale, w_bytes, w_scale, a, l
             nc.sync.dma_start(out=araw[2][:], in_=a_view[2])
             nc.sync.dma_start(out=araw[3][:], in_=a_view[3])
             load_x(1, 0, 2)
+            load_w(range(2))
             load_x(1, 2, 2)
             ws_view = w_scale.rearrange("(g q) n -> q g n", q=4)
             for q in range(4):
                 nc.sync.dma_start(out=ws[32 * q : 32 * (q + 1), :, 0 : N // 128], in_=ws_view[q].partition_broadcast(32))
-            load_w(0)
+            load_w(range(2, PASSES))
             for t in range(4):
                 nc.sync.dma_start(out=braw[:, t, :], in_=b_view[t])
 
@@ -327,9 +329,9 @@ def tile_dora_fp8_forward_d2_kernel(tc, x_bytes, x_scale, w_bytes, w_scale, a, l
                     nc.vector.tensor_tensor(out=gain_rows[:], in0=mag_sb[:], in1=inv_norm[:], op=MULT)
                 if u == W_WIDEN_FROM:
                     nc.sync.dma_start(out=out[0].rearrange("(p j) -> p j", p=64), in_=gain_rows[:])
-                    load_w(1)
+                    load_w(range(PASSES, 2 * PASSES))
                     nc.sync.dma_start(out=gain[:], in_=out[0].partition_broadcast(P))
-                    load_w(2)
+                    load_w(range(2 * PASSES, W_UNITS))
                 if u == X_UNITS - 1:
                     w_inter(0)
                 if u % 2 == 1:

@@ -26,14 +26,11 @@ X_UNITS = 4 * PASSES
 W_UNITS = CHUNKS * PASSES
 
 X_ON_SCALAR = (1, 3)
-A_ON_SCALAR = range(4, 7)
-W_WIDEN_FROM = 9
+A_ON_SCALAR = range(3, 7)
+W_WIDEN_AT = (8, 10, 14)
 
 
-def vector_blocks(v):
-    if v < PASSES:
-        return 3 if v == 1 else 4
-    return 2 if v < W_UNITS - 2 else 1
+VECTOR_BLOCKS = (4, 4, 4, 4, 0, 2, 1, 2, 2, 2, 0, 0)
 
 
 def tile_dora_fp8_forward_d2_kernel(tc, x_bytes, x_scale, w_bytes, w_scale, a, lam, b, mag, norm, out):
@@ -221,16 +218,15 @@ def tile_dora_fp8_forward_d2_kernel(tc, x_bytes, x_scale, w_bytes, w_scale, a, l
                 out=ww[v][:].rearrange("p t n -> p (t n)"), in_=wb[v][:].rearrange("p t n -> p (t n)").bitcast(E4M3)
             )
 
-        def w_inter(v):
+        def w_inter(v, engine):
             c, g = divmod(v, PASSES)
-            if v + 1 < W_UNITS and v + 1 not in ww:
-                w_widen(v + 1)
-            wg[v] = staged([P, CW, 4], "wg")
-            for e in [*range(vector_blocks(v), 4), *range(vector_blocks(v))]:
+            if v not in wg:
+                wg[v] = staged([P, CW, 4], "wg")
+            for e in range(VECTOR_BLOCKS[v]) if engine == "vector" else range(VECTOR_BLOCKS[v], 4):
                 cols = slice(128 * e, 128 * (e + 1))
                 dst, src = fours(wg[v][:, cols, :], ww[v][:, :, cols])
                 scale = ws[:, g, 4 * c + e : 4 * c + e + 1]
-                if e < vector_blocks(v):
+                if engine == "vector":
                     nc.vector.tensor_scalar(out=dst, in0=src, scalar1=scale, scalar2=None, op0=MULT)
                 else:
                     nc.scalar.activation(out=dst, in_=src, func=COPY, scale=scale)
@@ -308,7 +304,6 @@ def tile_dora_fp8_forward_d2_kernel(tc, x_bytes, x_scale, w_bytes, w_scale, a, l
             for t in range(4):
                 nc.sync.dma_start(out=braw[:, t, :], in_=b_view[t])
 
-            last_h = 2 * (PASSES - 1) + 5
             for u in range(X_UNITS):
                 x_widen(u)
                 x_turn(u)
@@ -316,96 +311,114 @@ def tile_dora_fp8_forward_d2_kernel(tc, x_bytes, x_scale, w_bytes, w_scale, a, l
                     x_out(u - 2)
                 if 1 <= u <= 2 * PASSES:
                     a_inter(u - 1)
-                if u > last_h:
-                    h_out(0, u - last_h - 1)
-                if u in (W_WIDEN_FROM, W_WIDEN_FROM + 1):
-                    w_widen(u - W_WIDEN_FROM)
+                if u in (12, 13):
+                    h_out(0, 2 * (u - 12))
+                    h_out(0, 2 * (u - 12) + 1)
+                if u in W_WIDEN_AT:
+                    w_widen(W_WIDEN_AT.index(u))
                 if u == 0:
-                    lam_turned = bank(7, [P, P], BF16)
-                    nc.tensor.transpose(lam_turned[:], lam_rows[:], ident_bf[:])
                     nc.vector.reciprocal(out=inv_norm[:], in_=norm_sb[:])
                 if u == 1:
-                    nc.scalar.copy(out=lam_cols[:], in_=lam_turned[:, 0:4])
                     nc.vector.tensor_tensor(out=gain_rows[:], in0=mag_sb[:], in1=inv_norm[:], op=MULT)
-                if u == W_WIDEN_FROM:
+                if u == 3:
+                    lam_turned = bank(7, [P, P], BF16)
+                    nc.tensor.transpose(lam_turned[:], lam_rows[:], ident_bf[:])
+                if u == 4:
+                    nc.scalar.copy(out=lam_cols[:], in_=lam_turned[:, 0:4])
+                if u == 9:
                     nc.sync.dma_start(out=out[0].rearrange("(p j) -> p j", p=64), in_=gain_rows[:])
                     load_w(range(PASSES, 2 * PASSES))
                     nc.sync.dma_start(out=gain[:], in_=out[0].partition_broadcast(P))
                     load_w(range(2 * PASSES, W_UNITS))
-                if u == X_UNITS - 1:
-                    w_inter(0)
-                if u % 2 == 1:
-                    step = u // 2
-                    if 1 <= step <= PASSES:
-                        a_quant(step - 1)
-                        x_quant(step - 1)
-                    if step >= PASSES + 2:
-                        x_quant(step - 2)
-                    if 2 <= step <= PASSES + 1:
-                        h_mm(step - 2)
-                    if u > last_h:
-                        h_mm(PASSES, (u - last_h - 2, u - last_h - 1))
-            h_mm(PASSES + 1)
-            x_out(X_UNITS - 2)
-            x_out(X_UNITS - 1)
-            x_quant(2 * PASSES - 2)
-            h_mm(PASSES + 2)
-
+                if u in (3, 5, 7, 9):
+                    a_quant(u // 2 - 1)
+                    x_quant(u // 2 - 1)
+                if u in (5, 7, 9):
+                    h_mm(u // 2 - 2)
+                if u == 10:
+                    h_mm(3)
+                if u in (13, 15):
+                    x_quant(u // 2 - 2)
+                    h_mm(u // 2 - 2)
+                if u == 14:
+                    w_inter(0, "vector")
+            x_out(14)
+            x_out(15)
+            w_inter(1, "vector")
+            x_quant(6)
+            h_mm(6)
             w_quant(0)
-            y_mm(0, 0, group_a)
-            w_inter(1)
-            x_quant(2 * PASSES - 1)
-            h_mm(2 * PASSES - 1)
-            h_inter(0, 0)
+            w_widen(3)
+            x_quant(7)
+            h_mm(7)
+
             w_quant(1)
+            y_mm(0, 0, group_a)
             y_mm(0, 1, group_a)
-            w_inter(2)
+            w_inter(2, "vector")
+            w_widen(4)
             for t in range(4):
                 h_out(1, t)
+            h_inter(0, 0)
             h_inter(0, 1)
             w_quant(2)
             y_mm(0, 2, group_a)
             y_mm(0, 0, group_b)
-            y_mm(0, 1, group_b)
-            b_first(0, "vector")
+            w_inter(3, "vector")
             b_first(1, "scalar")
-            w_inter(3)
+            b_first(0, "vector")
+            w_quant(3)
+            y_mm(0, 3, group_a)
+            y_mm(0, 1, group_b)
             h_quant(0)
-            h_inter(1, 0)
+            w_widen(5)
             quantise(bq[0][:], bqs[0][:], bg[0][:].rearrange("p n t -> p (n t)"))
             y_mm(0, UPDATE, group_a)
+            y_mm(0, 2, group_b)
+            y_mm(0, 3, group_b)
+            w_inter(4, "scalar")
+            h_inter(1, 0)
             h_inter(1, 1)
+            w_inter(5, "scalar")
+            w_inter(5, "vector")
+            h_quant(1)
+            y_mm(0, UPDATE, group_b)
 
-            for c in range(CHUNKS - 1):
-                v = PASSES * (c + 1)
-                w_inter(v)
-                w_quant(v - 1)
-                y_mm(c, 3, group_a)
-                y_mm(c, 2, group_b)
-                y_mm(c, 3, group_b)
-                w_inter(v + 1)
-                if c == 0:
-                    h_quant(1)
-                y_mm(c, UPDATE, group_b)
+            for c in range(1, CHUNKS):
+                v = PASSES * c
                 group_b = group_b[::-1]
                 w_quant(v)
-                b_later(c + 1, 0, wg[v])
-                y_out(c, group_a[::-1])
-                y_mm(c + 1, 0, group_a)
-                w_inter(v + 2)
+                b_later(c, 0, wg[v])
+                y_out(c - 1, group_a[::-1])
+                y_mm(c, 0, group_a)
+                w_widen(v + 2)
+                w_inter(v + 2, "scalar")
                 w_quant(v + 1)
-                y_mm(c + 1, 1, group_a)
-                b_later(c + 1, 1, wg[v + 1])
-                y_out(c, group_b)
-                y_mm(c + 1, 0, group_b)
-                y_mm(c + 1, 1, group_b)
+                y_mm(c, 1, group_a)
+                b_later(c, 1, wg[v + 1])
+                w_inter(v + 2, "vector")
+                y_out(c - 1, group_b)
+                y_mm(c, 0, group_b)
+                y_mm(c, 1, group_b)
+                w_widen(v + 3)
+                w_inter(v + 3, "scalar")
                 w_quant(v + 2)
-                w_inter(v + 3)
-                b_later_quant(c + 1, 0)
-                b_later_quant(c + 1, 1)
-                if c + 2 < CHUNKS:
-                    y_mm(c + 1, 2, group_a)
-                    y_mm(c + 1, UPDATE, group_a)
+                w_inter(v + 3, "vector")
+                b_later_quant(c, 0)
+                b_later_quant(c, 1)
+                if c + 1 < CHUNKS:
+                    y_mm(c, 2, group_a)
+                    y_mm(c, UPDATE, group_a)
+                    w_widen(v + 4)
+                    w_inter(v + 4, "scalar")
+                    w_quant(v + 3)
+                    y_mm(c, 3, group_a)
+                    for g in (2, 3, UPDATE):
+                        y_mm(c, g, group_b)
+                    w_inter(v + 4, "vector")
+                    w_widen(v + 5)
+                    w_inter(v + 5, "scalar")
+                    w_inter(v + 5, "vector")
 
             c = CHUNKS - 1
             w_quant(W_UNITS - 1)

@@ -22,15 +22,17 @@ UPDATE = PASSES
 TILES = T // P
 CW = 512
 CHUNKS = N // CW
+WHOLE = slice(0, CW)
+LAST_PARTS = (slice(0, 256), slice(256, 384), slice(384, 512))
 X_UNITS = 4 * PASSES
 W_UNITS = CHUNKS * PASSES
 
 X_ON_SCALAR = (1, 3)
-A_ON_SCALAR = range(3, 7)
-W_WIDEN_AT = (8, 10, 14)
+A_ON_SCALAR = range(3, 6)
+W_WIDEN_AT = (7, 9, 11)
 
 
-VECTOR_BLOCKS = (4, 4, 4, 4, 0, 2, 1, 2, 2, 2, 0, 0)
+VECTOR_BLOCKS = (4, 4, 4, 4, 0, 1, 1, 2, 2, 2, 1, 1)
 
 
 def tile_dora_fp8_forward_d2_kernel(tc, x_bytes, x_scale, w_bytes, w_scale, a, lam, b, mag, norm, out):
@@ -238,38 +240,44 @@ def tile_dora_fp8_forward_d2_kernel(tc, x_bytes, x_scale, w_bytes, w_scale, a, l
 
         acc, done, res = {}, {}, {}
 
+        def y_pass(c, g, i, part, n):
+            key = (c, i, part.start)
+            if key not in acc:
+                acc[key] = bank(n, [P, part.stop - part.start])
+                done[key] = 0
+            if g == UPDATE:
+                lhs, lhs_s = hq[:, P * i : P * (i + 1)], hqs[:, P * i : P * (i + 1)]
+                rhs, rhs_s = bq[c], bqs[c]
+            else:
+                rows = slice(P * (i % 4), P * (i % 4 + 1))
+                lhs, lhs_s = xq[:, i // 4, g, rows], xqs[:, i // 4, g, rows]
+                rhs, rhs_s = wq[PASSES * c + g], wqs[PASSES * c + g]
+            nc.tensor.matmul_mx(
+                out=acc[key][:],
+                lhsT=lhs.bitcast(MX),
+                lhsT_scale=lhs_s,
+                rhs=rhs[:, part].bitcast(MX),
+                rhs_scale=rhs_s[:, part],
+                start=(done[key] == 0),
+                stop=(done[key] == PASSES),
+            )
+            done[key] = done[key] + 1
+
         def y_mm(c, g, tiles):
             for i in tiles:
-                if (c, i) not in acc:
-                    acc[c, i] = bank(i, [P, CW])
-                    done[c, i] = 0
-                if g == UPDATE:
-                    lhs, lhs_s = hq[:, P * i : P * (i + 1)], hqs[:, P * i : P * (i + 1)]
-                    rhs, rhs_s = bq[c][:], bqs[c][:]
-                else:
-                    rows = slice(P * (i % 4), P * (i % 4 + 1))
-                    lhs, lhs_s = xq[:, i // 4, g, rows], xqs[:, i // 4, g, rows]
-                    rhs, rhs_s = wq[PASSES * c + g][:], wqs[PASSES * c + g][:]
-                nc.tensor.matmul_mx(
-                    out=acc[c, i][:],
-                    lhsT=lhs.bitcast(MX),
-                    lhsT_scale=lhs_s,
-                    rhs=rhs.bitcast(MX),
-                    rhs_scale=rhs_s,
-                    start=(done[c, i] == 0),
-                    stop=(done[c, i] == PASSES),
-                )
-                done[c, i] = done[c, i] + 1
+                y_pass(c, g, i, LAST_PARTS[0] if (c, i) == (CHUNKS - 1, TILES - 1) else WHOLE, i)
 
         def y_scale(c, i, part):
             if (c, i // 2) not in res:
                 res[c, i // 2] = big.tile([P, 2, CW], F32, name="res", tag="big", align_bytes=256)
             cols = slice(CW * c + part.start, CW * c + part.stop)
-            nc.vector.tensor_tensor(out=res[c, i // 2][:, i % 2, part], in0=acc[c, i][:, part], in1=gain[:, cols], op=MULT)
+            nc.vector.tensor_tensor(
+                out=res[c, i // 2][:, i % 2, part], in0=acc[c, i, part.start][:], in1=gain[:, cols], op=MULT
+            )
 
         def y_out(c, tiles):
             for n, i in enumerate(tiles):
-                y_scale(c, i, slice(0, CW))
+                y_scale(c, i, WHOLE)
                 if n % 2 == 1:
                     i0 = i - i % 2
                     nc.sync.dma_start(out=out_view[:, i0 : i0 + 2, CW * c : CW * (c + 1)], in_=res[c, i // 2][:])
@@ -379,6 +387,7 @@ def tile_dora_fp8_forward_d2_kernel(tc, x_bytes, x_scale, w_bytes, w_scale, a, l
             w_inter(4, "scalar")
             h_inter(1, 0)
             h_inter(1, 1)
+            w_widen(6)
             w_inter(5, "scalar")
             w_inter(5, "vector")
             h_quant(1)
@@ -391,16 +400,17 @@ def tile_dora_fp8_forward_d2_kernel(tc, x_bytes, x_scale, w_bytes, w_scale, a, l
                 b_later(c, 0, wg[v])
                 y_out(c - 1, group_a[::-1])
                 y_mm(c, 0, group_a)
-                w_widen(v + 2)
+                w_widen(v + 3)
                 w_inter(v + 2, "scalar")
+                w_inter(v + 2, "vector")
                 w_quant(v + 1)
                 y_mm(c, 1, group_a)
                 b_later(c, 1, wg[v + 1])
-                w_inter(v + 2, "vector")
                 y_out(c - 1, group_b)
                 y_mm(c, 0, group_b)
                 y_mm(c, 1, group_b)
-                w_widen(v + 3)
+                if c + 1 < CHUNKS:
+                    w_widen(v + 4)
                 w_inter(v + 3, "scalar")
                 w_quant(v + 2)
                 w_inter(v + 3, "vector")
@@ -409,26 +419,26 @@ def tile_dora_fp8_forward_d2_kernel(tc, x_bytes, x_scale, w_bytes, w_scale, a, l
                 if c + 1 < CHUNKS:
                     y_mm(c, 2, group_a)
                     y_mm(c, UPDATE, group_a)
-                    w_widen(v + 4)
+                    w_widen(v + 5)
                     w_inter(v + 4, "scalar")
                     w_quant(v + 3)
                     y_mm(c, 3, group_a)
                     for g in (2, 3, UPDATE):
                         y_mm(c, g, group_b)
                     w_inter(v + 4, "vector")
-                    w_widen(v + 5)
+                    w_widen(v + 6)
                     w_inter(v + 5, "scalar")
                     w_inter(v + 5, "vector")
 
             c = CHUNKS - 1
             w_quant(W_UNITS - 1)
-            for i in group_a + group_b:
-                for g in (2, UPDATE, 3):
-                    y_mm(c, g, [i])
-                parts = 2 if i == group_b[-1] else 1
-                for e in range(parts):
-                    part = slice(CW // parts * e, CW // parts * (e + 1))
-                    y_scale(c, i, part)
-                    nc.sync.dma_start(
-                        out=out_view[:, i, CW * c + part.start : CW * c + part.stop], in_=res[c, i // 2][:, i % 2, part]
-                    )
+            pieces = [(i, WHOLE, i, (2, UPDATE, 3)) for i in range(TILES - 1)]
+            pieces.append((TILES - 1, LAST_PARTS[0], TILES - 1, (2, UPDATE, 3)))
+            pieces.extend((TILES - 1, part, n, range(PASSES + 1)) for n, part in enumerate(LAST_PARTS[1:]))
+            for i, part, n, passes in pieces:
+                for g in passes:
+                    y_pass(c, g, i, part, n)
+                y_scale(c, i, part)
+                nc.sync.dma_start(
+                    out=out_view[:, i, CW * c + part.start : CW * c + part.stop], in_=res[c, i // 2][:, i % 2, part]
+                )

@@ -27,12 +27,7 @@ LAST_PARTS = (slice(0, 256), slice(256, 384), slice(384, 512))
 X_UNITS = 4 * PASSES
 W_UNITS = CHUNKS * PASSES
 
-X_ON_SCALAR = (1, 3)
-A_ON_SCALAR = range(3, 6)
-W_WIDEN_AT = (7, 9, 11)
-
-
-VECTOR_BLOCKS = (4, 4, 4, 4, 0, 1, 1, 2, 2, 2, 1, 1)
+VECTOR_BLOCKS = (4, 4, 4, 4, 1, 0, 2, 3, 1, 3, 1, 1)
 
 
 def tile_dora_fp8_forward_d2_kernel(tc, x_bytes, x_scale, w_bytes, w_scale, a, lam, b, mag, norm, out):
@@ -112,10 +107,11 @@ def tile_dora_fp8_forward_d2_kernel(tc, x_bytes, x_scale, w_bytes, w_scale, a, l
         def quantise(codes, scales, values):
             nc.vector.quantize_mx(out=codes.bitcast(MX), scales=scales, in_=values)
 
-        xw, xbank, xg = {}, {}, {}
+        xw, in_order, xbank, xg = {}, {}, {}, {}
 
-        def x_widen(u):
+        def x_widen(u, engine="vector"):
             half, g, j = u // 8, u % 8 // 2, u % 2
+            in_order[u] = engine == "scalar"
             xw[u] = widened.tile([P, 2, 512], BF16, name="xw", align_bytes=256)
             for i in range(2):
                 runs = xw[u][:, i, :].rearrange("p (h m e) -> p m h e", h=2, e=2)
@@ -123,7 +119,7 @@ def tile_dora_fp8_forward_d2_kernel(tc, x_bytes, x_scale, w_bytes, w_scale, a, l
                     k = 512 * (g % 2) + 128 * q
                     codes = xb[2 * half + g // 2][:, 2 * j + i, k : k + 128].bitcast(E4M3)
                     scale = xs[:, 4 * half + 2 * j + i, 4 * g + q : 4 * g + q + 1]
-                    if u in X_ON_SCALAR:
+                    if engine == "scalar":
                         nc.scalar.activation(
                             out=xw[u][:, i, 128 * q : 128 * (q + 1)], in_=codes, func=COPY, scale=scale
                         )
@@ -137,16 +133,15 @@ def tile_dora_fp8_forward_d2_kernel(tc, x_bytes, x_scale, w_bytes, w_scale, a, l
             for i in range(2):
                 words = xw[u][:, i, :].bitcast(F32)
                 for h in range(2):
-                    src = words[:, h : 2 * P : 2] if u in X_ON_SCALAR else words[:, P * h : P * (h + 1)]
+                    src = words[:, h : 2 * P : 2] if in_order[u] else words[:, P * h : P * (h + 1)]
                     nc.tensor.transpose(xbank[u][:, i, h, :], src, ident[:])
 
-        def x_out(u):
-            if u % 2 == 0:
+        def x_out(u, engine="scalar"):
+            if u // 2 not in xg:
                 xg[u // 2] = staged([P, 2, 2, P, 4], "xg")
             words = xg[u // 2][:, u % 2].rearrange("p i r t -> p (i r t)").bitcast(F32)
-            nc.scalar.copy(
-                out=words.rearrange("p (i r h) -> p i r h", i=2, h=2),
-                in_=xbank[u][:].rearrange("p i h r -> p i r h"),
+            copy_on(
+                engine, words.rearrange("p (i r h) -> p i r h", i=2, h=2), xbank[u][:].rearrange("p i h r -> p i r h")
             )
 
         def x_quant(d):
@@ -155,14 +150,14 @@ def tile_dora_fp8_forward_d2_kernel(tc, x_bytes, x_scale, w_bytes, w_scale, a, l
 
         ag, hbank, hb, hg = {}, {}, {}, {}
 
-        def a_inter(n):
+        def a_inter(n, engine="vector"):
             g, e = n // 2, 1 - n % 2
             if g not in ag:
                 ag[g] = staged([P, 4, P, 4], "wga")
             for t in (2 * e, 2 * e + 1):
                 dst = ag[g][:, t].rearrange("p (q c i) j -> p q c j i", c=2, i=4)
                 src = araw[g][:].rearrange("p j (q t c i) -> p t q c j i", t=4, c=2, i=4)[:, t]
-                copy_on("scalar" if n in A_ON_SCALAR else "vector", dst, src)
+                copy_on(engine, dst, src)
 
         def a_quant(g):
             quantise(aq[:, g, :], aqs[:, g, :], ag[g][:].rearrange("p t m j -> p (t m j)"))
@@ -187,11 +182,11 @@ def tile_dora_fp8_forward_d2_kernel(tc, x_bytes, x_scale, w_bytes, w_scale, a, l
                 hb[half] = staged([P, 4, 512], "hb")
             nc.scalar.activation(out=hb[half][:, t, :], in_=hbank[half, t][:], func=COPY, scale=lam_cols[:, t : t + 1])
 
-        def h_inter(half, e):
+        def h_inter(half, e, engine="vector"):
             if half not in hg:
                 hg[half] = staged([P, 512, 4], "hg")
             n = slice(256 * e, 256 * (e + 1))
-            copy_on("vector", *fours(hg[half][:, n, :], hb[half][:, :, n]))
+            copy_on(engine, *fours(hg[half][:, n, :], hb[half][:, :, n]))
 
         def h_quant(half):
             cols = slice(512 * half, 512 * (half + 1))
@@ -220,11 +215,13 @@ def tile_dora_fp8_forward_d2_kernel(tc, x_bytes, x_scale, w_bytes, w_scale, a, l
                 out=ww[v][:].rearrange("p t n -> p (t n)"), in_=wb[v][:].rearrange("p t n -> p (t n)").bitcast(E4M3)
             )
 
-        def w_inter(v, engine):
+        def w_inter(v, engine, blocks=None):
             c, g = divmod(v, PASSES)
             if v not in wg:
                 wg[v] = staged([P, CW, 4], "wg")
-            for e in range(VECTOR_BLOCKS[v]) if engine == "vector" else range(VECTOR_BLOCKS[v], 4):
+            if blocks is None:
+                blocks = range(VECTOR_BLOCKS[v]) if engine == "vector" else range(VECTOR_BLOCKS[v], 4)
+            for e in blocks:
                 cols = slice(128 * e, 128 * (e + 1))
                 dst, src = fours(wg[v][:, cols, :], ww[v][:, :, cols])
                 scale = ws[:, g, 4 * c + e : 4 * c + e + 1]
@@ -300,8 +297,8 @@ def tile_dora_fp8_forward_d2_kernel(tc, x_bytes, x_scale, w_bytes, w_scale, a, l
             load_x(0, 1, 1)
             nc.sync.dma_start(out=araw[1][:], in_=a_view[1])
             load_x(0, 2, 2)
-            nc.sync.dma_start(out=araw[2][:], in_=a_view[2])
             nc.sync.dma_start(out=araw[3][:], in_=a_view[3])
+            nc.sync.dma_start(out=araw[2][:], in_=a_view[2])
             load_x(1, 0, 2)
             load_w(range(2))
             load_x(1, 2, 2)
@@ -312,74 +309,137 @@ def tile_dora_fp8_forward_d2_kernel(tc, x_bytes, x_scale, w_bytes, w_scale, a, l
             for t in range(4):
                 nc.sync.dma_start(out=braw[:, t, :], in_=b_view[t])
 
-            for u in range(X_UNITS):
-                x_widen(u)
-                x_turn(u)
-                if u >= 2:
-                    x_out(u - 2)
-                if 1 <= u <= 2 * PASSES:
-                    a_inter(u - 1)
-                if u in (12, 13):
-                    h_out(0, 2 * (u - 12))
-                    h_out(0, 2 * (u - 12) + 1)
-                if u in W_WIDEN_AT:
-                    w_widen(W_WIDEN_AT.index(u))
-                if u == 0:
-                    nc.vector.reciprocal(out=inv_norm[:], in_=norm_sb[:])
-                if u == 1:
-                    nc.vector.tensor_tensor(out=gain_rows[:], in0=mag_sb[:], in1=inv_norm[:], op=MULT)
-                if u == 3:
-                    lam_turned = bank(7, [P, P], BF16)
-                    nc.tensor.transpose(lam_turned[:], lam_rows[:], ident_bf[:])
-                if u == 4:
-                    nc.scalar.copy(out=lam_cols[:], in_=lam_turned[:, 0:4])
-                if u == 9:
-                    nc.sync.dma_start(out=out[0].rearrange("(p j) -> p j", p=64), in_=gain_rows[:])
-                    load_w(range(PASSES, 2 * PASSES))
-                    nc.sync.dma_start(out=gain[:], in_=out[0].partition_broadcast(P))
-                    load_w(range(2 * PASSES, W_UNITS))
-                if u in (3, 5, 7, 9):
-                    a_quant(u // 2 - 1)
-                    x_quant(u // 2 - 1)
-                if u in (5, 7, 9):
-                    h_mm(u // 2 - 2)
-                if u == 10:
-                    h_mm(3)
-                if u in (13, 15):
-                    x_quant(u // 2 - 2)
-                    h_mm(u // 2 - 2)
-                if u == 14:
-                    w_inter(0, "vector")
+            x_widen(0)
+            x_turn(0)
+            x_widen(1)
+            x_turn(1)
+            nc.vector.reciprocal(out=inv_norm[:], in_=norm_sb[:])
+            x_out(0)
+            x_out(1)
+            a_inter(0)
+            a_inter(1)
+            nc.vector.tensor_tensor(out=gain_rows[:], in0=mag_sb[:], in1=inv_norm[:], op=MULT)
+            x_widen(2)
+            x_widen(3, "scalar")
+            x_turn(2)
+            x_turn(3)
+            lam_turned = bank(7, [P, P], BF16)
+            nc.tensor.transpose(lam_turned[:], lam_rows[:], ident_bf[:])
+            x_quant(0)
+            a_inter(2, "scalar")
+            a_inter(3)
+            a_quant(0)
+            x_widen(4)
+            x_widen(5)
+            x_widen(6)
+            x_widen(7, "scalar")
+            x_out(2)
+            nc.scalar.copy(out=lam_cols[:], in_=lam_turned[:, 0:4])
+            x_turn(4)
+            x_out(3)
+            x_turn(5)
+            x_turn(6)
+            h_mm(0, (0, 1))
+            x_out(4)
+            x_turn(7)
+            h_mm(0, (2, 3))
+            x_out(5)
+            a_inter(6)
+            a_quant(1)
+            a_inter(7)
+            x_quant(1)
+            a_inter(4, "scalar")
+            x_out(6)
+            x_out(7)
+            a_inter(5, "scalar")
+            x_widen(8)
+            x_widen(9)
+            nc.sync.dma_start(out=out[0].rearrange("(p j) -> p j", p=64), in_=gain_rows[:])
+            load_w(range(PASSES, 2 * PASSES))
+            nc.sync.dma_start(out=gain[:], in_=out[0].partition_broadcast(P))
+            load_w(range(2 * PASSES, W_UNITS))
+            x_turn(8)
+            h_mm(1, (0, 1))
+            x_turn(9)
+            h_mm(1, (2, 3))
+            x_quant(2)
+            x_widen(10)
+            x_widen(11)
+            x_turn(10)
+            x_turn(11)
+            a_quant(2)
+            x_quant(3)
+            a_quant(3)
+            h_mm(2)
+            h_mm(3)
+            w_widen(0)
+            x_out(8)
+            x_out(9)
+            w_widen(1)
+            x_out(10)
+            x_widen(12)
+            x_out(11, "vector")
+            x_widen(13)
+            x_widen(14)
+            x_quant(4)
+            x_widen(15)
+            x_quant(5)
+            x_turn(12)
+            x_turn(13)
+            x_turn(14)
+            h_out(0, 0)
+            h_out(0, 1)
+            h_mm(4, (0, 1))
+            x_turn(15)
+            h_out(0, 2)
+            h_out(0, 3)
+            h_mm(4, (2, 3))
+            h_mm(5)
+            x_out(12)
+            x_out(13)
             x_out(14)
             x_out(15)
-            w_inter(1, "vector")
+            w_inter(0, "vector")
+            w_inter(1, "vector", [0])
+            w_inter(1, "vector", [1])
             x_quant(6)
             h_mm(6)
             w_quant(0)
-            w_widen(3)
             x_quant(7)
             h_mm(7)
-
-            w_quant(1)
             y_mm(0, 0, group_a)
+            w_widen(2)
+            w_widen(3)
+            w_inter(1, "vector", [2])
+            w_inter(1, "vector", [3])
+            w_inter(2, "vector", [0])
+            w_quant(1)
             y_mm(0, 1, group_a)
-            w_inter(2, "vector")
-            w_widen(4)
-            for t in range(4):
-                h_out(1, t)
-            h_inter(0, 0)
-            h_inter(0, 1)
+            w_inter(2, "vector", [1])
+            w_inter(2, "vector", [2])
+            w_inter(2, "vector", [3])
+            h_inter(0, 0, "scalar")
+            h_out(1, 0)
+            h_out(1, 1)
+            h_out(1, 2)
+            h_out(1, 3)
+            w_inter(3, "vector", [0])
             w_quant(2)
             y_mm(0, 2, group_a)
             y_mm(0, 0, group_b)
-            w_inter(3, "vector")
-            b_first(1, "scalar")
-            b_first(0, "vector")
+            w_inter(3, "vector", [1])
+            w_inter(3, "vector", [2])
+            w_inter(3, "vector", [3])
+            h_inter(0, 1)
+            w_widen(4)
             w_quant(3)
             y_mm(0, 3, group_a)
             y_mm(0, 1, group_b)
+            b_first(0, "vector")
+            b_first(1, "vector")
             h_quant(0)
             w_widen(5)
+            w_inter(4, "vector")
             quantise(bq[0][:], bqs[0][:], bg[0][:].rearrange("p n t -> p (n t)"))
             y_mm(0, UPDATE, group_a)
             y_mm(0, 2, group_b)
@@ -387,48 +447,61 @@ def tile_dora_fp8_forward_d2_kernel(tc, x_bytes, x_scale, w_bytes, w_scale, a, l
             w_inter(4, "scalar")
             h_inter(1, 0)
             h_inter(1, 1)
-            w_widen(6)
             w_inter(5, "scalar")
             w_inter(5, "vector")
+            w_widen(6)
             h_quant(1)
             y_mm(0, UPDATE, group_b)
-
-            for c in range(1, CHUNKS):
-                v = PASSES * c
-                group_b = group_b[::-1]
-                w_quant(v)
-                b_later(c, 0, wg[v])
-                y_out(c - 1, group_a[::-1])
-                y_mm(c, 0, group_a)
-                w_widen(v + 3)
-                w_inter(v + 2, "scalar")
-                w_inter(v + 2, "vector")
-                w_quant(v + 1)
-                y_mm(c, 1, group_a)
-                b_later(c, 1, wg[v + 1])
-                y_out(c - 1, group_b)
-                y_mm(c, 0, group_b)
-                y_mm(c, 1, group_b)
-                if c + 1 < CHUNKS:
-                    w_widen(v + 4)
-                w_inter(v + 3, "scalar")
-                w_quant(v + 2)
-                w_inter(v + 3, "vector")
-                b_later_quant(c, 0)
-                b_later_quant(c, 1)
-                if c + 1 < CHUNKS:
-                    y_mm(c, 2, group_a)
-                    y_mm(c, UPDATE, group_a)
-                    w_widen(v + 5)
-                    w_inter(v + 4, "scalar")
-                    w_quant(v + 3)
-                    y_mm(c, 3, group_a)
-                    for g in (2, 3, UPDATE):
-                        y_mm(c, g, group_b)
-                    w_inter(v + 4, "vector")
-                    w_widen(v + 6)
-                    w_inter(v + 5, "scalar")
-                    w_inter(v + 5, "vector")
+            w_quant(4)
+            b_later(1, 0, wg[4])
+            y_out(0, group_a[::-1])
+            y_mm(1, 0, group_a)
+            w_widen(7)
+            w_inter(6, "scalar")
+            w_inter(6, "vector")
+            w_quant(5)
+            y_mm(1, 1, group_a)
+            b_later(1, 1, wg[5])
+            y_out(0, group_b[::-1])
+            y_mm(1, 0, group_b[::-1])
+            y_mm(1, 1, group_b[::-1])
+            w_widen(8)
+            w_inter(7, "scalar")
+            w_quant(6)
+            w_inter(7, "vector")
+            b_later_quant(1, 0)
+            b_later_quant(1, 1)
+            y_mm(1, 2, group_a)
+            y_mm(1, UPDATE, group_a)
+            w_widen(9)
+            w_inter(8, "scalar")
+            w_quant(7)
+            y_mm(1, 3, group_a)
+            y_mm(1, 2, group_b[::-1])
+            y_mm(1, 3, group_b[::-1])
+            y_mm(1, UPDATE, group_b[::-1])
+            w_inter(8, "vector")
+            w_widen(10)
+            w_inter(9, "scalar")
+            w_inter(9, "vector")
+            w_quant(8)
+            b_later(2, 0, wg[8])
+            y_out(1, group_a[::-1])
+            y_mm(2, 0, group_a)
+            w_widen(11)
+            w_inter(10, "scalar")
+            w_inter(10, "vector")
+            w_quant(9)
+            y_mm(2, 1, group_a)
+            b_later(2, 1, wg[9])
+            y_out(1, group_b)
+            y_mm(2, 0, group_b)
+            y_mm(2, 1, group_b)
+            w_inter(11, "scalar")
+            w_inter(11, "vector")
+            w_quant(10)
+            b_later_quant(2, 0)
+            b_later_quant(2, 1)
 
             c = CHUNKS - 1
             w_quant(W_UNITS - 1)

@@ -27,7 +27,7 @@ LAST_PARTS = (slice(0, 256), slice(256, 384), slice(384, 512))
 X_UNITS = 4 * PASSES
 W_UNITS = CHUNKS * PASSES
 
-VECTOR_BLOCKS = (4, 4, 4, 4, 1, 0, 2, 3, 1, 3, 1, 1)
+VECTOR_BLOCKS = (4, 4, 4, 2, 2, 1, 1, 2, 2, 2, 1, 1)
 
 
 def tile_dora_fp8_forward_d2_kernel(tc, x_bytes, x_scale, w_bytes, w_scale, a, lam, b, mag, norm, out):
@@ -81,7 +81,6 @@ def tile_dora_fp8_forward_d2_kernel(tc, x_bytes, x_scale, w_bytes, w_scale, a, l
 
         nc.gpsimd.memset(lam_rows[:], 0.0)
         make_identity(nc, ident[:])
-        make_identity(nc, ident_bf[:])
 
         def load_x(half, g, passes):
             k = 512 * (g % 2)
@@ -129,7 +128,7 @@ def tile_dora_fp8_forward_d2_kernel(tc, x_bytes, x_scale, w_bytes, w_scale, a, l
                         )
 
         def x_turn(u):
-            xbank[u] = bank(u % 4, [P, 2, 2, P])
+            xbank[u] = bank(u % 8, [P, 2, 2, P])
             for i in range(2):
                 words = xw[u][:, i, :].bitcast(F32)
                 for h in range(2):
@@ -166,7 +165,7 @@ def tile_dora_fp8_forward_d2_kernel(tc, x_bytes, x_scale, w_bytes, w_scale, a, l
             half, g = divmod(d, PASSES)
             for t in ts:
                 if g == 0:
-                    hbank[half, t] = bank(4 + t, [P, 512])
+                    hbank[half, t] = bank(4 * half + t, [P, 512])
                 nc.tensor.matmul_mx(
                     out=hbank[half, t][:],
                     lhsT=aq[:, g, P * t : P * (t + 1)].bitcast(MX),
@@ -285,168 +284,163 @@ def tile_dora_fp8_forward_d2_kernel(tc, x_bytes, x_scale, w_bytes, w_scale, a, l
             engines={mybir.EngineType.PE, mybir.EngineType.DVE, mybir.EngineType.Activation, mybir.EngineType.SP}
         ):
             nc.scalar.dma_start(out=xs[:], in_=x_scale.rearrange("(p i) k -> p i k", i=TILES))
-            for j in range(2):
-                nc.sync.dma_start(out=xb[0][:, 2 * j : 2 * j + 2, 0:512], in_=x_view[:, 2 * j : 2 * j + 2, 0:512])
-            nc.sync.dma_start(out=araw[0][:], in_=a_view[0])
+            nc.sync.dma_start(out=xb[0][:, 0:2, 0:512], in_=x_view[:, 0:2, 0:512])
+            nc.sync.dma_start(out=xb[0][:, 2:4, 0:512], in_=x_view[:, 2:4, 0:512])
+            load_x(0, 1, 1)
             nc.scalar.dma_start(out=norm_sb[:], in_=norm.rearrange("(p j) -> p j", p=64))
             nc.scalar.dma_start(out=mag_sb[:], in_=mag.rearrange("(p j) -> p j", p=64))
             nc.scalar.dma_start(
                 out=lam_rows[0:4, :].rearrange("t (q i) -> t q i", i=8),
                 in_=lam.rearrange("(q t i) -> t q i", t=4, i=8),
             )
-            load_x(0, 1, 1)
-            nc.sync.dma_start(out=araw[1][:], in_=a_view[1])
+            nc.scalar.activation(out=ident_bf[:], in_=ident[:], func=COPY)
             load_x(0, 2, 2)
-            nc.sync.dma_start(out=araw[3][:], in_=a_view[3])
-            nc.sync.dma_start(out=araw[2][:], in_=a_view[2])
             load_x(1, 0, 2)
-            load_w(range(2))
             load_x(1, 2, 2)
+            nc.sync.dma_start(out=araw[0][:], in_=a_view[0])
+            nc.sync.dma_start(out=araw[1][:], in_=a_view[1])
+            nc.sync.dma_start(out=araw[2][:], in_=a_view[2])
+            nc.sync.dma_start(out=araw[3][:], in_=a_view[3])
+            load_w([0])
+            load_w([1])
             ws_view = w_scale.rearrange("(g q) n -> q g n", q=4)
             for q in range(4):
                 nc.sync.dma_start(out=ws[32 * q : 32 * (q + 1), :, 0 : N // 128], in_=ws_view[q].partition_broadcast(32))
-            load_w(range(2, PASSES))
+            load_w([2])
             for t in range(4):
                 nc.sync.dma_start(out=braw[:, t, :], in_=b_view[t])
+            load_w([3])
 
             x_widen(0)
             x_turn(0)
-            x_widen(1)
-            x_turn(1)
-            nc.vector.reciprocal(out=inv_norm[:], in_=norm_sb[:])
-            x_out(0)
-            x_out(1)
-            a_inter(0)
-            a_inter(1)
-            nc.vector.tensor_tensor(out=gain_rows[:], in0=mag_sb[:], in1=inv_norm[:], op=MULT)
+            x_widen(1, "scalar")
             x_widen(2)
-            x_widen(3, "scalar")
+            x_turn(1)
             x_turn(2)
+            x_out(0)
+            x_widen(3)
             x_turn(3)
+            nc.vector.reciprocal(out=inv_norm[:], in_=norm_sb[:])
+            x_out(1)
+            x_widen(4)
+            x_turn(4)
+            nc.vector.tensor_tensor(out=gain_rows[:], in0=mag_sb[:], in1=inv_norm[:], op=MULT)
+            x_widen(7, "scalar")
             lam_turned = bank(7, [P, P], BF16)
             nc.tensor.transpose(lam_turned[:], lam_rows[:], ident_bf[:])
-            x_quant(0)
-            a_inter(2, "scalar")
-            a_inter(3)
-            a_quant(0)
-            x_widen(4)
             x_widen(5)
+            x_turn(5)
             x_widen(6)
-            x_widen(7, "scalar")
+            x_turn(6)
             x_out(2)
             nc.scalar.copy(out=lam_cols[:], in_=lam_turned[:, 0:4])
-            x_turn(4)
-            x_out(3)
-            x_turn(5)
-            x_turn(6)
-            h_mm(0, (0, 1))
-            x_out(4)
-            x_turn(7)
-            h_mm(0, (2, 3))
-            x_out(5)
-            a_inter(6)
-            a_quant(1)
-            a_inter(7)
-            x_quant(1)
-            a_inter(4, "scalar")
-            x_out(6)
-            x_out(7)
-            a_inter(5, "scalar")
+            x_widen(10, "scalar")
             x_widen(8)
+            x_turn(7)
+            x_out(3)
             x_widen(9)
-            nc.sync.dma_start(out=out[0].rearrange("(p j) -> p j", p=64), in_=gain_rows[:])
-            load_w(range(PASSES, 2 * PASSES))
-            nc.sync.dma_start(out=gain[:], in_=out[0].partition_broadcast(P))
-            load_w(range(2 * PASSES, W_UNITS))
             x_turn(8)
-            h_mm(1, (0, 1))
             x_turn(9)
-            h_mm(1, (2, 3))
-            x_quant(2)
-            x_widen(10)
+            x_out(4)
+            x_out(5)
             x_widen(11)
             x_turn(10)
             x_turn(11)
-            a_quant(2)
-            x_quant(3)
-            a_quant(3)
-            h_mm(2)
-            h_mm(3)
-            w_widen(0)
-            x_out(8)
-            x_out(9)
-            w_widen(1)
-            x_out(10)
+            x_out(6)
             x_widen(12)
-            x_out(11, "vector")
             x_widen(13)
-            x_widen(14)
-            x_quant(4)
-            x_widen(15)
-            x_quant(5)
+            a_inter(1, "scalar")
+            a_inter(0)
+            x_quant(0)
+            x_out(7)
             x_turn(12)
             x_turn(13)
+            x_out(8)
+            x_out(9)
+            x_widen(14)
+            x_widen(15)
             x_turn(14)
-            h_out(0, 0)
-            h_out(0, 1)
-            h_mm(4, (0, 1))
             x_turn(15)
-            h_out(0, 2)
-            h_out(0, 3)
-            h_mm(4, (2, 3))
-            h_mm(5)
+            x_out(10)
+            x_out(11)
+            a_quant(0)
+            h_mm(0)
             x_out(12)
             x_out(13)
             x_out(14)
             x_out(15)
+            nc.sync.dma_start(out=out[0].rearrange("(p j) -> p j", p=64), in_=gain_rows[:])
+            load_w(range(PASSES, 2 * PASSES))
+            nc.sync.dma_start(out=gain[:], in_=out[0].partition_broadcast(P))
+            load_w(range(2 * PASSES, W_UNITS))
+            a_inter(2)
+            a_inter(3)
+            x_quant(1)
+            a_quant(1)
+            h_mm(1)
+            a_inter(6, "scalar")
+            a_inter(7, "scalar")
+            a_inter(4)
+            x_quant(4)
+            a_inter(5)
+            h_mm(4)
+            x_quant(5)
+            h_mm(5)
+            x_quant(2)
+            a_quant(2)
+            h_mm(2)
+            x_quant(3)
+            a_quant(3)
+            h_mm(3)
+            w_widen(0)
+            w_widen(1)
+            w_widen(2)
+            x_quant(6)
+            x_quant(7)
+            h_mm(6)
+            h_mm(7)
             w_inter(0, "vector")
+            h_out(0, 0)
+            h_out(0, 1)
+            h_out(0, 2)
+            h_out(0, 3)
             w_inter(1, "vector", [0])
             w_inter(1, "vector", [1])
-            x_quant(6)
-            h_mm(6)
             w_quant(0)
-            x_quant(7)
-            h_mm(7)
             y_mm(0, 0, group_a)
-            w_widen(2)
-            w_widen(3)
             w_inter(1, "vector", [2])
             w_inter(1, "vector", [3])
-            w_inter(2, "vector", [0])
-            w_quant(1)
-            y_mm(0, 1, group_a)
-            w_inter(2, "vector", [1])
-            w_inter(2, "vector", [2])
-            w_inter(2, "vector", [3])
-            h_inter(0, 0, "scalar")
             h_out(1, 0)
             h_out(1, 1)
             h_out(1, 2)
             h_out(1, 3)
-            w_inter(3, "vector", [0])
+            b_first(0, "vector")
+            w_quant(1)
+            y_mm(0, 1, group_a)
+            w_inter(2, "vector")
+            b_first(1, "vector")
+            y_mm(0, 0, group_b)
+            y_mm(0, 1, group_b)
+            w_widen(3)
             w_quant(2)
             y_mm(0, 2, group_a)
-            y_mm(0, 0, group_b)
-            w_inter(3, "vector", [1])
-            w_inter(3, "vector", [2])
-            w_inter(3, "vector", [3])
+            y_mm(0, 2, group_b)
+            h_inter(0, 0)
             h_inter(0, 1)
             w_widen(4)
+            w_inter(3, "scalar")
+            w_inter(3, "vector")
+            quantise(bq[0][:], bqs[0][:], bg[0][:].rearrange("p n t -> p (n t)"))
+            h_quant(0)
+            y_mm(0, UPDATE, group_a)
+            h_inter(1, 0)
             w_quant(3)
             y_mm(0, 3, group_a)
-            y_mm(0, 1, group_b)
-            b_first(0, "vector")
-            b_first(1, "vector")
-            h_quant(0)
-            w_widen(5)
-            w_inter(4, "vector")
-            quantise(bq[0][:], bqs[0][:], bg[0][:].rearrange("p n t -> p (n t)"))
-            y_mm(0, UPDATE, group_a)
-            y_mm(0, 2, group_b)
             y_mm(0, 3, group_b)
+            w_widen(5)
             w_inter(4, "scalar")
-            h_inter(1, 0)
             h_inter(1, 1)
+            w_inter(4, "vector")
             w_inter(5, "scalar")
             w_inter(5, "vector")
             w_widen(6)
@@ -455,20 +449,20 @@ def tile_dora_fp8_forward_d2_kernel(tc, x_bytes, x_scale, w_bytes, w_scale, a, l
             w_quant(4)
             b_later(1, 0, wg[4])
             y_out(0, group_a[::-1])
-            y_mm(1, 0, group_a)
+            y_mm(1, 0, group_a[::-1])
             w_widen(7)
             w_inter(6, "scalar")
-            w_inter(6, "vector")
             w_quant(5)
             y_mm(1, 1, group_a)
             b_later(1, 1, wg[5])
             y_out(0, group_b[::-1])
+            w_inter(6, "vector")
             y_mm(1, 0, group_b[::-1])
             y_mm(1, 1, group_b[::-1])
             w_widen(8)
             w_inter(7, "scalar")
-            w_quant(6)
             w_inter(7, "vector")
+            w_quant(6)
             b_later_quant(1, 0)
             b_later_quant(1, 1)
             y_mm(1, 2, group_a)

@@ -27,7 +27,13 @@ LAST_PARTS = (slice(0, 256), slice(256, 384), slice(384, 512))
 X_UNITS = 4 * PASSES
 W_UNITS = CHUNKS * PASSES
 
-VECTOR_BLOCKS = (4, 4, 4, 2, 2, 1, 1, 2, 2, 2, 1, 1)
+
+def vector_blocks(v):
+    if v <= 2:
+        return 4
+    if v <= 4:
+        return 2
+    return 3 if 7 <= v <= 9 else 0
 
 
 def tile_dora_fp8_forward_d2_kernel(tc, x_bytes, x_scale, w_bytes, w_scale, a, lam, b, mag, norm, out):
@@ -82,12 +88,10 @@ def tile_dora_fp8_forward_d2_kernel(tc, x_bytes, x_scale, w_bytes, w_scale, a, l
         nc.gpsimd.memset(lam_rows[:], 0.0)
         make_identity(nc, ident[:])
 
-        def load_x(half, g, passes):
-            k = 512 * (g % 2)
-            nc.sync.dma_start(
-                out=xb[2 * half + g // 2][:, :, k : k + 512 * passes],
-                in_=x_view[:, 4 * half : 4 * half + 4, 512 * g : 512 * (g + passes)],
-            )
+        def load_x(n, tiles):
+            half, k = n // 2, K // 2 * (n % 2)
+            rows = slice(4 * half + tiles.start, 4 * half + tiles.stop)
+            nc.sync.dma_start(out=xb[n][:, tiles, :], in_=x_view[:, rows, k : k + K // 2])
 
         def load_w(units):
             for v in units:
@@ -135,12 +139,13 @@ def tile_dora_fp8_forward_d2_kernel(tc, x_bytes, x_scale, w_bytes, w_scale, a, l
                     src = words[:, h : 2 * P : 2] if in_order[u] else words[:, P * h : P * (h + 1)]
                     nc.tensor.transpose(xbank[u][:, i, h, :], src, ident[:])
 
-        def x_out(u, engine="scalar"):
+        def x_out(u):
             if u // 2 not in xg:
                 xg[u // 2] = staged([P, 2, 2, P, 4], "xg")
             words = xg[u // 2][:, u % 2].rearrange("p i r t -> p (i r t)").bitcast(F32)
-            copy_on(
-                engine, words.rearrange("p (i r h) -> p i r h", i=2, h=2), xbank[u][:].rearrange("p i h r -> p i r h")
+            nc.scalar.copy(
+                out=words.rearrange("p (i r h) -> p i r h", i=2, h=2),
+                in_=xbank[u][:].rearrange("p i h r -> p i r h"),
             )
 
         def x_quant(d):
@@ -181,11 +186,11 @@ def tile_dora_fp8_forward_d2_kernel(tc, x_bytes, x_scale, w_bytes, w_scale, a, l
                 hb[half] = staged([P, 4, 512], "hb")
             nc.scalar.activation(out=hb[half][:, t, :], in_=hbank[half, t][:], func=COPY, scale=lam_cols[:, t : t + 1])
 
-        def h_inter(half, e, engine="vector"):
+        def h_inter(half, e):
             if half not in hg:
                 hg[half] = staged([P, 512, 4], "hg")
             n = slice(256 * e, 256 * (e + 1))
-            copy_on(engine, *fours(hg[half][:, n, :], hb[half][:, :, n]))
+            copy_on("vector", *fours(hg[half][:, n, :], hb[half][:, :, n]))
 
         def h_quant(half):
             cols = slice(512 * half, 512 * (half + 1))
@@ -193,11 +198,11 @@ def tile_dora_fp8_forward_d2_kernel(tc, x_bytes, x_scale, w_bytes, w_scale, a, l
 
         bg, ww, wg = {}, {}, {}
 
-        def b_first(e, engine):
+        def b_first(e):
             if 0 not in bg:
                 bg[0] = staged([P, CW, 4], "wgb")
             n = slice(256 * e, 256 * (e + 1))
-            copy_on(engine, *fours(bg[0][:, n, :], braw[:, :, n]))
+            copy_on("vector", *fours(bg[0][:, n, :], braw[:, :, n]))
 
         def b_later(c, e, tile):
             bg[c, e] = tile
@@ -219,7 +224,7 @@ def tile_dora_fp8_forward_d2_kernel(tc, x_bytes, x_scale, w_bytes, w_scale, a, l
             if v not in wg:
                 wg[v] = staged([P, CW, 4], "wg")
             if blocks is None:
-                blocks = range(VECTOR_BLOCKS[v]) if engine == "vector" else range(VECTOR_BLOCKS[v], 4)
+                blocks = range(vector_blocks(v)) if engine == "vector" else range(vector_blocks(v), 4)
             for e in blocks:
                 cols = slice(128 * e, 128 * (e + 1))
                 dst, src = fours(wg[v][:, cols, :], ww[v][:, :, cols])
@@ -284,25 +289,23 @@ def tile_dora_fp8_forward_d2_kernel(tc, x_bytes, x_scale, w_bytes, w_scale, a, l
             engines={mybir.EngineType.PE, mybir.EngineType.DVE, mybir.EngineType.Activation, mybir.EngineType.SP}
         ):
             nc.scalar.dma_start(out=xs[:], in_=x_scale.rearrange("(p i) k -> p i k", i=TILES))
-            nc.sync.dma_start(out=xb[0][:, 0:2, 0:512], in_=x_view[:, 0:2, 0:512])
-            nc.sync.dma_start(out=xb[0][:, 2:4, 0:512], in_=x_view[:, 2:4, 0:512])
-            load_x(0, 1, 1)
-            nc.scalar.dma_start(out=norm_sb[:], in_=norm.rearrange("(p j) -> p j", p=64))
-            nc.scalar.dma_start(out=mag_sb[:], in_=mag.rearrange("(p j) -> p j", p=64))
+            load_x(0, slice(0, 2))
+            load_x(0, slice(2, 4))
             nc.scalar.dma_start(
                 out=lam_rows[0:4, :].rearrange("t (q i) -> t q i", i=8),
                 in_=lam.rearrange("(q t i) -> t q i", t=4, i=8),
             )
             nc.scalar.activation(out=ident_bf[:], in_=ident[:], func=COPY)
-            load_x(0, 2, 2)
-            load_x(1, 0, 2)
-            load_x(1, 2, 2)
+            load_x(1, slice(0, 2))
+            load_x(1, slice(2, 4))
+            load_x(2, slice(0, 4))
+            load_x(3, slice(0, 4))
             nc.sync.dma_start(out=araw[0][:], in_=a_view[0])
-            nc.sync.dma_start(out=araw[1][:], in_=a_view[1])
-            nc.sync.dma_start(out=araw[2][:], in_=a_view[2])
-            nc.sync.dma_start(out=araw[3][:], in_=a_view[3])
-            load_w([0])
-            load_w([1])
+            nc.sync.dma_start(out=norm_sb[:], in_=norm.rearrange("(p j) -> p j", p=64))
+            nc.sync.dma_start(out=mag_sb[:], in_=mag.rearrange("(p j) -> p j", p=64))
+            for g in range(1, PASSES):
+                nc.sync.dma_start(out=araw[g][:], in_=a_view[g])
+            load_w(range(2))
             ws_view = w_scale.rearrange("(g q) n -> q g n", q=4)
             for q in range(4):
                 nc.sync.dma_start(out=ws[32 * q : 32 * (q + 1), :, 0 : N // 128], in_=ws_view[q].partition_broadcast(32))
@@ -312,126 +315,113 @@ def tile_dora_fp8_forward_d2_kernel(tc, x_bytes, x_scale, w_bytes, w_scale, a, l
             load_w([3])
 
             x_widen(0)
+            x_widen(2, "scalar")
             x_turn(0)
-            x_widen(1, "scalar")
-            x_widen(2)
-            x_turn(1)
+            x_widen(1)
             x_turn(2)
-            x_out(0)
+            x_turn(1)
             x_widen(3)
             x_turn(3)
-            nc.vector.reciprocal(out=inv_norm[:], in_=norm_sb[:])
-            x_out(1)
+            x_out(0)
             x_widen(4)
-            x_turn(4)
-            nc.vector.tensor_tensor(out=gain_rows[:], in0=mag_sb[:], in1=inv_norm[:], op=MULT)
-            x_widen(7, "scalar")
+            x_widen(6, "scalar")
             lam_turned = bank(7, [P, P], BF16)
             nc.tensor.transpose(lam_turned[:], lam_rows[:], ident_bf[:])
-            x_widen(5)
-            x_turn(5)
-            x_widen(6)
-            x_turn(6)
+            x_turn(4)
             x_out(2)
+            x_out(1)
             nc.scalar.copy(out=lam_cols[:], in_=lam_turned[:, 0:4])
-            x_widen(10, "scalar")
-            x_widen(8)
+            x_widen(5)
+            x_turn(6)
+            x_widen(7)
+            x_turn(5)
             x_turn(7)
-            x_out(3)
-            x_widen(9)
-            x_turn(8)
-            x_turn(9)
-            x_out(4)
-            x_out(5)
-            x_widen(11)
-            x_turn(10)
-            x_turn(11)
-            x_out(6)
-            x_widen(12)
-            x_widen(13)
-            a_inter(1, "scalar")
-            a_inter(0)
-            x_quant(0)
-            x_out(7)
-            x_turn(12)
-            x_turn(13)
+            x_widen(10, "scalar")
+            for u in range(8, 14):
+                if u != 10:
+                    x_widen(u)
+                x_turn(u)
+                if u == 12:
+                    a_inter(2, "scalar")
+                    a_inter(1)
+                if u > 8:
+                    x_out(u - 6)
             x_out(8)
             x_out(9)
+            a_inter(0)
+
+            x_quant(0)
+            a_quant(0)
+            h_mm(0, (0, 1))
+            nc.vector.reciprocal(out=inv_norm[:], in_=norm_sb[:])
+            a_inter(3)
+            nc.vector.tensor_tensor(out=gain_rows[:], in0=mag_sb[:], in1=inv_norm[:], op=MULT)
             x_widen(14)
-            x_widen(15)
             x_turn(14)
-            x_turn(15)
             x_out(10)
             x_out(11)
-            a_quant(0)
-            h_mm(0)
+            h_mm(0, (2, 3))
+            x_quant(4)
+            x_widen(15)
             x_out(12)
             x_out(13)
+            x_turn(15)
+            h_mm(4, (0, 1))
+            a_quant(1)
+            x_quant(1)
+            h_mm(1)
+            a_inter(4, "scalar")
             x_out(14)
             x_out(15)
             nc.sync.dma_start(out=out[0].rearrange("(p j) -> p j", p=64), in_=gain_rows[:])
             load_w(range(PASSES, 2 * PASSES))
             nc.sync.dma_start(out=gain[:], in_=out[0].partition_broadcast(P))
             load_w(range(2 * PASSES, W_UNITS))
-            a_inter(2)
-            a_inter(3)
-            x_quant(1)
-            a_quant(1)
-            h_mm(1)
-            a_inter(6, "scalar")
-            a_inter(7, "scalar")
-            a_inter(4)
-            x_quant(4)
-            a_inter(5)
-            h_mm(4)
+            h_mm(4, (2, 3))
             x_quant(5)
             h_mm(5)
-            x_quant(2)
-            a_quant(2)
-            h_mm(2)
-            x_quant(3)
-            a_quant(3)
-            h_mm(3)
-            w_widen(0)
-            w_widen(1)
-            w_widen(2)
-            x_quant(6)
-            x_quant(7)
-            h_mm(6)
-            h_mm(7)
+            a_inter(5)
+            a_inter(6, "scalar")
+            a_inter(7)
+            for g in (2, 3):
+                x_quant(g)
+                a_quant(g)
+                h_mm(g)
+            for v in range(3):
+                w_widen(v)
+            for d in (6, 7):
+                x_quant(d)
+            for d in (6, 7):
+                h_mm(d)
+
             w_inter(0, "vector")
-            h_out(0, 0)
-            h_out(0, 1)
-            h_out(0, 2)
-            h_out(0, 3)
-            w_inter(1, "vector", [0])
-            w_inter(1, "vector", [1])
+            for t in range(4):
+                h_out(0, t)
+            w_inter(1, "vector", (0, 1))
             w_quant(0)
             y_mm(0, 0, group_a)
-            w_inter(1, "vector", [2])
-            w_inter(1, "vector", [3])
-            h_out(1, 0)
-            h_out(1, 1)
-            h_out(1, 2)
-            h_out(1, 3)
-            b_first(0, "vector")
+            w_inter(1, "vector", (2, 3))
+            for t in range(4):
+                h_out(1, t)
+            b_first(0)
             w_quant(1)
             y_mm(0, 1, group_a)
+            h_inter(0, 0)
             w_inter(2, "vector")
-            b_first(1, "vector")
+            b_first(1)
             y_mm(0, 0, group_b)
             y_mm(0, 1, group_b)
             w_widen(3)
             w_quant(2)
             y_mm(0, 2, group_a)
-            y_mm(0, 2, group_b)
-            h_inter(0, 0)
             h_inter(0, 1)
             w_widen(4)
             w_inter(3, "scalar")
-            w_inter(3, "vector")
-            quantise(bq[0][:], bqs[0][:], bg[0][:].rearrange("p n t -> p (n t)"))
+            w_inter(3, "vector", (0,))
             h_quant(0)
+            w_inter(3, "vector", (1,))
+            quantise(bq[0][:], bqs[0][:], bg[0][:].rearrange("p n t -> p (n t)"))
+            y_mm(0, 2, group_b)
             y_mm(0, UPDATE, group_a)
             h_inter(1, 0)
             w_quant(3)
@@ -442,60 +432,46 @@ def tile_dora_fp8_forward_d2_kernel(tc, x_bytes, x_scale, w_bytes, w_scale, a, l
             h_inter(1, 1)
             w_inter(4, "vector")
             w_inter(5, "scalar")
-            w_inter(5, "vector")
             w_widen(6)
             h_quant(1)
             y_mm(0, UPDATE, group_b)
-            w_quant(4)
-            b_later(1, 0, wg[4])
-            y_out(0, group_a[::-1])
-            y_mm(1, 0, group_a[::-1])
-            w_widen(7)
-            w_inter(6, "scalar")
-            w_quant(5)
-            y_mm(1, 1, group_a)
-            b_later(1, 1, wg[5])
-            y_out(0, group_b[::-1])
-            w_inter(6, "vector")
-            y_mm(1, 0, group_b[::-1])
-            y_mm(1, 1, group_b[::-1])
-            w_widen(8)
-            w_inter(7, "scalar")
-            w_inter(7, "vector")
-            w_quant(6)
-            b_later_quant(1, 0)
-            b_later_quant(1, 1)
-            y_mm(1, 2, group_a)
-            y_mm(1, UPDATE, group_a)
-            w_widen(9)
-            w_inter(8, "scalar")
-            w_quant(7)
-            y_mm(1, 3, group_a)
-            y_mm(1, 2, group_b[::-1])
-            y_mm(1, 3, group_b[::-1])
-            y_mm(1, UPDATE, group_b[::-1])
-            w_inter(8, "vector")
-            w_widen(10)
-            w_inter(9, "scalar")
-            w_inter(9, "vector")
-            w_quant(8)
-            b_later(2, 0, wg[8])
-            y_out(1, group_a[::-1])
-            y_mm(2, 0, group_a)
-            w_widen(11)
-            w_inter(10, "scalar")
-            w_inter(10, "vector")
-            w_quant(9)
-            y_mm(2, 1, group_a)
-            b_later(2, 1, wg[9])
-            y_out(1, group_b)
-            y_mm(2, 0, group_b)
-            y_mm(2, 1, group_b)
-            w_inter(11, "scalar")
-            w_inter(11, "vector")
-            w_quant(10)
-            b_later_quant(2, 0)
-            b_later_quant(2, 1)
+
+            for c in range(1, CHUNKS):
+                v = PASSES * c
+                group_b = group_b[::-1]
+                w_quant(v)
+                b_later(c, 0, wg[v])
+                y_out(c - 1, group_a[::-1])
+                y_mm(c, 0, group_a[::-1])
+                w_widen(v + 3)
+                w_inter(v + 2, "scalar")
+                w_quant(v + 1)
+                y_mm(c, 1, group_a)
+                b_later(c, 1, wg[v + 1])
+                y_out(c - 1, group_b)
+                for pair in (group_b[:2], group_b[2:]):
+                    y_mm(c, 0, pair)
+                    y_mm(c, 1, pair)
+                if c + 1 < CHUNKS:
+                    w_widen(v + 4)
+                w_inter(v + 3, "scalar")
+                b_later_quant(c, 0)
+                b_later_quant(c, 1)
+                w_quant(v + 2)
+                if c + 1 < CHUNKS:
+                    w_inter(v + 3, "vector")
+                    y_mm(c, UPDATE, group_a)
+                    y_mm(c, 2, group_a)
+                    w_widen(v + 5)
+                    w_inter(v + 4, "scalar")
+                    w_quant(v + 3)
+                    y_mm(c, 3, group_a)
+                    for g in (2, 3, UPDATE):
+                        y_mm(c, g, group_b)
+                    w_inter(v + 4, "vector")
+                    w_widen(v + 6)
+                    w_inter(v + 5, "scalar")
+                    w_inter(v + 5, "vector")
 
             c = CHUNKS - 1
             w_quant(W_UNITS - 1)

@@ -27,13 +27,12 @@ LAST_PARTS = (slice(0, 256), slice(256, 384), slice(384, 512))
 X_UNITS = 4 * PASSES
 W_UNITS = CHUNKS * PASSES
 
+X_ORDER = [4 * (n // 2) + n % 2 + 2 * k for n in range(4) for k in range(2)] + list(range(8, X_UNITS))
 
-def vector_blocks(v):
-    if v <= 2:
-        return 4
-    if v <= 4:
-        return 2
-    return 3 if 7 <= v <= 9 else 0
+X_ON_SCALAR = {1 + 4 * k: 1 + 5 * k for k in range(3)}
+EMPTY_LAG = 3
+BLOCKS_BESIDE_H = 2
+BLOCKS_BETWEEN = 3
 
 
 def tile_dora_fp8_forward_d2_kernel(tc, x_bytes, x_scale, w_bytes, w_scale, a, lam, b, mag, norm, out):
@@ -132,7 +131,7 @@ def tile_dora_fp8_forward_d2_kernel(tc, x_bytes, x_scale, w_bytes, w_scale, a, l
                         )
 
         def x_turn(u):
-            xbank[u] = bank(u % 8, [P, 2, 2, P])
+            xbank[u] = bank(X_ORDER.index(u) % 8, [P, 2, 2, P])
             for i in range(2):
                 words = xw[u][:, i, :].bitcast(F32)
                 for h in range(2):
@@ -219,12 +218,10 @@ def tile_dora_fp8_forward_d2_kernel(tc, x_bytes, x_scale, w_bytes, w_scale, a, l
                 out=ww[v][:].rearrange("p t n -> p (t n)"), in_=wb[v][:].rearrange("p t n -> p (t n)").bitcast(E4M3)
             )
 
-        def w_inter(v, engine, blocks=None):
+        def w_inter(v, engine, blocks=range(4)):
             c, g = divmod(v, PASSES)
             if v not in wg:
                 wg[v] = staged([P, CW, 4], "wg")
-            if blocks is None:
-                blocks = range(vector_blocks(v)) if engine == "vector" else range(vector_blocks(v), 4)
             for e in blocks:
                 cols = slice(128 * e, 128 * (e + 1))
                 dst, src = fours(wg[v][:, cols, :], ww[v][:, :, cols])
@@ -233,6 +230,12 @@ def tile_dora_fp8_forward_d2_kernel(tc, x_bytes, x_scale, w_bytes, w_scale, a, l
                     nc.vector.tensor_scalar(out=dst, in0=src, scalar1=scale, scalar2=None, op0=MULT)
                 else:
                     nc.scalar.activation(out=dst, in_=src, func=COPY, scale=scale)
+
+        def w_shared(v, blocks):
+            if v + 1 < W_UNITS:
+                w_widen(v + 1)
+            w_inter(v, "scalar", range(blocks, 4))
+            w_inter(v, "vector", range(blocks))
 
         def w_quant(v):
             wq[v] = keep.tile([P, CW], U32, name=f"wq{v}", tag="wq", bufs=2 * PASSES, align_bytes=256)
@@ -305,175 +308,118 @@ def tile_dora_fp8_forward_d2_kernel(tc, x_bytes, x_scale, w_bytes, w_scale, a, l
             nc.sync.dma_start(out=mag_sb[:], in_=mag.rearrange("(p j) -> p j", p=64))
             for g in range(1, PASSES):
                 nc.sync.dma_start(out=araw[g][:], in_=a_view[g])
-            load_w(range(2))
+            load_w(range(3))
             ws_view = w_scale.rearrange("(g q) n -> q g n", q=4)
             for q in range(4):
                 nc.sync.dma_start(out=ws[32 * q : 32 * (q + 1), :, 0 : N // 128], in_=ws_view[q].partition_broadcast(32))
-            load_w([2])
             for t in range(4):
                 nc.sync.dma_start(out=braw[:, t, :], in_=b_view[t])
             load_w([3])
 
-            x_widen(0)
-            x_widen(2, "scalar")
-            x_turn(0)
-            x_widen(1)
-            x_turn(2)
-            x_turn(1)
-            x_widen(3)
-            x_turn(3)
-            x_out(0)
-            x_widen(4)
-            x_widen(6, "scalar")
-            lam_turned = bank(7, [P, P], BF16)
-            nc.tensor.transpose(lam_turned[:], lam_rows[:], ident_bf[:])
-            x_turn(4)
-            x_out(2)
-            x_out(1)
-            nc.scalar.copy(out=lam_cols[:], in_=lam_turned[:, 0:4])
-            x_widen(5)
-            x_turn(6)
-            x_widen(7)
-            x_turn(5)
-            x_turn(7)
-            x_widen(10, "scalar")
-            for u in range(8, 14):
-                if u != 10:
+            for n, u in enumerate(X_ORDER):
+                if n not in X_ON_SCALAR.values():
                     x_widen(u)
+                if n in X_ON_SCALAR:
+                    x_widen(X_ORDER[X_ON_SCALAR[n]], "scalar")
                 x_turn(u)
-                if u == 12:
+                if n == 4:
+                    lam_turned = bank(7, [P, P], BF16)
+                    nc.tensor.transpose(lam_turned[:], lam_rows[:], ident_bf[:])
+                if n == 5:
+                    nc.scalar.copy(out=lam_cols[:], in_=lam_turned[:, 0:4])
+                if n >= EMPTY_LAG:
+                    x_out(X_ORDER[n - EMPTY_LAG])
+                if n - EMPTY_LAG == 11:
                     a_inter(2, "scalar")
-                    a_inter(1)
-                if u > 8:
-                    x_out(u - 6)
-            x_out(8)
-            x_out(9)
+            for u in X_ORDER[-EMPTY_LAG:]:
+                x_out(u)
+
             a_inter(0)
+            a_inter(1)
+            for g in range(PASSES + 1):
+                if g < PASSES:
+                    x_quant(g)
+                    a_quant(g)
+                    h_mm(g)
+                if g + 1 < PASSES:
+                    a_inter(2 * g + 3)
+                if g + 2 < PASSES:
+                    a_inter(2 * g + 4, "scalar")
+                if g == 0:
+                    nc.vector.reciprocal(out=inv_norm[:], in_=norm_sb[:])
+                if g == 1:
+                    nc.vector.tensor_tensor(out=gain_rows[:], in0=mag_sb[:], in1=inv_norm[:], op=MULT)
+                    nc.sync.dma_start(out=out[0].rearrange("(p j) -> p j", p=64), in_=gain_rows[:])
+                    load_w(range(PASSES, 2 * PASSES))
+                    nc.sync.dma_start(out=gain[:], in_=out[0].partition_broadcast(P))
+                    load_w(range(2 * PASSES, W_UNITS))
+                if g >= 1:
+                    x_quant(PASSES + g - 1)
+                    h_mm(PASSES + g - 1)
+                if g >= 2:
+                    w_widen(g - 2)
 
-            x_quant(0)
-            a_quant(0)
-            h_mm(0, (0, 1))
-            nc.vector.reciprocal(out=inv_norm[:], in_=norm_sb[:])
-            a_inter(3)
-            nc.vector.tensor_tensor(out=gain_rows[:], in0=mag_sb[:], in1=inv_norm[:], op=MULT)
-            x_widen(14)
-            x_turn(14)
-            x_out(10)
-            x_out(11)
-            h_mm(0, (2, 3))
-            x_quant(4)
-            x_widen(15)
-            x_out(12)
-            x_out(13)
-            x_turn(15)
-            h_mm(4, (0, 1))
-            a_quant(1)
-            x_quant(1)
-            h_mm(1)
-            a_inter(4, "scalar")
-            x_out(14)
-            x_out(15)
-            nc.sync.dma_start(out=out[0].rearrange("(p j) -> p j", p=64), in_=gain_rows[:])
-            load_w(range(PASSES, 2 * PASSES))
-            nc.sync.dma_start(out=gain[:], in_=out[0].partition_broadcast(P))
-            load_w(range(2 * PASSES, W_UNITS))
-            h_mm(4, (2, 3))
-            x_quant(5)
-            h_mm(5)
-            a_inter(5)
-            a_inter(6, "scalar")
-            a_inter(7)
-            for g in (2, 3):
-                x_quant(g)
-                a_quant(g)
-                h_mm(g)
-            for v in range(3):
-                w_widen(v)
-            for d in (6, 7):
-                x_quant(d)
-            for d in (6, 7):
-                h_mm(d)
-
-            w_inter(0, "vector")
-            for t in range(4):
-                h_out(0, t)
-            w_inter(1, "vector", (0, 1))
-            w_quant(0)
-            y_mm(0, 0, group_a)
-            w_inter(1, "vector", (2, 3))
-            for t in range(4):
-                h_out(1, t)
-            b_first(0)
-            w_quant(1)
-            y_mm(0, 1, group_a)
-            h_inter(0, 0)
-            w_inter(2, "vector")
-            b_first(1)
+            for half in range(2):
+                w_inter(half, "vector")
+                for t in range(4):
+                    h_out(half, t)
+            for g in range(2):
+                w_quant(g)
+                y_mm(0, g, group_a)
             y_mm(0, 0, group_b)
-            y_mm(0, 1, group_b)
             w_widen(3)
+            w_inter(2, "vector")
+            b_first(0)
             w_quant(2)
             y_mm(0, 2, group_a)
-            h_inter(0, 1)
-            w_widen(4)
-            w_inter(3, "scalar")
-            w_inter(3, "vector", (0,))
-            h_quant(0)
-            w_inter(3, "vector", (1,))
-            quantise(bq[0][:], bqs[0][:], bg[0][:].rearrange("p n t -> p (n t)"))
-            y_mm(0, 2, group_b)
-            y_mm(0, UPDATE, group_a)
-            h_inter(1, 0)
+            y_mm(0, 1, group_b)
+            b_first(1)
+            w_shared(3, BLOCKS_BESIDE_H)
+            h_inter(0, 0)
             w_quant(3)
             y_mm(0, 3, group_a)
+            y_mm(0, 2, group_b)
+            h_inter(0, 1)
+            quantise(bq[0][:], bqs[0][:], bg[0][:].rearrange("p n t -> p (n t)"))
+            h_quant(0)
+            y_mm(0, UPDATE, group_a)
             y_mm(0, 3, group_b)
-            w_widen(5)
-            w_inter(4, "scalar")
+            h_inter(1, 0)
             h_inter(1, 1)
-            w_inter(4, "vector")
-            w_inter(5, "scalar")
-            w_widen(6)
+            w_shared(4, BLOCKS_BESIDE_H)
             h_quant(1)
             y_mm(0, UPDATE, group_b)
+            w_shared(5, 0)
 
             for c in range(1, CHUNKS):
                 v = PASSES * c
-                group_b = group_b[::-1]
                 w_quant(v)
                 b_later(c, 0, wg[v])
-                y_out(c - 1, group_a[::-1])
-                y_mm(c, 0, group_a[::-1])
-                w_widen(v + 3)
-                w_inter(v + 2, "scalar")
+                y_out(c - 1, group_a)
+                y_mm(c, 0, group_a)
+                w_shared(v + 2, 0)
                 w_quant(v + 1)
                 y_mm(c, 1, group_a)
                 b_later(c, 1, wg[v + 1])
                 y_out(c - 1, group_b)
-                for pair in (group_b[:2], group_b[2:]):
-                    y_mm(c, 0, pair)
-                    y_mm(c, 1, pair)
-                if c + 1 < CHUNKS:
-                    w_widen(v + 4)
-                w_inter(v + 3, "scalar")
+                y_mm(c, 0, group_b)
+                y_mm(c, 1, group_b)
                 b_later_quant(c, 0)
                 b_later_quant(c, 1)
                 w_quant(v + 2)
                 if c + 1 < CHUNKS:
-                    w_inter(v + 3, "vector")
                     y_mm(c, UPDATE, group_a)
                     y_mm(c, 2, group_a)
-                    w_widen(v + 5)
-                    w_inter(v + 4, "scalar")
+                    w_shared(v + 3, BLOCKS_BETWEEN)
+                    w_shared(v + 4, BLOCKS_BETWEEN)
                     w_quant(v + 3)
                     y_mm(c, 3, group_a)
                     for g in (2, 3, UPDATE):
                         y_mm(c, g, group_b)
-                    w_inter(v + 4, "vector")
-                    w_widen(v + 6)
-                    w_inter(v + 5, "scalar")
-                    w_inter(v + 5, "vector")
+                    w_shared(v + 5, BLOCKS_BETWEEN)
 
             c = CHUNKS - 1
+            w_shared(W_UNITS - 1, 0)
             w_quant(W_UNITS - 1)
             pieces = [(i, WHOLE, i, (2, UPDATE, 3)) for i in range(TILES - 1)]
             pieces.append((TILES - 1, LAST_PARTS[0], TILES - 1, (2, UPDATE, 3)))

@@ -336,28 +336,27 @@ def tile_dora_fp8_forward_d2_kernel(tc, x_bytes, x_scale, w_bytes, w_scale, a, l
 
             a_inter(0)
             a_inter(1)
-            for g in range(PASSES + 1):
-                if g < PASSES:
+            for first in (0, 2):
+                for g in (first, first + 1):
                     x_quant(g)
                     a_quant(g)
                     h_mm(g)
-                if g + 1 < PASSES:
-                    a_inter(2 * g + 3)
-                if g + 2 < PASSES:
-                    a_inter(2 * g + 4, "scalar")
-                if g == 0:
+                    if g == 0:
+                        a_inter(3)
+                for g in (first, first + 1):
+                    x_quant(PASSES + g)
+                    h_mm(PASSES + g)
+                if first == 0:
+                    for n in range(4, 8):
+                        a_inter(n, "vector" if n % 2 else "scalar")
                     nc.vector.reciprocal(out=inv_norm[:], in_=norm_sb[:])
-                if g == 1:
-                    nc.vector.tensor_tensor(out=gain_rows[:], in0=mag_sb[:], in1=inv_norm[:], op=MULT)
-                    nc.sync.dma_start(out=out[0].rearrange("(p j) -> p j", p=64), in_=gain_rows[:])
                     load_w(range(PASSES, 2 * PASSES))
-                    nc.sync.dma_start(out=gain[:], in_=out[0].partition_broadcast(P))
-                    load_w(range(2 * PASSES, W_UNITS))
-                if g >= 1:
-                    x_quant(PASSES + g - 1)
-                    h_mm(PASSES + g - 1)
-                if g >= 2:
-                    w_widen(g - 2)
+                    for v in range(3):
+                        w_widen(v)
+            nc.vector.tensor_tensor(out=gain_rows[:], in0=mag_sb[:], in1=inv_norm[:], op=MULT)
+            nc.sync.dma_start(out=out[0].rearrange("(p j) -> p j", p=64), in_=gain_rows[:])
+            load_w(range(2 * PASSES, W_UNITS))
+            nc.sync.dma_start(out=gain[:], in_=out[0].partition_broadcast(P))
 
             for half in range(2):
                 w_inter(half, "vector")
@@ -402,8 +401,9 @@ def tile_dora_fp8_forward_d2_kernel(tc, x_bytes, x_scale, w_bytes, w_scale, a, l
                 y_mm(c, 1, group_a)
                 b_later(c, 1, wg[v + 1])
                 y_out(c - 1, group_b)
-                y_mm(c, 0, group_b)
-                y_mm(c, 1, group_b)
+                for i in group_b:
+                    y_mm(c, 0, [i])
+                    y_mm(c, 1, [i])
                 b_later_quant(c, 0)
                 b_later_quant(c, 1)
                 w_quant(v + 2)

@@ -31,7 +31,6 @@ X_ORDER = [4 * (n // 2) + n % 2 + 2 * k for n in range(4) for k in range(2)] + l
 
 X_ON_SCALAR = {1 + 4 * k: 1 + 5 * k for k in range(3)}
 EMPTY_LAG = 3
-BLOCKS_BESIDE_H = 2
 BLOCKS_BETWEEN = 3
 
 
@@ -344,27 +343,29 @@ def tile_dora_fp8_forward_d2_kernel(tc, x_bytes, x_scale, w_bytes, w_scale, a, l
                     if g == 0:
                         a_inter(3)
                 for g in (first, first + 1):
+                    if g == PASSES - 1:
+                        w_inter(0, "vector")
                     x_quant(PASSES + g)
                     h_mm(PASSES + g)
                 if first == 0:
                     for n in range(4, 8):
                         a_inter(n, "vector" if n % 2 else "scalar")
                     nc.vector.reciprocal(out=inv_norm[:], in_=norm_sb[:])
-                    load_w(range(PASSES, 2 * PASSES))
+                    load_w(range(PASSES, W_UNITS))
                     for v in range(3):
                         w_widen(v)
-            nc.vector.tensor_tensor(out=gain_rows[:], in0=mag_sb[:], in1=inv_norm[:], op=MULT)
-            nc.sync.dma_start(out=out[0].rearrange("(p j) -> p j", p=64), in_=gain_rows[:])
-            load_w(range(2 * PASSES, W_UNITS))
-            nc.sync.dma_start(out=gain[:], in_=out[0].partition_broadcast(P))
 
             for half in range(2):
-                w_inter(half, "vector")
                 for t in range(4):
                     h_out(half, t)
-            for g in range(2):
-                w_quant(g)
-                y_mm(0, g, group_a)
+            w_quant(0)
+            y_mm(0, 0, group_a)
+            w_inter(1, "vector")
+            nc.vector.tensor_tensor(out=gain_rows[:], in0=mag_sb[:], in1=inv_norm[:], op=MULT)
+            nc.sync.dma_start(out=out[0].rearrange("(p j) -> p j", p=64), in_=gain_rows[:])
+            nc.sync.dma_start(out=gain[:], in_=out[0].partition_broadcast(P))
+            w_quant(1)
+            y_mm(0, 1, group_a)
             y_mm(0, 0, group_b)
             w_widen(3)
             w_inter(2, "vector")
@@ -373,7 +374,7 @@ def tile_dora_fp8_forward_d2_kernel(tc, x_bytes, x_scale, w_bytes, w_scale, a, l
             y_mm(0, 2, group_a)
             y_mm(0, 1, group_b)
             b_first(1)
-            w_shared(3, BLOCKS_BESIDE_H)
+            w_inter(3, "vector")
             h_inter(0, 0)
             w_quant(3)
             y_mm(0, 3, group_a)
@@ -383,12 +384,14 @@ def tile_dora_fp8_forward_d2_kernel(tc, x_bytes, x_scale, w_bytes, w_scale, a, l
             h_quant(0)
             y_mm(0, UPDATE, group_a)
             y_mm(0, 3, group_b)
+            w_widen(4)
+            w_shared(4, 0)
+            w_inter(5, "scalar")
+            w_widen(6)
             h_inter(1, 0)
             h_inter(1, 1)
-            w_shared(4, BLOCKS_BESIDE_H)
             h_quant(1)
             y_mm(0, UPDATE, group_b)
-            w_shared(5, 0)
 
             for c in range(1, CHUNKS):
                 v = PASSES * c

@@ -13,7 +13,6 @@ U8 = mybir.dt.uint8
 E4M3 = mybir.dt.float8_e4m3fn
 MX = mybir.dt.float8_e4m3fn_x4
 MULT = mybir.AluOpType.mult
-ADD = mybir.AluOpType.add
 COPY = mybir.ActivationFunctionType.Copy
 
 P = 128
@@ -28,10 +27,8 @@ X_UNITS = 4 * PASSES
 W_UNITS = CHUNKS * PASSES
 
 X_ORDER = [4 * (n // 2) + n % 2 + 2 * k for n in range(4) for k in range(2)] + list(range(8, X_UNITS))
-
-X_ON_SCALAR = {1 + 4 * k: 1 + 5 * k for k in range(3)}
+X_ON_SCALAR = 1
 EMPTY_LAG = 3
-BLOCKS_BETWEEN = 3
 
 
 def tile_dora_fp8_forward_d2_kernel(tc, x_bytes, x_scale, w_bytes, w_scale, a, lam, b, mag, norm, out):
@@ -91,6 +88,9 @@ def tile_dora_fp8_forward_d2_kernel(tc, x_bytes, x_scale, w_bytes, w_scale, a, l
             rows = slice(4 * half + tiles.start, 4 * half + tiles.stop)
             nc.sync.dma_start(out=xb[n][:, tiles, :], in_=x_view[:, rows, k : k + K // 2])
 
+        def load_a(g):
+            nc.sync.dma_start(out=araw[g][:], in_=a_view[g])
+
         def load_w(units):
             for v in units:
                 c, g = divmod(v, PASSES)
@@ -146,27 +146,27 @@ def tile_dora_fp8_forward_d2_kernel(tc, x_bytes, x_scale, w_bytes, w_scale, a, l
                 in_=xbank[u][:].rearrange("p i h r -> p i r h"),
             )
 
-        def x_quant(d):
-            half, g = divmod(d, PASSES)
+        def x_quant(half, g):
+            d = PASSES * half + g
             quantise(xq[:, half, g, :], xqs[:, half, g, :], xg[d][:].rearrange("p j i r t -> p (j i r t)"))
 
         ag, hbank, hb, hg = {}, {}, {}, {}
 
-        def a_inter(n, engine="vector"):
-            g, e = n // 2, 1 - n % 2
+        def a_inter(g, e, engine):
             if g not in ag:
-                ag[g] = staged([P, 4, P, 4], "wga")
+                ag[g] = staged([P, 4, P, 4], "ag")
             for t in (2 * e, 2 * e + 1):
                 dst = ag[g][:, t].rearrange("p (q c i) j -> p q c j i", c=2, i=4)
                 src = araw[g][:].rearrange("p j (q t c i) -> p t q c j i", t=4, c=2, i=4)[:, t]
                 copy_on(engine, dst, src)
 
-        def a_quant(g):
-            quantise(aq[:, g, :], aqs[:, g, :], ag[g][:].rearrange("p t m j -> p (t m j)"))
+        def a_quant(g, halves):
+            cols = slice(256 * halves.start, 256 * halves.stop)
+            values = ag[g][:, 2 * halves.start : 2 * halves.stop].rearrange("p t m j -> p (t m j)")
+            quantise(aq[:, g, cols], aqs[:, g, cols], values)
 
-        def h_mm(d, ts=range(4)):
-            half, g = divmod(d, PASSES)
-            for t in ts:
+        def h_mm(half, g):
+            for t in range(4):
                 if g == 0:
                     hbank[half, t] = bank(4 * half + t, [P, 512])
                 nc.tensor.matmul_mx(
@@ -179,62 +179,50 @@ def tile_dora_fp8_forward_d2_kernel(tc, x_bytes, x_scale, w_bytes, w_scale, a, l
                     stop=(g == PASSES - 1),
                 )
 
-        def h_out(half, t):
-            if half not in hb:
-                hb[half] = staged([P, 4, 512], "hb")
-            nc.scalar.activation(out=hb[half][:, t, :], in_=hbank[half, t][:], func=COPY, scale=lam_cols[:, t : t + 1])
+        def h_out(half):
+            hb[half] = staged([P, 4, 512], "hb")
+            for t in range(4):
+                nc.scalar.activation(
+                    out=hb[half][:, t, :], in_=hbank[half, t][:], func=COPY, scale=lam_cols[:, t : t + 1]
+                )
 
-        def h_inter(half, e):
+        def h_inter(half, e, engine):
             if half not in hg:
                 hg[half] = staged([P, 512, 4], "hg")
             n = slice(256 * e, 256 * (e + 1))
-            copy_on("vector", *fours(hg[half][:, n, :], hb[half][:, :, n]))
+            copy_on(engine, *fours(hg[half][:, n, :], hb[half][:, :, n]))
 
         def h_quant(half):
             cols = slice(512 * half, 512 * (half + 1))
             quantise(hq[:, cols], hqs[:, cols], hg[half][:].rearrange("p n t -> p (n t)"))
 
-        bg, ww, wg = {}, {}, {}
+        bg, wg = {}, {}
 
-        def b_first(e):
-            if 0 not in bg:
-                bg[0] = staged([P, CW, 4], "wgb")
+        def b_inter(c, e, engine):
+            if c not in bg:
+                bg[c] = staged([P, CW, 4], "bg")
             n = slice(256 * e, 256 * (e + 1))
-            copy_on("vector", *fours(bg[0][:, n, :], braw[:, :, n]))
+            copy_on(engine, *fours(bg[c][:, n, :], braw[:, :, CW * c + n.start : CW * c + n.stop]))
 
-        def b_later(c, e, tile):
-            bg[c, e] = tile
-            src = braw[:, :, CW * c + 256 * e : CW * c + 256 * (e + 1)].rearrange("p t n -> p n t")
-            nc.gpsimd.tensor_scalar(out=tile[:, 0:256, :], in0=src, scalar1=1.0, scalar2=0.0, op0=MULT, op1=ADD)
+        def b_quant(c):
+            quantise(bq[c][:], bqs[c][:], bg[c][:].rearrange("p n t -> p (n t)"))
 
-        def b_later_quant(c, e):
-            cols = slice(256 * e, 256 * (e + 1))
-            quantise(bq[c][:, cols], bqs[c][:, cols], bg[c, e][:, 0:256, :].rearrange("p n t -> p (n t)"))
-
-        def w_widen(v):
-            ww[v] = staged([P, 4, CW], "ww")
-            nc.scalar.copy(
-                out=ww[v][:].rearrange("p t n -> p (t n)"), in_=wb[v][:].rearrange("p t n -> p (t n)").bitcast(E4M3)
-            )
-
-        def w_inter(v, engine, blocks=range(4)):
+        def w_inter(v, engine, blocks=slice(0, 4)):
             c, g = divmod(v, PASSES)
+            rows = wb[v][:, :, 128 * blocks.start : 128 * blocks.stop].bitcast(E4M3)
+            if engine == "scalar":
+                cast = staged([P, 4, 128 * (blocks.stop - blocks.start)], "cast")
+                nc.scalar.copy(out=cast[:], in_=rows)
+                rows = cast[:]
             if v not in wg:
                 wg[v] = staged([P, CW, 4], "wg")
-            for e in blocks:
-                cols = slice(128 * e, 128 * (e + 1))
-                dst, src = fours(wg[v][:, cols, :], ww[v][:, :, cols])
+            for n, e in enumerate(range(blocks.start, blocks.stop)):
+                dst, src = fours(wg[v][:, 128 * e : 128 * (e + 1), :], rows[:, :, 128 * n : 128 * (n + 1)])
                 scale = ws[:, g, 4 * c + e : 4 * c + e + 1]
                 if engine == "vector":
                     nc.vector.tensor_scalar(out=dst, in0=src, scalar1=scale, scalar2=None, op0=MULT)
                 else:
                     nc.scalar.activation(out=dst, in_=src, func=COPY, scale=scale)
-
-        def w_shared(v, blocks):
-            if v + 1 < W_UNITS:
-                w_widen(v + 1)
-            w_inter(v, "scalar", range(blocks, 4))
-            w_inter(v, "vector", range(blocks))
 
         def w_quant(v):
             wq[v] = keep.tile([P, CW], U32, name=f"wq{v}", tag="wq", bufs=2 * PASSES, align_bytes=256)
@@ -279,13 +267,18 @@ def tile_dora_fp8_forward_d2_kernel(tc, x_bytes, x_scale, w_bytes, w_scale, a, l
             )
 
         def y_out(c, tiles):
-            for n, i in enumerate(tiles):
+            for i in tiles:
                 y_scale(c, i, WHOLE)
-                if n % 2 == 1:
-                    i0 = i - i % 2
-                    nc.sync.dma_start(out=out_view[:, i0 : i0 + 2, CW * c : CW * (c + 1)], in_=res[c, i // 2][:])
+                if i % 2 == 1:
+                    nc.sync.dma_start(out=out_view[:, i - 1 : i + 1, CW * c : CW * (c + 1)], in_=res[c, i // 2][:])
 
         group_a, group_b = [0, 1, 2, 3], [4, 5, 6, 7]
+        first, second, both = slice(0, 1), slice(1, 2), slice(0, 2)
+
+        def y_by_turns(c, g_a, g_b):
+            for i, j in zip(group_a, group_b):
+                y_mm(c, g_a, [i])
+                y_mm(c, g_b, [j])
 
         with tc.manual_schedule(
             engines={mybir.EngineType.PE, mybir.EngineType.DVE, mybir.EngineType.Activation, mybir.EngineType.SP}
@@ -298,28 +291,28 @@ def tile_dora_fp8_forward_d2_kernel(tc, x_bytes, x_scale, w_bytes, w_scale, a, l
                 in_=lam.rearrange("(q t i) -> t q i", t=4, i=8),
             )
             nc.scalar.activation(out=ident_bf[:], in_=ident[:], func=COPY)
+            load_a(0)
             load_x(1, slice(0, 2))
             load_x(1, slice(2, 4))
             load_x(2, slice(0, 4))
             load_x(3, slice(0, 4))
-            nc.sync.dma_start(out=araw[0][:], in_=a_view[0])
+            load_a(1)
             nc.sync.dma_start(out=norm_sb[:], in_=norm.rearrange("(p j) -> p j", p=64))
             nc.sync.dma_start(out=mag_sb[:], in_=mag.rearrange("(p j) -> p j", p=64))
-            for g in range(1, PASSES):
-                nc.sync.dma_start(out=araw[g][:], in_=a_view[g])
-            load_w(range(3))
+            load_a(2)
+            load_a(3)
+            load_w(range(2))
             ws_view = w_scale.rearrange("(g q) n -> q g n", q=4)
             for q in range(4):
                 nc.sync.dma_start(out=ws[32 * q : 32 * (q + 1), :, 0 : N // 128], in_=ws_view[q].partition_broadcast(32))
             for t in range(4):
                 nc.sync.dma_start(out=braw[:, t, :], in_=b_view[t])
-            load_w([3])
+            load_w(range(2, W_UNITS))
 
+            x_widen(X_ORDER[X_ON_SCALAR], "scalar")
             for n, u in enumerate(X_ORDER):
-                if n not in X_ON_SCALAR.values():
+                if n != X_ON_SCALAR:
                     x_widen(u)
-                if n in X_ON_SCALAR:
-                    x_widen(X_ORDER[X_ON_SCALAR[n]], "scalar")
                 x_turn(u)
                 if n == 4:
                     lam_turned = bank(7, [P, P], BF16)
@@ -328,104 +321,105 @@ def tile_dora_fp8_forward_d2_kernel(tc, x_bytes, x_scale, w_bytes, w_scale, a, l
                     nc.scalar.copy(out=lam_cols[:], in_=lam_turned[:, 0:4])
                 if n >= EMPTY_LAG:
                     x_out(X_ORDER[n - EMPTY_LAG])
-                if n - EMPTY_LAG == 11:
-                    a_inter(2, "scalar")
+                if n in (3, 4):
+                    a_inter(0, n - 3, "scalar")
             for u in X_ORDER[-EMPTY_LAG:]:
                 x_out(u)
 
-            a_inter(0)
-            a_inter(1)
-            for first in (0, 2):
-                for g in (first, first + 1):
-                    x_quant(g)
-                    a_quant(g)
-                    h_mm(g)
-                    if g == 0:
-                        a_inter(3)
-                for g in (first, first + 1):
-                    if g == PASSES - 1:
-                        w_inter(0, "vector")
-                    x_quant(PASSES + g)
-                    h_mm(PASSES + g)
-                if first == 0:
-                    for n in range(4, 8):
-                        a_inter(n, "vector" if n % 2 else "scalar")
-                    nc.vector.reciprocal(out=inv_norm[:], in_=norm_sb[:])
-                    load_w(range(PASSES, W_UNITS))
-                    for v in range(3):
-                        w_widen(v)
+            x_quant(0, 0)
+            a_quant(0, both)
+            h_mm(0, 0)
+            a_inter(1, 0, "vector")
+            x_quant(1, 0)
+            h_mm(1, 0)
+            a_inter(1, 1, "vector")
+            x_quant(0, 1)
+            a_quant(1, both)
+            h_mm(0, 1)
+            x_quant(1, 1)
+            h_mm(1, 1)
+            for g in (2, 3):
+                a_inter(g, 0, "scalar")
+                a_inter(g, 1, "scalar")
+                x_quant(0, g)
+                a_quant(g, both)
+                h_mm(0, g)
+                if g == 3:
+                    w_inter(0, "vector")
+                x_quant(1, g)
+                h_mm(1, g)
 
-            for half in range(2):
-                for t in range(4):
-                    h_out(half, t)
+            b_inter(0, 0, "scalar")
+            b_inter(0, 1, "scalar")
+            h_out(0)
+            h_out(1)
             w_quant(0)
-            y_mm(0, 0, group_a)
             w_inter(1, "vector")
+            nc.vector.reciprocal(out=inv_norm[:], in_=norm_sb[:])
+            w_quant(1)
             nc.vector.tensor_tensor(out=gain_rows[:], in0=mag_sb[:], in1=inv_norm[:], op=MULT)
             nc.sync.dma_start(out=out[0].rearrange("(p j) -> p j", p=64), in_=gain_rows[:])
             nc.sync.dma_start(out=gain[:], in_=out[0].partition_broadcast(P))
-            w_quant(1)
-            y_mm(0, 1, group_a)
-            y_mm(0, 0, group_b)
-            w_widen(3)
-            w_inter(2, "vector")
-            b_first(0)
-            w_quant(2)
-            y_mm(0, 2, group_a)
+            y_mm(0, 0, group_a)
+            for i, j in zip(group_a, group_b):
+                y_mm(0, 0, [j])
+                y_mm(0, 1, [i])
             y_mm(0, 1, group_b)
-            b_first(1)
+            h_inter(0, 0, "scalar")
+            h_inter(0, 1, "scalar")
+            h_inter(1, 0, "scalar")
+            h_inter(1, 1, "scalar")
+            w_inter(2, "vector")
             w_inter(3, "vector")
-            h_inter(0, 0)
+            w_quant(2)
             w_quant(3)
+            y_mm(0, 2, group_a + group_b)
             y_mm(0, 3, group_a)
-            y_mm(0, 2, group_b)
-            h_inter(0, 1)
-            quantise(bq[0][:], bqs[0][:], bg[0][:].rearrange("p n t -> p (n t)"))
+            w_inter(4, "vector")
+            b_quant(0)
+            w_quant(4)
             h_quant(0)
-            y_mm(0, UPDATE, group_a)
-            y_mm(0, 3, group_b)
-            w_widen(4)
-            w_shared(4, 0)
-            w_inter(5, "scalar")
-            w_widen(6)
-            h_inter(1, 0)
-            h_inter(1, 1)
+            y_by_turns(0, UPDATE, 3)
+            w_inter(6, "vector", slice(0, 2))
             h_quant(1)
             y_mm(0, UPDATE, group_b)
+            w_inter(5, "scalar")
 
-            for c in range(1, CHUNKS):
-                v = PASSES * c
-                w_quant(v)
-                b_later(c, 0, wg[v])
-                y_out(c - 1, group_a)
-                y_mm(c, 0, group_a)
-                w_shared(v + 2, 0)
-                w_quant(v + 1)
-                y_mm(c, 1, group_a)
-                b_later(c, 1, wg[v + 1])
-                y_out(c - 1, group_b)
-                for i in group_b:
-                    y_mm(c, 0, [i])
-                    y_mm(c, 1, [i])
-                b_later_quant(c, 0)
-                b_later_quant(c, 1)
-                w_quant(v + 2)
-                if c + 1 < CHUNKS:
-                    y_mm(c, UPDATE, group_a)
-                    y_mm(c, 2, group_a)
-                    w_shared(v + 3, BLOCKS_BETWEEN)
-                    w_shared(v + 4, BLOCKS_BETWEEN)
-                    w_quant(v + 3)
-                    y_mm(c, 3, group_a)
-                    for g in (2, 3, UPDATE):
-                        y_mm(c, g, group_b)
-                    w_shared(v + 5, BLOCKS_BETWEEN)
+            y_out(0, group_a + group_b)
+            y_mm(1, 0, group_a + group_b)
+            w_quant(5)
+            y_mm(1, 1, group_a + group_b)
+            b_inter(1, 0, "scalar")
+            b_inter(1, 1, "scalar")
+            w_inter(9, "scalar")
+            w_inter(6, "vector", slice(2, 4))
+            w_inter(7, "vector", slice(0, 2))
+            w_quant(6)
+            y_mm(1, 2, group_a + group_b)
+            w_inter(7, "vector", slice(2, 4))
+            w_inter(8, "vector", slice(0, 2))
+            w_quant(7)
+            y_mm(1, 3, group_a)
+            w_inter(8, "vector", slice(2, 4))
+            b_quant(1)
+            w_quant(8)
+            w_quant(9)
+            y_by_turns(1, UPDATE, 3)
+            y_mm(1, UPDATE, group_b)
+            b_inter(2, 0, "scalar")
+            b_inter(2, 1, "scalar")
+            w_inter(10, "scalar")
 
             c = CHUNKS - 1
-            w_shared(W_UNITS - 1, 0)
-            w_quant(W_UNITS - 1)
-            pieces = [(i, WHOLE, i, (2, UPDATE, 3)) for i in range(TILES - 1)]
-            pieces.append((TILES - 1, LAST_PARTS[0], TILES - 1, (2, UPDATE, 3)))
+            y_out(1, group_a + group_b)
+            y_mm(2, 0, group_a + group_b)
+            y_mm(2, 1, group_a + group_b)
+            w_inter(11, "vector")
+            b_quant(c)
+            w_quant(10)
+            w_quant(11)
+            pieces = [(i, WHOLE, i, (UPDATE, 2, 3)) for i in range(TILES - 1)]
+            pieces.append((TILES - 1, LAST_PARTS[0], TILES - 1, (UPDATE, 2, 3)))
             pieces.extend((TILES - 1, part, n, range(PASSES + 1)) for n, part in enumerate(LAST_PARTS[1:]))
             for i, part, n, passes in pieces:
                 for g in passes:

@@ -62,8 +62,10 @@ def tile_dora_fp8_forward_d2_kernel(tc, x_bytes, x_scale, w_bytes, w_scale, a, l
         gain = kept([P, N], F32, "gain")
         xb = [big.tile([P, 4, K // 2], U8, name=f"xb{n}", tag="big", align_bytes=256) for n in range(4)]
         araw = [big.tile([P, 4, R], BF16, name=f"araw{g}", tag="big", align_bytes=256) for g in range(PASSES)]
-        wb = [kept([P, 4, CW], U8, f"wb{v}") for v in range(W_UNITS)]
-        braw = kept([P, 4, N], BF16, "braw")
+        wb_first = [kept([P, 4, CW], U8, f"wb_first{g}") for g in range(PASSES)]
+        wb_later = [kept([P, 4, N - CW], U8, f"wb_later{g}") for g in range(PASSES)]
+        braw_first = kept([P, 4, CW], BF16, "braw_first")
+        braw_later = kept([P, 4, N - CW], BF16, "braw_later")
         xq = kept([P, 2, PASSES, 512], U32, "xq")
         xqs = kept([P, 2, PASSES, 512], U8, "xqs")
         aq = kept([P, PASSES, R], U32, "aq")
@@ -91,10 +93,15 @@ def tile_dora_fp8_forward_d2_kernel(tc, x_bytes, x_scale, w_bytes, w_scale, a, l
         def load_a(g):
             nc.sync.dma_start(out=araw[g][:], in_=a_view[g])
 
-        def load_w(units):
-            for v in units:
-                c, g = divmod(v, PASSES)
-                nc.sync.dma_start(out=wb[v][:], in_=w_view[g][:, :, CW * c : CW * (c + 1)])
+        def load_w(tiles, g, cols):
+            nc.sync.dma_start(out=tiles[g][:], in_=w_view[g][:, :, cols])
+
+        def load_b(tile, cols):
+            for t in range(4):
+                nc.sync.dma_start(out=tile[:, t, :], in_=b_view[t][:, :, cols])
+
+        def columns(first, rest, c, start, stop):
+            return first[:, :, start:stop] if c == 0 else rest[:, :, CW * (c - 1) + start : CW * (c - 1) + stop]
 
         def copy_on(engine, dst, src):
             if engine == "vector":
@@ -202,14 +209,14 @@ def tile_dora_fp8_forward_d2_kernel(tc, x_bytes, x_scale, w_bytes, w_scale, a, l
             if c not in bg:
                 bg[c] = staged([P, CW, 4], "bg")
             n = slice(256 * e, 256 * (e + 1))
-            copy_on(engine, *fours(bg[c][:, n, :], braw[:, :, CW * c + n.start : CW * c + n.stop]))
+            copy_on(engine, *fours(bg[c][:, n, :], columns(braw_first, braw_later, c, n.start, n.stop)))
 
         def b_quant(c):
             quantise(bq[c][:], bqs[c][:], bg[c][:].rearrange("p n t -> p (n t)"))
 
         def w_inter(v, engine, blocks=slice(0, 4)):
             c, g = divmod(v, PASSES)
-            rows = wb[v][:, :, 128 * blocks.start : 128 * blocks.stop].bitcast(E4M3)
+            rows = columns(wb_first[g], wb_later[g], c, 128 * blocks.start, 128 * blocks.stop).bitcast(E4M3)
             if engine == "scalar":
                 cast = staged([P, 4, 128 * (blocks.stop - blocks.start)], "cast")
                 nc.scalar.copy(out=cast[:], in_=rows)
@@ -273,7 +280,8 @@ def tile_dora_fp8_forward_d2_kernel(tc, x_bytes, x_scale, w_bytes, w_scale, a, l
                     nc.sync.dma_start(out=out_view[:, i - 1 : i + 1, CW * c : CW * (c + 1)], in_=res[c, i // 2][:])
 
         group_a, group_b = [0, 1, 2, 3], [4, 5, 6, 7]
-        first, second, both = slice(0, 1), slice(1, 2), slice(0, 2)
+        both = slice(0, 2)
+        later = slice(CW, N)
 
         def y_by_turns(c, g_a, g_b):
             for i, j in zip(group_a, group_b):
@@ -301,13 +309,13 @@ def tile_dora_fp8_forward_d2_kernel(tc, x_bytes, x_scale, w_bytes, w_scale, a, l
             nc.sync.dma_start(out=mag_sb[:], in_=mag.rearrange("(p j) -> p j", p=64))
             load_a(2)
             load_a(3)
-            load_w(range(2))
+            load_w(wb_first, 0, WHOLE)
             ws_view = w_scale.rearrange("(g q) n -> q g n", q=4)
             for q in range(4):
                 nc.sync.dma_start(out=ws[32 * q : 32 * (q + 1), :, 0 : N // 128], in_=ws_view[q].partition_broadcast(32))
-            for t in range(4):
-                nc.sync.dma_start(out=braw[:, t, :], in_=b_view[t])
-            load_w(range(2, W_UNITS))
+            load_b(braw_first, WHOLE)
+            for g in range(1, PASSES):
+                load_w(wb_first, g, WHOLE)
 
             x_widen(X_ORDER[X_ON_SCALAR], "scalar")
             for n, u in enumerate(X_ORDER):
@@ -336,8 +344,17 @@ def tile_dora_fp8_forward_d2_kernel(tc, x_bytes, x_scale, w_bytes, w_scale, a, l
             x_quant(0, 1)
             a_quant(1, both)
             h_mm(0, 1)
+            nc.vector.reciprocal(out=inv_norm[:], in_=norm_sb[:])
             x_quant(1, 1)
             h_mm(1, 1)
+            nc.vector.tensor_tensor(out=gain_rows[:], in0=mag_sb[:], in1=inv_norm[:], op=MULT)
+            nc.sync.dma_start(out=out[0].rearrange("(p j) -> p j", p=64), in_=gain_rows[:])
+            load_w(wb_later, 0, later)
+            load_w(wb_later, 1, later)
+            nc.sync.dma_start(out=gain[:], in_=out[0].partition_broadcast(P))
+            load_w(wb_later, 2, later)
+            load_b(braw_later, later)
+            load_w(wb_later, 3, later)
             for g in (2, 3):
                 a_inter(g, 0, "scalar")
                 a_inter(g, 1, "scalar")
@@ -353,13 +370,11 @@ def tile_dora_fp8_forward_d2_kernel(tc, x_bytes, x_scale, w_bytes, w_scale, a, l
             b_inter(0, 1, "scalar")
             h_out(0)
             h_out(1)
+            w_inter(1, "vector", slice(0, 2))
             w_quant(0)
-            w_inter(1, "vector")
-            nc.vector.reciprocal(out=inv_norm[:], in_=norm_sb[:])
+            w_inter(1, "vector", slice(2, 4))
+            w_inter(2, "vector", slice(0, 1))
             w_quant(1)
-            nc.vector.tensor_tensor(out=gain_rows[:], in0=mag_sb[:], in1=inv_norm[:], op=MULT)
-            nc.sync.dma_start(out=out[0].rearrange("(p j) -> p j", p=64), in_=gain_rows[:])
-            nc.sync.dma_start(out=gain[:], in_=out[0].partition_broadcast(P))
             y_mm(0, 0, group_a)
             for i, j in zip(group_a, group_b):
                 y_mm(0, 0, [j])
@@ -369,7 +384,7 @@ def tile_dora_fp8_forward_d2_kernel(tc, x_bytes, x_scale, w_bytes, w_scale, a, l
             h_inter(0, 1, "scalar")
             h_inter(1, 0, "scalar")
             h_inter(1, 1, "scalar")
-            w_inter(2, "vector")
+            w_inter(2, "vector", slice(1, 4))
             w_inter(3, "vector")
             w_quant(2)
             w_quant(3)

@@ -13,6 +13,7 @@ U8 = mybir.dt.uint8
 E4M3 = mybir.dt.float8_e4m3fn
 MX = mybir.dt.float8_e4m3fn_x4
 MULT = mybir.AluOpType.mult
+ADD = mybir.AluOpType.add
 COPY = mybir.ActivationFunctionType.Copy
 
 P = 128
@@ -28,6 +29,8 @@ W_UNITS = CHUNKS * PASSES
 
 X_ORDER = [4 * (n // 2) + n % 2 + 2 * k for n in range(4) for k in range(2)] + list(range(8, X_UNITS))
 X_ON_SCALAR = 1
+X_BANKS = list(range(8)) + [0, 1] + [4, 5, 6, 7, 4, 5]
+EARLY = 13
 EMPTY_LAG = 3
 
 
@@ -137,7 +140,7 @@ def tile_dora_fp8_forward_d2_kernel(tc, x_bytes, x_scale, w_bytes, w_scale, a, l
                         )
 
         def x_turn(u):
-            xbank[u] = bank(X_ORDER.index(u) % 8, [P, 2, 2, P])
+            xbank[u] = bank(X_BANKS[X_ORDER.index(u)], [P, 2, 2, P])
             for i in range(2):
                 words = xw[u][:, i, :].bitcast(F32)
                 for h in range(2):
@@ -172,8 +175,8 @@ def tile_dora_fp8_forward_d2_kernel(tc, x_bytes, x_scale, w_bytes, w_scale, a, l
             values = ag[g][:, 2 * halves.start : 2 * halves.stop].rearrange("p t m j -> p (t m j)")
             quantise(aq[:, g, cols], aqs[:, g, cols], values)
 
-        def h_mm(half, g):
-            for t in range(4):
+        def h_mm(half, g, ts=range(4)):
+            for t in ts:
                 if g == 0:
                     hbank[half, t] = bank(4 * half + t, [P, 512])
                 nc.tensor.matmul_mx(
@@ -210,6 +213,11 @@ def tile_dora_fp8_forward_d2_kernel(tc, x_bytes, x_scale, w_bytes, w_scale, a, l
                 bg[c] = staged([P, CW, 4], "bg")
             n = slice(256 * e, 256 * (e + 1))
             copy_on(engine, *fours(bg[c][:, n, :], columns(braw_first, braw_later, c, n.start, n.stop)))
+
+        def b_later(c, tile):
+            bg[c] = tile
+            src = columns(braw_first, braw_later, c, 0, CW).rearrange("p t n -> p n t")
+            nc.gpsimd.tensor_scalar(out=tile[:], in0=src, scalar1=1.0, scalar2=0.0, op0=MULT, op1=ADD)
 
         def b_quant(c):
             quantise(bq[c][:], bqs[c][:], bg[c][:].rearrange("p n t -> p (n t)"))
@@ -280,7 +288,7 @@ def tile_dora_fp8_forward_d2_kernel(tc, x_bytes, x_scale, w_bytes, w_scale, a, l
                     nc.sync.dma_start(out=out_view[:, i - 1 : i + 1, CW * c : CW * (c + 1)], in_=res[c, i // 2][:])
 
         group_a, group_b = [0, 1, 2, 3], [4, 5, 6, 7]
-        both = slice(0, 2)
+        first, second, both = slice(0, 1), slice(1, 2), slice(0, 2)
         later = slice(CW, N)
 
         def y_by_turns(c, g_a, g_b):
@@ -299,8 +307,8 @@ def tile_dora_fp8_forward_d2_kernel(tc, x_bytes, x_scale, w_bytes, w_scale, a, l
                 in_=lam.rearrange("(q t i) -> t q i", t=4, i=8),
             )
             nc.scalar.activation(out=ident_bf[:], in_=ident[:], func=COPY)
-            load_a(0)
             load_x(1, slice(0, 2))
+            load_a(0)
             load_x(1, slice(2, 4))
             load_x(2, slice(0, 4))
             load_x(3, slice(0, 4))
@@ -319,6 +327,14 @@ def tile_dora_fp8_forward_d2_kernel(tc, x_bytes, x_scale, w_bytes, w_scale, a, l
 
             x_widen(X_ORDER[X_ON_SCALAR], "scalar")
             for n, u in enumerate(X_ORDER):
+                if n >= EMPTY_LAG:
+                    x_out(X_ORDER[n - EMPTY_LAG])
+                if n == EARLY - 1:
+                    x_quant(0, 0)
+                if n == EARLY:
+                    a_quant(0, both)
+                    h_mm(0, 0, (2, 3, 0, 1))
+                    a_inter(1, 0, "scalar")
                 if n != X_ON_SCALAR:
                     x_widen(u)
                 x_turn(u)
@@ -327,26 +343,33 @@ def tile_dora_fp8_forward_d2_kernel(tc, x_bytes, x_scale, w_bytes, w_scale, a, l
                     nc.tensor.transpose(lam_turned[:], lam_rows[:], ident_bf[:])
                 if n == 5:
                     nc.scalar.copy(out=lam_cols[:], in_=lam_turned[:, 0:4])
-                if n >= EMPTY_LAG:
-                    x_out(X_ORDER[n - EMPTY_LAG])
-                if n in (3, 4):
-                    a_inter(0, n - 3, "scalar")
+                if n in (4, 6):
+                    a_inter(0, n // 6, "scalar")
             for u in X_ORDER[-EMPTY_LAG:]:
                 x_out(u)
 
-            x_quant(0, 0)
-            a_quant(0, both)
-            h_mm(0, 0)
-            a_inter(1, 0, "vector")
-            x_quant(1, 0)
-            h_mm(1, 0)
-            a_inter(1, 1, "vector")
             x_quant(0, 1)
-            a_quant(1, both)
-            h_mm(0, 1)
-            nc.vector.reciprocal(out=inv_norm[:], in_=norm_sb[:])
+            a_quant(1, first)
+            h_mm(0, 1, (0, 1))
+            x_quant(1, 0)
+            h_mm(1, 0, (2, 3, 0, 1))
+            a_inter(1, 1, "vector")
             x_quant(1, 1)
+            a_quant(1, second)
+            h_mm(0, 1, (2, 3))
             h_mm(1, 1)
+            a_inter(2, 1, "scalar")
+            a_inter(3, 0, "scalar")
+            a_inter(3, 1, "scalar")
+            a_inter(2, 0, "vector")
+            x_quant(0, 2)
+            a_quant(2, first)
+            x_quant(1, 2)
+            a_quant(2, second)
+            h_mm(0, 2)
+            h_mm(1, 2)
+            nc.vector.reciprocal(out=inv_norm[:], in_=norm_sb[:])
+            x_quant(0, 3)
             nc.vector.tensor_tensor(out=gain_rows[:], in0=mag_sb[:], in1=inv_norm[:], op=MULT)
             nc.sync.dma_start(out=out[0].rearrange("(p j) -> p j", p=64), in_=gain_rows[:])
             load_w(wb_later, 0, later)
@@ -355,24 +378,20 @@ def tile_dora_fp8_forward_d2_kernel(tc, x_bytes, x_scale, w_bytes, w_scale, a, l
             load_w(wb_later, 2, later)
             load_b(braw_later, later)
             load_w(wb_later, 3, later)
-            for g in (2, 3):
-                a_inter(g, 0, "scalar")
-                a_inter(g, 1, "scalar")
-                x_quant(0, g)
-                a_quant(g, both)
-                h_mm(0, g)
-                if g == 3:
-                    w_inter(0, "vector")
-                x_quant(1, g)
-                h_mm(1, g)
+            a_quant(3, first)
+            w_inter(0, "vector", slice(0, 2))
+            a_quant(3, second)
+            h_mm(0, 3)
+            x_quant(1, 3)
+            h_mm(1, 3)
 
             b_inter(0, 0, "scalar")
-            b_inter(0, 1, "scalar")
             h_out(0)
             h_out(1)
-            w_inter(1, "vector", slice(0, 2))
+            w_inter(0, "vector", slice(2, 4))
+            w_inter(1, "vector", slice(0, 1))
             w_quant(0)
-            w_inter(1, "vector", slice(2, 4))
+            w_inter(1, "vector", slice(1, 4))
             w_inter(2, "vector", slice(0, 1))
             w_quant(1)
             y_mm(0, 0, group_a)
@@ -385,51 +404,51 @@ def tile_dora_fp8_forward_d2_kernel(tc, x_bytes, x_scale, w_bytes, w_scale, a, l
             h_inter(1, 0, "scalar")
             h_inter(1, 1, "scalar")
             w_inter(2, "vector", slice(1, 4))
-            w_inter(3, "vector")
+            w_inter(3, "vector", slice(0, 1))
             w_quant(2)
+            w_inter(3, "vector", slice(1, 4))
+            b_inter(0, 1, "vector")
             w_quant(3)
             y_mm(0, 2, group_a + group_b)
             y_mm(0, 3, group_a)
-            w_inter(4, "vector")
             b_quant(0)
-            w_quant(4)
+            w_inter(4, "vector", slice(0, 2))
             h_quant(0)
             y_by_turns(0, UPDATE, 3)
-            w_inter(6, "vector", slice(0, 2))
+            w_inter(4, "vector", slice(2, 4))
+            w_inter(6, "vector", slice(0, 1))
+            w_quant(4)
             h_quant(1)
             y_mm(0, UPDATE, group_b)
+            b_later(1, hg[1])
             w_inter(5, "scalar")
 
             y_out(0, group_a + group_b)
             y_mm(1, 0, group_a + group_b)
             w_quant(5)
             y_mm(1, 1, group_a + group_b)
-            b_inter(1, 0, "scalar")
-            b_inter(1, 1, "scalar")
+            w_inter(7, "scalar")
             w_inter(9, "scalar")
-            w_inter(6, "vector", slice(2, 4))
-            w_inter(7, "vector", slice(0, 2))
+            w_inter(6, "vector", slice(1, 4))
+            b_quant(1)
             w_quant(6)
             y_mm(1, 2, group_a + group_b)
-            w_inter(7, "vector", slice(2, 4))
-            w_inter(8, "vector", slice(0, 2))
+            w_inter(8, "vector")
             w_quant(7)
             y_mm(1, 3, group_a)
-            w_inter(8, "vector", slice(2, 4))
-            b_quant(1)
             w_quant(8)
+            w_inter(11, "vector", slice(0, 2))
             w_quant(9)
             y_by_turns(1, UPDATE, 3)
             y_mm(1, UPDATE, group_b)
-            b_inter(2, 0, "scalar")
-            b_inter(2, 1, "scalar")
+            b_later(2, wg[9])
             w_inter(10, "scalar")
+            w_inter(11, "scalar", slice(2, 4))
 
             c = CHUNKS - 1
             y_out(1, group_a + group_b)
             y_mm(2, 0, group_a + group_b)
             y_mm(2, 1, group_a + group_b)
-            w_inter(11, "vector")
             b_quant(c)
             w_quant(10)
             w_quant(11)

@@ -112,8 +112,8 @@ def tile_dora_fp8_forward_d2_kernel(tc, x_bytes, x_scale, w_bytes, w_scale, a, l
             else:
                 nc.scalar.copy(out=dst, in_=src)
 
-        def fours(dst, src):
-            return dst.rearrange("p (c i) t -> p c t i", i=4), src.rearrange("p t (c i) -> p c t i", i=4)
+        def in_runs(dst, src, run=4):
+            return dst.rearrange("p (c i) t -> p c t i", i=run), src.rearrange("p t (c i) -> p c t i", i=run)
 
         def quantise(codes, scales, values):
             nc.vector.quantize_mx(out=codes.bitcast(MX), scales=scales, in_=values)
@@ -200,7 +200,7 @@ def tile_dora_fp8_forward_d2_kernel(tc, x_bytes, x_scale, w_bytes, w_scale, a, l
             if half not in hg:
                 hg[half] = staged([P, 512, 4], "hg")
             n = slice(256 * e, 256 * (e + 1))
-            copy_on(engine, *fours(hg[half][:, n, :], hb[half][:, :, n]))
+            copy_on(engine, *in_runs(hg[half][:, n, :], hb[half][:, :, n]))
 
         def h_quant(half):
             cols = slice(512 * half, 512 * (half + 1))
@@ -212,7 +212,7 @@ def tile_dora_fp8_forward_d2_kernel(tc, x_bytes, x_scale, w_bytes, w_scale, a, l
             if c not in bg:
                 bg[c] = staged([P, CW, 4], "bg")
             n = slice(256 * e, 256 * (e + 1))
-            copy_on(engine, *fours(bg[c][:, n, :], columns(braw_first, braw_later, c, n.start, n.stop)))
+            copy_on(engine, *in_runs(bg[c][:, n, :], columns(braw_first, braw_later, c, n.start, n.stop)))
 
         def b_later(c, tile):
             bg[c] = tile
@@ -232,7 +232,11 @@ def tile_dora_fp8_forward_d2_kernel(tc, x_bytes, x_scale, w_bytes, w_scale, a, l
             if v not in wg:
                 wg[v] = staged([P, CW, 4], "wg")
             for n, e in enumerate(range(blocks.start, blocks.stop)):
-                dst, src = fours(wg[v][:, 128 * e : 128 * (e + 1), :], rows[:, :, 128 * n : 128 * (n + 1)])
+                dst, src = in_runs(
+                    wg[v][:, 128 * e : 128 * (e + 1), :],
+                    rows[:, :, 128 * n : 128 * (n + 1)],
+                    8 if engine == "vector" else 4,
+                )
                 scale = ws[:, g, 4 * c + e : 4 * c + e + 1]
                 if engine == "vector":
                     nc.vector.tensor_scalar(out=dst, in0=src, scalar1=scale, scalar2=None, op0=MULT)

@@ -206,7 +206,7 @@ def tile_dora_fp8_forward_d2_kernel(tc, x_bytes, x_scale, w_bytes, w_scale, a, l
             cols = slice(512 * half, 512 * (half + 1))
             quantise(hq[:, cols], hqs[:, cols], hg[half][:].rearrange("p n t -> p (n t)"))
 
-        bg, wg = {}, {}
+        bg, cast, wg = {}, {}, {}
 
         def b_inter(c, e, engine):
             if c not in bg:
@@ -222,13 +222,17 @@ def tile_dora_fp8_forward_d2_kernel(tc, x_bytes, x_scale, w_bytes, w_scale, a, l
         def b_quant(c):
             quantise(bq[c][:], bqs[c][:], bg[c][:].rearrange("p n t -> p (n t)"))
 
+        def w_bytes_of(v, blocks):
+            c, g = divmod(v, PASSES)
+            return columns(wb_first[g], wb_later[g], c, 128 * blocks.start, 128 * blocks.stop).bitcast(E4M3)
+
+        def w_cast(v, blocks=slice(0, 4)):
+            cast[v] = staged([P, 4, 128 * (blocks.stop - blocks.start)], "cast")
+            nc.scalar.copy(out=cast[v][:], in_=w_bytes_of(v, blocks))
+
         def w_inter(v, engine, blocks=slice(0, 4)):
             c, g = divmod(v, PASSES)
-            rows = columns(wb_first[g], wb_later[g], c, 128 * blocks.start, 128 * blocks.stop).bitcast(E4M3)
-            if engine == "scalar":
-                cast = staged([P, 4, 128 * (blocks.stop - blocks.start)], "cast")
-                nc.scalar.copy(out=cast[:], in_=rows)
-                rows = cast[:]
+            rows = w_bytes_of(v, blocks) if engine == "vector" else cast[v][:]
             if v not in wg:
                 wg[v] = staged([P, CW, 4], "wg")
             for n, e in enumerate(range(blocks.start, blocks.stop)):
@@ -353,8 +357,17 @@ def tile_dora_fp8_forward_d2_kernel(tc, x_bytes, x_scale, w_bytes, w_scale, a, l
                 x_out(u)
 
             x_quant(0, 1)
+            nc.vector.reciprocal(out=inv_norm[:], in_=norm_sb[:])
             a_quant(1, first)
             h_mm(0, 1, (0, 1))
+            nc.vector.tensor_tensor(out=gain_rows[:], in0=mag_sb[:], in1=inv_norm[:], op=MULT)
+            nc.sync.dma_start(out=out[0].rearrange("(p j) -> p j", p=64), in_=gain_rows[:])
+            load_w(wb_later, 0, later)
+            load_w(wb_later, 1, later)
+            nc.sync.dma_start(out=gain[:], in_=out[0].partition_broadcast(P))
+            load_w(wb_later, 2, later)
+            load_b(braw_later, later)
+            load_w(wb_later, 3, later)
             x_quant(1, 0)
             h_mm(1, 0, (2, 3, 0, 1))
             a_inter(1, 1, "vector")
@@ -371,21 +384,14 @@ def tile_dora_fp8_forward_d2_kernel(tc, x_bytes, x_scale, w_bytes, w_scale, a, l
             x_quant(1, 2)
             a_quant(2, second)
             h_mm(0, 2)
-            h_mm(1, 2)
-            nc.vector.reciprocal(out=inv_norm[:], in_=norm_sb[:])
+            h_mm(1, 2, (0, 1))
             x_quant(0, 3)
-            nc.vector.tensor_tensor(out=gain_rows[:], in0=mag_sb[:], in1=inv_norm[:], op=MULT)
-            nc.sync.dma_start(out=out[0].rearrange("(p j) -> p j", p=64), in_=gain_rows[:])
-            load_w(wb_later, 0, later)
-            load_w(wb_later, 1, later)
-            nc.sync.dma_start(out=gain[:], in_=out[0].partition_broadcast(P))
-            load_w(wb_later, 2, later)
-            load_b(braw_later, later)
-            load_w(wb_later, 3, later)
             a_quant(3, first)
+            h_mm(0, 3, (0, 1))
+            h_mm(1, 2, (2, 3))
             w_inter(0, "vector", slice(0, 2))
             a_quant(3, second)
-            h_mm(0, 3)
+            h_mm(0, 3, (2, 3))
             x_quant(1, 3)
             h_mm(1, 3)
 
@@ -407,6 +413,7 @@ def tile_dora_fp8_forward_d2_kernel(tc, x_bytes, x_scale, w_bytes, w_scale, a, l
             h_inter(0, 1, "scalar")
             h_inter(1, 0, "scalar")
             h_inter(1, 1, "scalar")
+            w_cast(5)
             w_inter(2, "vector", slice(1, 4))
             w_inter(3, "vector", slice(0, 1))
             w_quant(2)
@@ -415,44 +422,51 @@ def tile_dora_fp8_forward_d2_kernel(tc, x_bytes, x_scale, w_bytes, w_scale, a, l
             w_quant(3)
             y_mm(0, 2, group_a + group_b)
             y_mm(0, 3, group_a)
+            w_inter(4, "vector")
             b_quant(0)
-            w_inter(4, "vector", slice(0, 2))
             h_quant(0)
             y_by_turns(0, UPDATE, 3)
-            w_inter(4, "vector", slice(2, 4))
-            w_inter(6, "vector", slice(0, 1))
             w_quant(4)
             h_quant(1)
             y_mm(0, UPDATE, group_b)
             b_later(1, hg[1])
             w_inter(5, "scalar")
 
-            y_out(0, group_a + group_b)
-            y_mm(1, 0, group_a + group_b)
+            y_out(0, range(7))
+            y_mm(1, 0, range(7))
             w_quant(5)
-            y_mm(1, 1, group_a + group_b)
-            w_inter(7, "scalar")
+            y_mm(1, 1, group_a)
+            y_out(0, [7])
+            y_mm(1, 0, [7])
+            y_mm(1, 1, group_b)
+            w_cast(6, slice(2, 4))
+            w_cast(9)
+            w_inter(6, "scalar", slice(2, 4))
+            w_cast(10)
             w_inter(9, "scalar")
-            w_inter(6, "vector", slice(1, 4))
+            w_inter(6, "vector", slice(0, 2))
             b_quant(1)
             w_quant(6)
             y_mm(1, 2, group_a + group_b)
-            w_inter(8, "vector")
+            w_inter(7, "vector")
+            w_inter(8, "vector", slice(0, 1))
             w_quant(7)
             y_mm(1, 3, group_a)
-            w_quant(8)
-            w_inter(11, "vector", slice(0, 2))
+            w_inter(8, "vector", slice(1, 4))
             w_quant(9)
+            w_quant(8)
             y_by_turns(1, UPDATE, 3)
             y_mm(1, UPDATE, group_b)
-            b_later(2, wg[9])
+            b_later(2, wg[8])
+            w_cast(11)
             w_inter(10, "scalar")
-            w_inter(11, "scalar", slice(2, 4))
+            w_inter(11, "scalar")
 
             c = CHUNKS - 1
             y_out(1, group_a + group_b)
-            y_mm(2, 0, group_a + group_b)
-            y_mm(2, 1, group_a + group_b)
+            for group in (group_a, group_b):
+                y_mm(2, 0, group)
+                y_mm(2, 1, group)
             b_quant(c)
             w_quant(10)
             w_quant(11)

@@ -66,7 +66,7 @@ def tile_dora_fp8_forward_d2_kernel(tc, x_bytes, x_scale, w_bytes, w_scale, a, l
         xb = [big.tile([P, 4, K // 2], U8, name=f"xb{n}", tag="big", align_bytes=256) for n in range(4)]
         araw = [big.tile([P, 4, R], BF16, name=f"araw{g}", tag="big", align_bytes=256) for g in range(PASSES)]
         wb_first = [kept([P, 4, CW], U8, f"wb_first{g}") for g in range(PASSES)]
-        wb_later = [kept([P, 4, N - CW], U8, f"wb_later{g}") for g in range(PASSES)]
+        wb_later = [kept([P, CHUNKS - 1, 4, CW], U8, f"wb_later{g}") for g in range(PASSES)]
         braw_first = kept([P, 4, CW], BF16, "braw_first")
         braw_later = kept([P, 4, N - CW], BF16, "braw_later")
         xq = kept([P, 2, PASSES, 512], U32, "xq")
@@ -98,6 +98,10 @@ def tile_dora_fp8_forward_d2_kernel(tc, x_bytes, x_scale, w_bytes, w_scale, a, l
 
         def load_w(tiles, g, cols):
             nc.sync.dma_start(out=tiles[g][:], in_=w_view[g][:, :, cols])
+
+        def load_w_later(g):
+            for c in range(1, CHUNKS):
+                nc.sync.dma_start(out=wb_later[g][:, c - 1], in_=w_view[g][:, :, CW * c : CW * (c + 1)])
 
         def load_b(tile, cols):
             for t in range(4):
@@ -222,25 +226,23 @@ def tile_dora_fp8_forward_d2_kernel(tc, x_bytes, x_scale, w_bytes, w_scale, a, l
         def b_quant(c):
             quantise(bq[c][:], bqs[c][:], bg[c][:].rearrange("p n t -> p (n t)"))
 
-        def w_bytes_of(v, blocks):
+        def w_cast(v, own=True):
             c, g = divmod(v, PASSES)
-            return columns(wb_first[g], wb_later[g], c, 128 * blocks.start, 128 * blocks.stop).bitcast(E4M3)
-
-        def w_cast(v, blocks=slice(0, 4)):
-            cast[v] = staged([P, 4, 128 * (blocks.stop - blocks.start)], "cast")
-            nc.scalar.copy(out=cast[v][:], in_=w_bytes_of(v, blocks))
+            if own:
+                cast[v] = staged([P, 4, CW], "cast")
+            else:
+                cast[v] = big.tile([P, 4, CW], BF16, name="cast_v", tag="big", align_bytes=256)
+            codes = wb_first[g][:] if c == 0 else wb_later[g][:, c - 1]
+            nc.scalar.copy(
+                out=cast[v][:].rearrange("p t n -> p (t n)"), in_=codes.rearrange("p t n -> p (t n)").bitcast(E4M3)
+            )
 
         def w_inter(v, engine, blocks=slice(0, 4)):
             c, g = divmod(v, PASSES)
-            rows = w_bytes_of(v, blocks) if engine == "vector" else cast[v][:]
             if v not in wg:
                 wg[v] = staged([P, CW, 4], "wg")
-            for n, e in enumerate(range(blocks.start, blocks.stop)):
-                dst, src = in_runs(
-                    wg[v][:, 128 * e : 128 * (e + 1), :],
-                    rows[:, :, 128 * n : 128 * (n + 1)],
-                    8 if engine == "vector" else 4,
-                )
+            for e in range(blocks.start, blocks.stop):
+                dst, src = in_runs(wg[v][:, 128 * e : 128 * (e + 1), :], cast[v][:, :, 128 * e : 128 * (e + 1)])
                 scale = ws[:, g, 4 * c + e : 4 * c + e + 1]
                 if engine == "vector":
                     nc.vector.tensor_scalar(out=dst, in0=src, scalar1=scale, scalar2=None, op0=MULT)
@@ -362,12 +364,12 @@ def tile_dora_fp8_forward_d2_kernel(tc, x_bytes, x_scale, w_bytes, w_scale, a, l
             h_mm(0, 1, (0, 1))
             nc.vector.tensor_tensor(out=gain_rows[:], in0=mag_sb[:], in1=inv_norm[:], op=MULT)
             nc.sync.dma_start(out=out[0].rearrange("(p j) -> p j", p=64), in_=gain_rows[:])
-            load_w(wb_later, 0, later)
-            load_w(wb_later, 1, later)
+            load_w_later(0)
+            load_w_later(1)
             nc.sync.dma_start(out=gain[:], in_=out[0].partition_broadcast(P))
-            load_w(wb_later, 2, later)
+            load_w_later(2)
             load_b(braw_later, later)
-            load_w(wb_later, 3, later)
+            load_w_later(3)
             x_quant(1, 0)
             h_mm(1, 0, (2, 3, 0, 1))
             a_inter(1, 1, "vector")
@@ -378,6 +380,8 @@ def tile_dora_fp8_forward_d2_kernel(tc, x_bytes, x_scale, w_bytes, w_scale, a, l
             a_inter(2, 1, "scalar")
             a_inter(3, 0, "scalar")
             a_inter(3, 1, "scalar")
+            w_cast(0, False)
+            w_cast(1, False)
             a_inter(2, 0, "vector")
             x_quant(0, 2)
             a_quant(2, first)
@@ -397,8 +401,10 @@ def tile_dora_fp8_forward_d2_kernel(tc, x_bytes, x_scale, w_bytes, w_scale, a, l
 
             b_inter(0, 0, "scalar")
             h_out(0)
+            w_cast(2, False)
             h_out(1)
             w_inter(0, "vector", slice(2, 4))
+            w_cast(3, False)
             w_inter(1, "vector", slice(0, 1))
             w_quant(0)
             w_inter(1, "vector", slice(1, 4))
@@ -411,6 +417,7 @@ def tile_dora_fp8_forward_d2_kernel(tc, x_bytes, x_scale, w_bytes, w_scale, a, l
             y_mm(0, 1, group_b)
             h_inter(0, 0, "scalar")
             h_inter(0, 1, "scalar")
+            w_cast(4, False)
             h_inter(1, 0, "scalar")
             h_inter(1, 1, "scalar")
             w_cast(5)
@@ -439,9 +446,11 @@ def tile_dora_fp8_forward_d2_kernel(tc, x_bytes, x_scale, w_bytes, w_scale, a, l
             y_out(0, [7])
             y_mm(1, 0, [7])
             y_mm(1, 1, group_b)
-            w_cast(6, slice(2, 4))
+            w_cast(6)
+            w_cast(7, False)
             w_cast(9)
             w_inter(6, "scalar", slice(2, 4))
+            w_cast(8, False)
             w_cast(10)
             w_inter(9, "scalar")
             w_inter(6, "vector", slice(0, 2))

@@ -28,26 +28,28 @@ X_UNITS = 4 * PASSES
 W_UNITS = CHUNKS * PASSES
 
 X_ORDER = [4 * (n // 2) + n % 2 + 2 * k for n in range(4) for k in range(2)] + list(range(8, X_UNITS))
-X_ON_SCALAR = 1
-X_BANKS = list(range(8)) + [0, 1] + [4, 5, 6, 7, 4, 5]
-EARLY = 13
-EMPTY_LAG = 3
+RING = 28
+LAST_PASSES = (UPDATE, 2, 3)
+H_BANK = (0, 4)
+Y_BANK = (0, 4)
 
 
 def tile_dora_fp8_forward_d2_kernel(tc, x_bytes, x_scale, w_bytes, w_scale, a, lam, b, mag, norm, out):
     nc = tc.nc
     with ExitStack() as ctx:
         keep = ctx.enter_context(tc.tile_pool(name="keep", bufs=1))
-        big = ctx.enter_context(tc.tile_pool(name="big", bufs=14))
-        widened = ctx.enter_context(tc.tile_pool(name="widened", bufs=6))
-        stage = ctx.enter_context(tc.tile_pool(name="stage", bufs=13))
+        ring = ctx.enter_context(tc.tile_pool(name="ring", bufs=1))
+        widened = ctx.enter_context(tc.tile_pool(name="widened", bufs=8))
         psum = ctx.enter_context(tc.psum_pool(name="psum", bufs=1))
 
         def kept(shape, dtype, name):
-            return keep.tile(shape, dtype, name=name, align_bytes=256)
+            return keep.tile(shape, dtype, name=name, align_bytes=64)
 
-        def staged(shape, name):
-            return stage.tile(shape, BF16, name=name, tag="stage", align_bytes=256)
+        taken = []
+
+        def staged(shape, name, dtype=BF16):
+            taken.append(name)
+            return ring.tile(shape, dtype, name=name, tag=f"slot{len(taken) % RING}", align_bytes=64)
 
         def bank(n, shape, dtype=F32):
             return psum.tile(shape, dtype, name=f"bank{n}", tag=f"bank{n}")
@@ -63,8 +65,8 @@ def tile_dora_fp8_forward_d2_kernel(tc, x_bytes, x_scale, w_bytes, w_scale, a, l
         inv_norm = kept([64, N // 64], F32, "inv_norm")
         gain_rows = kept([64, N // 64], F32, "gain_rows")
         gain = kept([P, N], F32, "gain")
-        xb = [big.tile([P, 4, K // 2], U8, name=f"xb{n}", tag="big", align_bytes=256) for n in range(4)]
-        araw = [big.tile([P, 4, R], BF16, name=f"araw{g}", tag="big", align_bytes=256) for g in range(PASSES)]
+        xb = [staged([P, 4, K // 2], f"xb{n}", U8) for n in range(4)]
+        araw = [staged([P, 4, R], f"araw{g}") for g in range(PASSES)]
         wb_first = [kept([P, 4, CW], U8, f"wb_first{g}") for g in range(PASSES)]
         wb_later = [kept([P, CHUNKS - 1, 4, CW], U8, f"wb_later{g}") for g in range(PASSES)]
         braw_first = kept([P, 4, CW], BF16, "braw_first")
@@ -93,8 +95,8 @@ def tile_dora_fp8_forward_d2_kernel(tc, x_bytes, x_scale, w_bytes, w_scale, a, l
             rows = slice(4 * half + tiles.start, 4 * half + tiles.stop)
             nc.sync.dma_start(out=xb[n][:, tiles, :], in_=x_view[:, rows, k : k + K // 2])
 
-        def load_a(g):
-            nc.sync.dma_start(out=araw[g][:], in_=a_view[g])
+        def load_a(g, ranks=slice(0, R)):
+            nc.sync.dma_start(out=araw[g][:, :, ranks], in_=a_view[g][:, :, ranks])
 
         def load_w(tiles, g, cols):
             nc.sync.dma_start(out=tiles[g][:], in_=w_view[g][:, :, cols])
@@ -127,7 +129,7 @@ def tile_dora_fp8_forward_d2_kernel(tc, x_bytes, x_scale, w_bytes, w_scale, a, l
         def x_widen(u, engine="vector"):
             half, g, j = u // 8, u % 8 // 2, u % 2
             in_order[u] = engine == "scalar"
-            xw[u] = widened.tile([P, 2, 512], BF16, name="xw", align_bytes=256)
+            xw[u] = widened.tile([P, 2, 512], BF16, name="xw", align_bytes=64)
             for i in range(2):
                 runs = xw[u][:, i, :].rearrange("p (h m e) -> p m h e", h=2, e=2)
                 for q in range(4):
@@ -143,8 +145,8 @@ def tile_dora_fp8_forward_d2_kernel(tc, x_bytes, x_scale, w_bytes, w_scale, a, l
                             out=runs[:, 32 * q : 32 * (q + 1), :, :], in0=codes, scalar1=scale, scalar2=None, op0=MULT
                         )
 
-        def x_turn(u):
-            xbank[u] = bank(X_BANKS[X_ORDER.index(u)], [P, 2, 2, P])
+        def x_turn(u, n):
+            xbank[u] = bank(n, [P, 2, 2, P])
             for i in range(2):
                 words = xw[u][:, i, :].bitcast(F32)
                 for h in range(2):
@@ -164,7 +166,22 @@ def tile_dora_fp8_forward_d2_kernel(tc, x_bytes, x_scale, w_bytes, w_scale, a, l
             d = PASSES * half + g
             quantise(xq[:, half, g, :], xqs[:, half, g, :], xg[d][:].rearrange("p j i r t -> p (j i r t)"))
 
-        ag, hbank, hb, hg = {}, {}, {}, {}
+        abank, ag, hbank, hb, hg = {}, {}, {}, {}, {}
+
+        def a_turn(g, e, n):
+            abank[g, e] = bank(n, [P, 2, 512], BF16)
+            for k in range(2):
+                r = 256 * e + 128 * k
+                src = araw[g][:, :, r : r + 128].rearrange("p j r -> p r j")
+                nc.tensor.matmul(abank[g, e][:, k, :], lhsT=ident_bf[:], rhs=src, start=True, stop=True)
+
+        def a_out(g, e):
+            if g not in ag:
+                ag[g] = staged([P, 4, P, 4], "ag")
+            nc.scalar.copy(
+                out=ag[g][:].rearrange("p t (q i) j -> p q t (i j)", i=8)[:, 8 * e : 8 * (e + 1)],
+                in_=abank[g, e][:].rearrange("p k (q t w) -> p (k q) t w", t=4, w=32),
+            )
 
         def a_inter(g, e, engine):
             if g not in ag:
@@ -182,7 +199,7 @@ def tile_dora_fp8_forward_d2_kernel(tc, x_bytes, x_scale, w_bytes, w_scale, a, l
         def h_mm(half, g, ts=range(4)):
             for t in ts:
                 if g == 0:
-                    hbank[half, t] = bank(4 * half + t, [P, 512])
+                    hbank[half, t] = bank(H_BANK[half] + t, [P, 512])
                 nc.tensor.matmul_mx(
                     out=hbank[half, t][:],
                     lhsT=aq[:, g, P * t : P * (t + 1)].bitcast(MX),
@@ -193,9 +210,10 @@ def tile_dora_fp8_forward_d2_kernel(tc, x_bytes, x_scale, w_bytes, w_scale, a, l
                     stop=(g == PASSES - 1),
                 )
 
-        def h_out(half):
-            hb[half] = staged([P, 4, 512], "hb")
-            for t in range(4):
+        def h_out(half, ts=range(4)):
+            if half not in hb:
+                hb[half] = staged([P, 4, 512], "hb")
+            for t in ts:
                 nc.scalar.activation(
                     out=hb[half][:, t, :], in_=hbank[half, t][:], func=COPY, scale=lam_cols[:, t : t + 1]
                 )
@@ -226,12 +244,9 @@ def tile_dora_fp8_forward_d2_kernel(tc, x_bytes, x_scale, w_bytes, w_scale, a, l
         def b_quant(c):
             quantise(bq[c][:], bqs[c][:], bg[c][:].rearrange("p n t -> p (n t)"))
 
-        def w_cast(v, own=True):
+        def w_cast(v):
             c, g = divmod(v, PASSES)
-            if own:
-                cast[v] = staged([P, 4, CW], "cast")
-            else:
-                cast[v] = big.tile([P, 4, CW], BF16, name="cast_v", tag="big", align_bytes=256)
+            cast[v] = staged([P, 4, CW], "cast")
             codes = wb_first[g][:] if c == 0 else wb_later[g][:, c - 1]
             nc.scalar.copy(
                 out=cast[v][:].rearrange("p t n -> p (t n)"), in_=codes.rearrange("p t n -> p (t n)").bitcast(E4M3)
@@ -250,8 +265,8 @@ def tile_dora_fp8_forward_d2_kernel(tc, x_bytes, x_scale, w_bytes, w_scale, a, l
                     nc.scalar.activation(out=dst, in_=src, func=COPY, scale=scale)
 
         def w_quant(v):
-            wq[v] = keep.tile([P, CW], U32, name=f"wq{v}", tag="wq", bufs=2 * PASSES, align_bytes=256)
-            wqs[v] = keep.tile([P, CW], U8, name=f"wqs{v}", tag="wqs", bufs=2 * PASSES, align_bytes=256)
+            wq[v] = keep.tile([P, CW], U32, name=f"wq{v}", tag="wq", bufs=2 * PASSES, align_bytes=64)
+            wqs[v] = keep.tile([P, CW], U8, name=f"wqs{v}", tag="wqs", bufs=2 * PASSES, align_bytes=64)
             quantise(wq[v][:], wqs[v][:], wg[v][:].rearrange("p n t -> p (n t)"))
 
         acc, done, res = {}, {}, {}
@@ -281,11 +296,11 @@ def tile_dora_fp8_forward_d2_kernel(tc, x_bytes, x_scale, w_bytes, w_scale, a, l
 
         def y_mm(c, g, tiles):
             for i in tiles:
-                y_pass(c, g, i, LAST_PARTS[0] if (c, i) == (CHUNKS - 1, TILES - 1) else WHOLE, i)
+                y_pass(c, g, i, LAST_PARTS[0] if (c, i) == (CHUNKS - 1, TILES - 1) else WHOLE, Y_BANK[i // 4] + i % 4)
 
         def y_scale(c, i, part):
             if (c, i // 2) not in res:
-                res[c, i // 2] = big.tile([P, 2, CW], F32, name="res", tag="big", align_bytes=256)
+                res[c, i // 2] = staged([P, 2, CW], "res", F32)
             cols = slice(CW * c + part.start, CW * c + part.stop)
             nc.vector.tensor_tensor(
                 out=res[c, i // 2][:, i % 2, part], in0=acc[c, i, part.start][:], in1=gain[:, cols], op=MULT
@@ -318,50 +333,95 @@ def tile_dora_fp8_forward_d2_kernel(tc, x_bytes, x_scale, w_bytes, w_scale, a, l
             )
             nc.scalar.activation(out=ident_bf[:], in_=ident[:], func=COPY)
             load_x(1, slice(0, 2))
-            load_a(0)
             load_x(1, slice(2, 4))
-            load_x(2, slice(0, 4))
-            load_x(3, slice(0, 4))
+            load_a(0)
+            load_x(2, slice(0, 2))
             load_a(1)
+            load_x(2, slice(2, 4))
+            load_a(2)
+            load_x(3, slice(0, 4))
+            load_a(3)
             nc.sync.dma_start(out=norm_sb[:], in_=norm.rearrange("(p j) -> p j", p=64))
             nc.sync.dma_start(out=mag_sb[:], in_=mag.rearrange("(p j) -> p j", p=64))
-            load_a(2)
-            load_a(3)
             load_w(wb_first, 0, WHOLE)
             ws_view = w_scale.rearrange("(g q) n -> q g n", q=4)
             for q in range(4):
                 nc.sync.dma_start(out=ws[32 * q : 32 * (q + 1), :, 0 : N // 128], in_=ws_view[q].partition_broadcast(32))
-            load_b(braw_first, WHOLE)
             for g in range(1, PASSES):
                 load_w(wb_first, g, WHOLE)
+            load_b(braw_first, WHOLE)
 
-            x_widen(X_ORDER[X_ON_SCALAR], "scalar")
-            for n, u in enumerate(X_ORDER):
-                if n >= EMPTY_LAG:
-                    x_out(X_ORDER[n - EMPTY_LAG])
-                if n == EARLY - 1:
-                    x_quant(0, 0)
-                if n == EARLY:
-                    a_quant(0, both)
-                    h_mm(0, 0, (2, 3, 0, 1))
-                    a_inter(1, 0, "scalar")
-                if n != X_ON_SCALAR:
-                    x_widen(u)
-                x_turn(u)
-                if n == 4:
-                    lam_turned = bank(7, [P, P], BF16)
-                    nc.tensor.transpose(lam_turned[:], lam_rows[:], ident_bf[:])
-                if n == 5:
-                    nc.scalar.copy(out=lam_cols[:], in_=lam_turned[:, 0:4])
-                if n in (4, 6):
-                    a_inter(0, n // 6, "scalar")
-            for u in X_ORDER[-EMPTY_LAG:]:
-                x_out(u)
-
+            x_widen(2, "scalar")
+            x_widen(3, "scalar")
+            x_widen(0)
+            x_turn(0, 0)
+            x_out(0)
+            x_widen(1)
+            x_turn(1, 1)
+            x_turn(2, 2)
+            x_turn(3, 3)
+            x_out(1)
+            x_out(2)
+            x_widen(4)
+            x_turn(4, 4)
+            x_widen(6)
+            x_turn(6, 5)
+            x_widen(5)
+            x_turn(5, 6)
+            x_widen(7)
+            x_turn(7, 7)
+            a_turn(1, 0, 0)
+            a_turn(1, 1, 1)
+            lam_turned = bank(2, [P, P], BF16)
+            nc.tensor.transpose(lam_turned[:], lam_rows[:], ident_bf[:])
+            x_widen(8)
+            x_widen(10)
+            x_quant(0, 0)
+            x_widen(9)
+            x_widen(11)
+            a_inter(0, 0, "scalar")
+            x_out(3)
+            x_turn(8, 3)
+            x_out(4)
+            x_turn(10, 4)
+            a_inter(0, 1, "scalar")
+            x_out(6)
+            x_turn(9, 5)
+            x_out(5)
+            a_turn(2, 0, 6)
+            x_out(7)
+            a_turn(2, 1, 7)
+            a_out(1, 0)
+            a_out(1, 1)
+            nc.scalar.copy(out=lam_cols[:], in_=lam_turned[:, 0:4])
+            x_out(8)
+            x_out(10)
+            x_out(9)
+            a_out(2, 0)
+            a_out(2, 1)
+            a_quant(0, both)
+            h_mm(0, 0)
+            x_turn(11, 4)
+            x_out(11)
+            x_widen(12)
+            x_turn(12, 5)
+            x_out(12)
             x_quant(0, 1)
+            x_widen(14)
+            a_quant(1, both)
+            h_mm(0, 1)
+            x_turn(14, 6)
+            x_widen(13)
+            x_turn(13, 7)
+            x_quant(0, 2)
+            x_widen(15)
+            x_turn(15, 4)
+            a_inter(3, 0, "vector")
+            a_quant(2, both)
+            h_mm(0, 2)
+            x_quant(1, 0)
             nc.vector.reciprocal(out=inv_norm[:], in_=norm_sb[:])
-            a_quant(1, first)
-            h_mm(0, 1, (0, 1))
+            x_quant(0, 3)
             nc.vector.tensor_tensor(out=gain_rows[:], in0=mag_sb[:], in1=inv_norm[:], op=MULT)
             nc.sync.dma_start(out=out[0].rearrange("(p j) -> p j", p=64), in_=gain_rows[:])
             load_w_later(0)
@@ -370,118 +430,121 @@ def tile_dora_fp8_forward_d2_kernel(tc, x_bytes, x_scale, w_bytes, w_scale, a, l
             load_w_later(2)
             load_b(braw_later, later)
             load_w_later(3)
-            x_quant(1, 0)
-            h_mm(1, 0, (2, 3, 0, 1))
-            a_inter(1, 1, "vector")
-            x_quant(1, 1)
-            a_quant(1, second)
-            h_mm(0, 1, (2, 3))
-            h_mm(1, 1)
-            a_inter(2, 1, "scalar")
-            a_inter(3, 0, "scalar")
             a_inter(3, 1, "scalar")
-            w_cast(0, False)
-            w_cast(1, False)
-            a_inter(2, 0, "vector")
-            x_quant(0, 2)
-            a_quant(2, first)
+            x_out(14)
+            x_out(13)
+            x_out(15)
+            h_mm(1, 0, (1, 2, 3, 0))
+            a_quant(3, both)
+            h_mm(0, 3)
+            x_quant(1, 1)
+            h_mm(1, 1)
             x_quant(1, 2)
-            a_quant(2, second)
-            h_mm(0, 2)
-            h_mm(1, 2, (0, 1))
-            x_quant(0, 3)
-            a_quant(3, first)
-            h_mm(0, 3, (0, 1))
-            h_mm(1, 2, (2, 3))
+            h_mm(1, 2)
+            w_cast(0)
             w_inter(0, "vector", slice(0, 2))
-            a_quant(3, second)
-            h_mm(0, 3, (2, 3))
             x_quant(1, 3)
             h_mm(1, 3)
-
-            b_inter(0, 0, "scalar")
-            h_out(0)
-            w_cast(2, False)
-            h_out(1)
             w_inter(0, "vector", slice(2, 4))
-            w_cast(3, False)
+            w_cast(1)
             w_inter(1, "vector", slice(0, 1))
             w_quant(0)
             w_inter(1, "vector", slice(1, 4))
-            w_inter(2, "vector", slice(0, 1))
+            b_inter(0, 0, "vector")
             w_quant(1)
+            h_out(0)
             y_mm(0, 0, group_a)
-            for i, j in zip(group_a, group_b):
-                y_mm(0, 0, [j])
-                y_mm(0, 1, [i])
-            y_mm(0, 1, group_b)
-            h_inter(0, 0, "scalar")
-            h_inter(0, 1, "scalar")
-            w_cast(4, False)
-            h_inter(1, 0, "scalar")
-            h_inter(1, 1, "scalar")
-            w_cast(5)
-            w_inter(2, "vector", slice(1, 4))
-            w_inter(3, "vector", slice(0, 1))
-            w_quant(2)
-            w_inter(3, "vector", slice(1, 4))
+            y_mm(0, 1, [0])
+            w_cast(2)
+            w_inter(2, "vector")
             b_inter(0, 1, "vector")
+            w_quant(2)
+            h_out(1, (0, 1))
+            y_mm(0, 0, [4])
+            y_mm(0, 1, [1])
+            y_mm(0, 0, [5])
+            y_mm(0, 1, [2])
+            w_cast(3)
+            w_inter(3, "vector")
+            b_quant(0)
             w_quant(3)
+            h_out(1, (2, 3))
+            y_mm(0, 0, [6])
+            y_mm(0, 1, [3])
+            y_mm(0, 0, [7])
+            y_mm(0, 1, group_b)
             y_mm(0, 2, group_a + group_b)
             y_mm(0, 3, group_a)
-            w_inter(4, "vector")
-            b_quant(0)
+            h_inter(1, 0, "vector")
+            h_inter(0, 0, "scalar")
+            h_inter(0, 1, "scalar")
             h_quant(0)
-            y_by_turns(0, UPDATE, 3)
-            w_quant(4)
+            y_mm(0, UPDATE, [0])
+            y_mm(0, 3, [4])
+            y_mm(0, UPDATE, [1])
+            y_mm(0, 3, [5])
+            y_mm(0, UPDATE, [2])
+            y_mm(0, 3, [6])
+            y_mm(0, UPDATE, [3])
+            y_mm(0, 3, [7])
+            w_cast(4)
+            w_inter(4, "vector")
+            h_inter(1, 1, "scalar")
             h_quant(1)
             y_mm(0, UPDATE, group_b)
-            b_later(1, hg[1])
+            w_quant(4)
+            b_later(1, wg[4])
+            y_out(0, [0, 1, 2, 3, 4, 5, 6])
+            y_mm(1, 0, [0, 1, 2, 3, 4, 5, 6])
+            w_cast(5)
+            w_cast(6)
             w_inter(5, "scalar")
-
-            y_out(0, range(7))
-            y_mm(1, 0, range(7))
             w_quant(5)
             y_mm(1, 1, group_a)
             y_out(0, [7])
             y_mm(1, 0, [7])
             y_mm(1, 1, group_b)
-            w_cast(6)
-            w_cast(7, False)
-            w_cast(9)
-            w_inter(6, "scalar", slice(2, 4))
-            w_cast(8, False)
-            w_cast(10)
-            w_inter(9, "scalar")
-            w_inter(6, "vector", slice(0, 2))
+            w_inter(6, "vector")
             b_quant(1)
             w_quant(6)
             y_mm(1, 2, group_a + group_b)
+            w_cast(7)
             w_inter(7, "vector")
+            w_cast(8)
             w_inter(8, "vector", slice(0, 1))
             w_quant(7)
             y_mm(1, 3, group_a)
+            y_mm(1, UPDATE, [0])
+            y_mm(1, 3, [4])
+            y_mm(1, UPDATE, [1])
+            y_mm(1, 3, [5])
+            y_mm(1, UPDATE, [2])
+            y_mm(1, 3, [6])
+            y_mm(1, UPDATE, [3])
+            y_mm(1, 3, [7])
+            y_mm(1, UPDATE, group_b)
             w_inter(8, "vector", slice(1, 4))
+            w_cast(9)
+            w_cast(10)
+            w_inter(9, "scalar")
             w_quant(9)
             w_quant(8)
-            y_by_turns(1, UPDATE, 3)
-            y_mm(1, UPDATE, group_b)
             b_later(2, wg[8])
+            y_out(1, [0, 1, 2, 3, 4, 5, 6, 7])
+            y_mm(2, 0, group_a)
+            y_mm(2, 1, group_a)
+            y_mm(2, 0, group_b)
+            y_mm(2, 1, group_b)
+            b_quant(2)
             w_cast(11)
             w_inter(10, "scalar")
-            w_inter(11, "scalar")
-
-            c = CHUNKS - 1
-            y_out(1, group_a + group_b)
-            for group in (group_a, group_b):
-                y_mm(2, 0, group)
-                y_mm(2, 1, group)
-            b_quant(c)
             w_quant(10)
+            w_inter(11, "scalar")
             w_quant(11)
-            pieces = [(i, WHOLE, i, (UPDATE, 2, 3)) for i in range(TILES - 1)]
-            pieces.append((TILES - 1, LAST_PARTS[0], TILES - 1, (UPDATE, 2, 3)))
-            pieces.extend((TILES - 1, part, n, range(PASSES + 1)) for n, part in enumerate(LAST_PARTS[1:]))
+            c = CHUNKS - 1
+            pieces = [(i, WHOLE, Y_BANK[i // 4] + i % 4, LAST_PASSES) for i in range(TILES - 1)]
+            pieces.append((TILES - 1, LAST_PARTS[0], Y_BANK[1] + 3, LAST_PASSES))
+            pieces.extend((TILES - 1, part, Y_BANK[0] + n, range(PASSES + 1)) for n, part in enumerate(LAST_PARTS[1:]))
             for i, part, n, passes in pieces:
                 for g in passes:
                     y_pass(c, g, i, part, n)

@@ -231,18 +231,18 @@ def tile_dora_fp8_forward_d2_kernel(tc, x_bytes, x_scale, w_bytes, w_scale, a, l
         bg, cast, wg = {}, {}, {}
 
         def b_inter(c, e, engine):
-            if c not in bg:
-                bg[c] = staged([P, CW, 4], "bg")
+            if (c, 0) not in bg:
+                bg[c, 0] = staged([P, CW, 4], "bg")
             n = slice(256 * e, 256 * (e + 1))
-            copy_on(engine, *in_runs(bg[c][:, n, :], columns(braw_first, braw_later, c, n.start, n.stop)))
+            copy_on(engine, *in_runs(bg[c, 0][:, n, :], columns(braw_first, braw_later, c, n.start, n.stop)))
 
-        def b_later(c, tile):
-            bg[c] = tile
-            src = columns(braw_first, braw_later, c, 0, CW).rearrange("p t n -> p n t")
-            nc.gpsimd.tensor_scalar(out=tile[:], in0=src, scalar1=1.0, scalar2=0.0, op0=MULT, op1=ADD)
+        def b_later(c, tile, n=WHOLE):
+            bg[c, n.start] = tile
+            src = columns(braw_first, braw_later, c, n.start, n.stop).rearrange("p t n -> p n t")
+            nc.gpsimd.tensor_scalar(out=tile[:, n, :], in0=src, scalar1=1.0, scalar2=0.0, op0=MULT, op1=ADD)
 
-        def b_quant(c):
-            quantise(bq[c][:], bqs[c][:], bg[c][:].rearrange("p n t -> p (n t)"))
+        def b_quant(c, n=WHOLE):
+            quantise(bq[c][:, n], bqs[c][:, n], bg[c, n.start][:, n, :].rearrange("p n t -> p (n t)"))
 
         def w_cast(v):
             c, g = divmod(v, PASSES)
@@ -333,8 +333,8 @@ def tile_dora_fp8_forward_d2_kernel(tc, x_bytes, x_scale, w_bytes, w_scale, a, l
             )
             nc.scalar.activation(out=ident_bf[:], in_=ident[:], func=COPY)
             load_x(1, slice(0, 2))
-            load_x(1, slice(2, 4))
             load_a(0)
+            load_x(1, slice(2, 4))
             load_x(2, slice(0, 2))
             load_a(1)
             load_x(2, slice(2, 4))
@@ -352,16 +352,16 @@ def tile_dora_fp8_forward_d2_kernel(tc, x_bytes, x_scale, w_bytes, w_scale, a, l
             load_b(braw_first, WHOLE)
 
             x_widen(2, "scalar")
-            x_widen(3, "scalar")
             x_widen(0)
             x_turn(0, 0)
+            x_turn(2, 1)
             x_out(0)
-            x_widen(1)
-            x_turn(1, 1)
-            x_turn(2, 2)
-            x_turn(3, 3)
-            x_out(1)
             x_out(2)
+            x_widen(1)
+            x_turn(1, 2)
+            x_out(1)
+            x_widen(3)
+            x_turn(3, 3)
             x_widen(4)
             x_turn(4, 4)
             x_widen(6)
@@ -378,50 +378,55 @@ def tile_dora_fp8_forward_d2_kernel(tc, x_bytes, x_scale, w_bytes, w_scale, a, l
             x_widen(10)
             x_quant(0, 0)
             x_widen(9)
-            x_widen(11)
             a_inter(0, 0, "scalar")
             x_out(3)
             x_turn(8, 3)
+            a_inter(0, 1, "scalar")
             x_out(4)
             x_turn(10, 4)
-            a_inter(0, 1, "scalar")
             x_out(6)
             x_turn(9, 5)
             x_out(5)
-            a_turn(2, 0, 6)
             x_out(7)
-            a_turn(2, 1, 7)
             a_out(1, 0)
             a_out(1, 1)
             nc.scalar.copy(out=lam_cols[:], in_=lam_turned[:, 0:4])
             x_out(8)
             x_out(10)
-            x_out(9)
-            a_out(2, 0)
-            a_out(2, 1)
             a_quant(0, both)
+            x_widen(11)
+            x_turn(11, 6)
             h_mm(0, 0)
-            x_turn(11, 4)
-            x_out(11)
             x_widen(12)
-            x_turn(12, 5)
-            x_out(12)
+            x_turn(12, 7)
             x_quant(0, 1)
             x_widen(14)
+            x_turn(14, 4)
             a_quant(1, both)
             h_mm(0, 1)
-            x_turn(14, 6)
+            a_inter(2, 1, "vector")
             x_widen(13)
-            x_turn(13, 7)
             x_quant(0, 2)
             x_widen(15)
-            x_turn(15, 4)
-            a_inter(3, 0, "vector")
+            a_inter(2, 0, "scalar")
+            x_out(9)
+            x_turn(13, 5)
+            x_out(11)
+            x_turn(15, 6)
+            x_out(12)
+            x_out(14)
+            x_out(13)
+            x_out(15)
             a_quant(2, both)
             h_mm(0, 2)
+            a_inter(3, 0, "vector")
             x_quant(1, 0)
+            h_mm(1, 0, (3, 0, 1, 2))
+            a_inter(3, 1, "vector")
+            x_quant(1, 1)
+            h_mm(1, 1)
             nc.vector.reciprocal(out=inv_norm[:], in_=norm_sb[:])
-            x_quant(0, 3)
+            a_quant(3, both)
             nc.vector.tensor_tensor(out=gain_rows[:], in0=mag_sb[:], in1=inv_norm[:], op=MULT)
             nc.sync.dma_start(out=out[0].rearrange("(p j) -> p j", p=64), in_=gain_rows[:])
             load_w_later(0)
@@ -430,15 +435,8 @@ def tile_dora_fp8_forward_d2_kernel(tc, x_bytes, x_scale, w_bytes, w_scale, a, l
             load_w_later(2)
             load_b(braw_later, later)
             load_w_later(3)
-            a_inter(3, 1, "scalar")
-            x_out(14)
-            x_out(13)
-            x_out(15)
-            h_mm(1, 0, (1, 2, 3, 0))
-            a_quant(3, both)
+            x_quant(0, 3)
             h_mm(0, 3)
-            x_quant(1, 1)
-            h_mm(1, 1)
             x_quant(1, 2)
             h_mm(1, 2)
             w_cast(0)
@@ -450,35 +448,29 @@ def tile_dora_fp8_forward_d2_kernel(tc, x_bytes, x_scale, w_bytes, w_scale, a, l
             w_inter(1, "vector", slice(0, 1))
             w_quant(0)
             w_inter(1, "vector", slice(1, 4))
-            b_inter(0, 0, "vector")
-            w_quant(1)
-            h_out(0)
-            y_mm(0, 0, group_a)
-            y_mm(0, 1, [0])
             w_cast(2)
-            w_inter(2, "vector")
-            b_inter(0, 1, "vector")
+            w_inter(2, "vector", slice(0, 1))
+            w_quant(1)
+            w_inter(2, "vector", slice(1, 4))
+            b_inter(0, 0, "vector")
             w_quant(2)
+            h_out(0)
             h_out(1, (0, 1))
-            y_mm(0, 0, [4])
-            y_mm(0, 1, [1])
-            y_mm(0, 0, [5])
-            y_mm(0, 1, [2])
+            y_mm(0, 0, [0, 1, 2, 3, 4, 5])
+            y_mm(0, 1, group_a)
             w_cast(3)
             w_inter(3, "vector")
-            b_quant(0)
+            b_inter(0, 1, "vector")
             w_quant(3)
             h_out(1, (2, 3))
-            y_mm(0, 0, [6])
-            y_mm(0, 1, [3])
-            y_mm(0, 0, [7])
+            y_mm(0, 0, [6, 7])
             y_mm(0, 1, group_b)
             y_mm(0, 2, group_a + group_b)
             y_mm(0, 3, group_a)
-            h_inter(1, 0, "vector")
             h_inter(0, 0, "scalar")
             h_inter(0, 1, "scalar")
             h_quant(0)
+            b_quant(0)
             y_mm(0, UPDATE, [0])
             y_mm(0, 3, [4])
             y_mm(0, UPDATE, [1])
@@ -489,29 +481,30 @@ def tile_dora_fp8_forward_d2_kernel(tc, x_bytes, x_scale, w_bytes, w_scale, a, l
             y_mm(0, 3, [7])
             w_cast(4)
             w_inter(4, "vector")
+            h_inter(1, 0, "scalar")
             h_inter(1, 1, "scalar")
             h_quant(1)
             y_mm(0, UPDATE, group_b)
             w_quant(4)
             b_later(1, wg[4])
-            y_out(0, [0, 1, 2, 3, 4, 5, 6])
-            y_mm(1, 0, [0, 1, 2, 3, 4, 5, 6])
+            y_out(0, [0, 1, 2, 3, 4, 5])
+            y_mm(1, 0, [0, 1, 2, 3, 4, 5])
             w_cast(5)
             w_cast(6)
             w_inter(5, "scalar")
             w_quant(5)
             y_mm(1, 1, group_a)
-            y_out(0, [7])
-            y_mm(1, 0, [7])
+            y_out(0, [6, 7])
+            y_mm(1, 0, [6, 7])
             y_mm(1, 1, group_b)
-            w_inter(6, "vector")
-            b_quant(1)
+            w_inter(6, "vector", slice(0, 2))
+            w_cast(7)
+            w_inter(7, "vector", slice(0, 1))
+            w_inter(6, "scalar", slice(2, 4))
             w_quant(6)
             y_mm(1, 2, group_a + group_b)
-            w_cast(7)
-            w_inter(7, "vector")
-            w_cast(8)
-            w_inter(8, "vector", slice(0, 1))
+            w_inter(7, "vector", slice(1, 4))
+            b_quant(1)
             w_quant(7)
             y_mm(1, 3, group_a)
             y_mm(1, UPDATE, [0])
@@ -523,9 +516,9 @@ def tile_dora_fp8_forward_d2_kernel(tc, x_bytes, x_scale, w_bytes, w_scale, a, l
             y_mm(1, UPDATE, [3])
             y_mm(1, 3, [7])
             y_mm(1, UPDATE, group_b)
-            w_inter(8, "vector", slice(1, 4))
+            w_cast(8)
+            w_inter(8, "vector")
             w_cast(9)
-            w_cast(10)
             w_inter(9, "scalar")
             w_quant(9)
             w_quant(8)
@@ -536,6 +529,7 @@ def tile_dora_fp8_forward_d2_kernel(tc, x_bytes, x_scale, w_bytes, w_scale, a, l
             y_mm(2, 0, group_b)
             y_mm(2, 1, group_b)
             b_quant(2)
+            w_cast(10)
             w_cast(11)
             w_inter(10, "scalar")
             w_quant(10)

@@ -101,9 +101,9 @@ def tile_dora_fp8_forward_d2_kernel(tc, x_bytes, x_scale, w_bytes, w_scale, a, l
         def load_w(tiles, g, cols):
             nc.sync.dma_start(out=tiles[g][:], in_=w_view[g][:, :, cols])
 
-        def load_w_later(g):
-            for c in range(1, CHUNKS):
-                nc.sync.dma_start(out=wb_later[g][:, c - 1], in_=w_view[g][:, :, CW * c : CW * (c + 1)])
+        def load_w_later(v):
+            c, g = divmod(v, PASSES)
+            nc.sync.dma_start(out=wb_later[g][:, c - 1], in_=w_view[g][:, :, CW * c : CW * (c + 1)])
 
         def load_b(tile, cols):
             for t in range(4):
@@ -405,7 +405,17 @@ def tile_dora_fp8_forward_d2_kernel(tc, x_bytes, x_scale, w_bytes, w_scale, a, l
             a_quant(1, both)
             h_mm(0, 1)
             a_inter(2, 1, "vector")
+            nc.vector.reciprocal(out=inv_norm[:], in_=norm_sb[:])
             x_widen(13)
+            nc.vector.tensor_tensor(out=gain_rows[:], in0=mag_sb[:], in1=inv_norm[:], op=MULT)
+            nc.sync.dma_start(out=out[0].rearrange("(p j) -> p j", p=64), in_=gain_rows[:])
+            load_w_later(4)
+            load_w_later(5)
+            load_w_later(6)
+            nc.sync.dma_start(out=gain[:], in_=out[0].partition_broadcast(P))
+            load_b(braw_later, later)
+            for v in range(7, W_UNITS):
+                load_w_later(v)
             x_quant(0, 2)
             x_widen(15)
             a_inter(2, 0, "scalar")
@@ -425,16 +435,7 @@ def tile_dora_fp8_forward_d2_kernel(tc, x_bytes, x_scale, w_bytes, w_scale, a, l
             a_inter(3, 1, "vector")
             x_quant(1, 1)
             h_mm(1, 1)
-            nc.vector.reciprocal(out=inv_norm[:], in_=norm_sb[:])
             a_quant(3, both)
-            nc.vector.tensor_tensor(out=gain_rows[:], in0=mag_sb[:], in1=inv_norm[:], op=MULT)
-            nc.sync.dma_start(out=out[0].rearrange("(p j) -> p j", p=64), in_=gain_rows[:])
-            load_w_later(0)
-            load_w_later(1)
-            nc.sync.dma_start(out=gain[:], in_=out[0].partition_broadcast(P))
-            load_w_later(2)
-            load_b(braw_later, later)
-            load_w_later(3)
             x_quant(0, 3)
             h_mm(0, 3)
             x_quant(1, 2)

@@ -87,7 +87,7 @@ def tile_dora_fp8_forward_d2_kernel(tc, x_bytes, x_scale, w_bytes, w_scale, a, l
         b_view = b.rearrange("(q t i) n -> t q i n", t=4, i=8)
         out_view = out.rearrange("(p i) n -> p i n", i=TILES)
 
-        nc.gpsimd.memset(lam_rows[:], 0.0)
+        nc.vector.memset(lam_rows[:], 0.0)
         make_identity(nc, ident[:])
 
         def load_x(n, tiles):
@@ -344,11 +344,12 @@ def tile_dora_fp8_forward_d2_kernel(tc, x_bytes, x_scale, w_bytes, w_scale, a, l
             nc.sync.dma_start(out=norm_sb[:], in_=norm.rearrange("(p j) -> p j", p=64))
             nc.sync.dma_start(out=mag_sb[:], in_=mag.rearrange("(p j) -> p j", p=64))
             load_w(wb_first, 0, WHOLE)
+            load_w(wb_first, 1, WHOLE)
+            load_w(wb_first, 2, WHOLE)
             ws_view = w_scale.rearrange("(g q) n -> q g n", q=4)
             for q in range(4):
                 nc.sync.dma_start(out=ws[32 * q : 32 * (q + 1), :, 0 : N // 128], in_=ws_view[q].partition_broadcast(32))
-            for g in range(1, PASSES):
-                load_w(wb_first, g, WHOLE)
+            load_w(wb_first, 3, WHOLE)
             load_b(braw_first, WHOLE)
 
             x_widen(2, "scalar")
@@ -532,9 +533,10 @@ def tile_dora_fp8_forward_d2_kernel(tc, x_bytes, x_scale, w_bytes, w_scale, a, l
             b_quant(2)
             w_cast(10)
             w_cast(11)
+            w_inter(11, "vector", slice(0, 2))
             w_inter(10, "scalar")
             w_quant(10)
-            w_inter(11, "scalar")
+            w_inter(11, "scalar", slice(2, 4))
             w_quant(11)
             c = CHUNKS - 1
             pieces = [(i, WHOLE, Y_BANK[i // 4] + i % 4, LAST_PASSES) for i in range(TILES - 1)]

from contextlib import ExitStack

import concourse.mybir as mybir
from concourse.masks import make_identity

T, K, N, R = 1024, 2048, 1536, 512
FLOPS = 2 * T * (K * N + K * R + R * N)

F32 = mybir.dt.float32
BF16 = mybir.dt.bfloat16
U32 = mybir.dt.uint32
U8 = mybir.dt.uint8
E4M3 = mybir.dt.float8_e4m3fn
MX = mybir.dt.float8_e4m3fn_x4
MULT = mybir.AluOpType.mult
ADD = mybir.AluOpType.add
COPY = mybir.ActivationFunctionType.Copy

P = 128
PASSES = K // 512
UPDATE = PASSES
TILES = T // P
CW = 512
CHUNKS = N // CW
WHOLE = slice(0, CW)
LAST_PARTS = (slice(0, 256), slice(256, 384), slice(384, 512))
X_UNITS = 4 * PASSES
W_UNITS = CHUNKS * PASSES

X_ORDER = [4 * (n // 2) + n % 2 + 2 * k for n in range(4) for k in range(2)] + list(range(8, X_UNITS))
RING = 28
LAST_PASSES = (UPDATE, 2, 3)
H_BANK = (0, 4)
Y_BANK = (0, 4)


def tile_dora_fp8_forward_d2_kernel(tc, x_bytes, x_scale, w_bytes, w_scale, a, lam, b, mag, norm, out):
    nc = tc.nc
    with ExitStack() as ctx:
        keep = ctx.enter_context(tc.tile_pool(name="keep", bufs=1))
        ring = ctx.enter_context(tc.tile_pool(name="ring", bufs=1))
        widened = ctx.enter_context(tc.tile_pool(name="widened", bufs=8))
        psum = ctx.enter_context(tc.psum_pool(name="psum", bufs=1))

        def kept(shape, dtype, name):
            return keep.tile(shape, dtype, name=name, align_bytes=64)

        taken = []

        def staged(shape, name, dtype=BF16):
            taken.append(name)
            return ring.tile(shape, dtype, name=name, tag=f"slot{len(taken) % RING}", align_bytes=64)

        def bank(n, shape, dtype=F32):
            return psum.tile(shape, dtype, name=f"bank{n}", tag=f"bank{n}")

        ident = kept([P, P], F32, "ident")
        xs = kept([P, TILES, K // 128], F32, "xs")
        ws = kept([P, PASSES, 16], F32, "ws")
        lam_rows = kept([P, P], BF16, "lam_rows")
        ident_bf = kept([P, P], BF16, "ident_bf")
        lam_cols = kept([P, 4], F32, "lam_cols")
        mag_sb = kept([64, N // 64], BF16, "mag_sb")
        norm_sb = kept([64, N // 64], BF16, "norm_sb")
        inv_norm = kept([64, N // 64], F32, "inv_norm")
        gain_rows = kept([64, N // 64], F32, "gain_rows")
        gain = kept([P, N], F32, "gain")
        xb = [staged([P, 4, K // 2], f"xb{n}", U8) for n in range(4)]
        araw = [staged([P, 4, R], f"araw{g}") for g in range(PASSES)]
        wb_first = [kept([P, 4, CW], U8, f"wb_first{g}") for g in range(PASSES)]
        wb_later = [kept([P, CHUNKS - 1, 4, CW], U8, f"wb_later{g}") for g in range(PASSES)]
        braw_first = kept([P, 4, CW], BF16, "braw_first")
        braw_later = kept([P, 4, N - CW], BF16, "braw_later")
        xq = kept([P, 2, PASSES, 512], U32, "xq")
        xqs = kept([P, 2, PASSES, 512], U8, "xqs")
        aq = kept([P, PASSES, R], U32, "aq")
        aqs = kept([P, PASSES, R], U8, "aqs")
        wq, wqs = {}, {}
        bq = [kept([P, CW], U32, f"bq{c}") for c in range(CHUNKS)]
        bqs = [kept([P, CW], U8, f"bqs{c}") for c in range(CHUNKS)]
        hq = kept([P, T], U32, "hq")
        hqs = kept([P, T], U8, "hqs")

        x_view = x_bytes.rearrange("(p i) k -> p i k", i=TILES)
        a_view = a.rearrange("(g p t) r -> g p t r", p=P, t=4)
        w_view = w_bytes.rearrange("(g p t) n -> g p t n", p=P, t=4)
        b_view = b.rearrange("(q t i) n -> t q i n", t=4, i=8)
        out_view = out.rearrange("(p i) n -> p i n", i=TILES)

        nc.vector.memset(lam_rows[:], 0.0)
        make_identity(nc, ident[:])

        def load_x(n, tiles):
            half, k = n // 2, K // 2 * (n % 2)
            rows = slice(4 * half + tiles.start, 4 * half + tiles.stop)
            nc.sync.dma_start(out=xb[n][:, tiles, :], in_=x_view[:, rows, k : k + K // 2])

        def load_a(g, ranks=slice(0, R)):
            nc.sync.dma_start(out=araw[g][:, :, ranks], in_=a_view[g][:, :, ranks])

        def load_w(tiles, g, cols):
            nc.sync.dma_start(out=tiles[g][:], in_=w_view[g][:, :, cols])

        def load_w_later(v):
            c, g = divmod(v, PASSES)
            nc.sync.dma_start(out=wb_later[g][:, c - 1], in_=w_view[g][:, :, CW * c : CW * (c + 1)])

        def load_b(tile, cols):
            for t in range(4):
                nc.sync.dma_start(out=tile[:, t, :], in_=b_view[t][:, :, cols])

        def columns(first, rest, c, start, stop):
            return first[:, :, start:stop] if c == 0 else rest[:, :, CW * (c - 1) + start : CW * (c - 1) + stop]

        def copy_on(engine, dst, src):
            if engine == "vector":
                nc.vector.tensor_copy(out=dst, in_=src)
            else:
                nc.scalar.copy(out=dst, in_=src)

        def in_runs(dst, src, run=4):
            return dst.rearrange("p (c i) t -> p c t i", i=run), src.rearrange("p t (c i) -> p c t i", i=run)

        def quantise(codes, scales, values):
            nc.vector.quantize_mx(out=codes.bitcast(MX), scales=scales, in_=values)

        xw, in_order, xbank, xg = {}, {}, {}, {}

        def x_widen(u, engine="vector"):
            half, g, j = u // 8, u % 8 // 2, u % 2
            in_order[u] = engine == "scalar"
            xw[u] = widened.tile([P, 2, 512], BF16, name="xw", align_bytes=64)
            for i in range(2):
                runs = xw[u][:, i, :].rearrange("p (h m e) -> p m h e", h=2, e=2)
                for q in range(4):
                    k = 512 * (g % 2) + 128 * q
                    codes = xb[2 * half + g // 2][:, 2 * j + i, k : k + 128].bitcast(E4M3)
                    scale = xs[:, 4 * half + 2 * j + i, 4 * g + q : 4 * g + q + 1]
                    if engine == "scalar":
                        nc.scalar.activation(
                            out=xw[u][:, i, 128 * q : 128 * (q + 1)], in_=codes, func=COPY, scale=scale
                        )
                    else:
                        nc.vector.tensor_scalar(
                            out=runs[:, 32 * q : 32 * (q + 1), :, :], in0=codes, scalar1=scale, scalar2=None, op0=MULT
                        )

        def x_turn(u, n):
            xbank[u] = bank(n, [P, 2, 2, P])
            for i in range(2):
                words = xw[u][:, i, :].bitcast(F32)
                for h in range(2):
                    src = words[:, h : 2 * P : 2] if in_order[u] else words[:, P * h : P * (h + 1)]
                    nc.tensor.transpose(xbank[u][:, i, h, :], src, ident[:])

        def x_out(u):
            if u // 2 not in xg:
                xg[u // 2] = staged([P, 2, 2, P, 4], "xg")
            words = xg[u // 2][:, u % 2].rearrange("p i r t -> p (i r t)").bitcast(F32)
            nc.scalar.copy(
                out=words.rearrange("p (i r h) -> p i r h", i=2, h=2),
                in_=xbank[u][:].rearrange("p i h r -> p i r h"),
            )

        def x_quant(half, g):
            d = PASSES * half + g
            quantise(xq[:, half, g, :], xqs[:, half, g, :], xg[d][:].rearrange("p j i r t -> p (j i r t)"))

        abank, ag, hbank, hb, hg = {}, {}, {}, {}, {}

        def a_turn(g, e, n):
            abank[g, e] = bank(n, [P, 2, 512], BF16)
            for k in range(2):
                r = 256 * e + 128 * k
                src = araw[g][:, :, r : r + 128].rearrange("p j r -> p r j")
                nc.tensor.matmul(abank[g, e][:, k, :], lhsT=ident_bf[:], rhs=src, start=True, stop=True)

        def a_out(g, e):
            if g not in ag:
                ag[g] = staged([P, 4, P, 4], "ag")
            nc.scalar.copy(
                out=ag[g][:].rearrange("p t (q i) j -> p q t (i j)", i=8)[:, 8 * e : 8 * (e + 1)],
                in_=abank[g, e][:].rearrange("p k (q t w) -> p (k q) t w", t=4, w=32),
            )

        def a_inter(g, e, engine):
            if g not in ag:
                ag[g] = staged([P, 4, P, 4], "ag")
            for t in (2 * e, 2 * e + 1):
                dst = ag[g][:, t].rearrange("p (q c i) j -> p q c j i", c=2, i=4)
                src = araw[g][:].rearrange("p j (q t c i) -> p t q c j i", t=4, c=2, i=4)[:, t]
                copy_on(engine, dst, src)

        def a_quant(g, halves):
            cols = slice(256 * halves.start, 256 * halves.stop)
            values = ag[g][:, 2 * halves.start : 2 * halves.stop].rearrange("p t m j -> p (t m j)")
            quantise(aq[:, g, cols], aqs[:, g, cols], values)

        def h_mm(half, g, ts=range(4)):
            for t in ts:
                if g == 0:
                    hbank[half, t] = bank(H_BANK[half] + t, [P, 512])
                nc.tensor.matmul_mx(
                    out=hbank[half, t][:],
                    lhsT=aq[:, g, P * t : P * (t + 1)].bitcast(MX),
                    lhsT_scale=aqs[:, g, P * t : P * (t + 1)],
                    rhs=xq[:, half, g, :].bitcast(MX),
                    rhs_scale=xqs[:, half, g, :],
                    start=(g == 0),
                    stop=(g == PASSES - 1),
                )

        def h_out(half, ts=range(4)):
            if half not in hb:
                hb[half] = staged([P, 4, 512], "hb")
            for t in ts:
                nc.scalar.activation(
                    out=hb[half][:, t, :], in_=hbank[half, t][:], func=COPY, scale=lam_cols[:, t : t + 1]
                )

        def h_inter(half, e, engine):
            if half not in hg:
                hg[half] = staged([P, 512, 4], "hg")
            n = slice(256 * e, 256 * (e + 1))
            copy_on(engine, *in_runs(hg[half][:, n, :], hb[half][:, :, n]))

        def h_quant(half):
            cols = slice(512 * half, 512 * (half + 1))
            quantise(hq[:, cols], hqs[:, cols], hg[half][:].rearrange("p n t -> p (n t)"))

        bg, cast, wg = {}, {}, {}

        def b_inter(c, e, engine):
            if (c, 0) not in bg:
                bg[c, 0] = staged([P, CW, 4], "bg")
            n = slice(256 * e, 256 * (e + 1))
            copy_on(engine, *in_runs(bg[c, 0][:, n, :], columns(braw_first, braw_later, c, n.start, n.stop)))

        def b_later(c, tile, n=WHOLE):
            bg[c, n.start] = tile
            src = columns(braw_first, braw_later, c, n.start, n.stop).rearrange("p t n -> p n t")
            nc.gpsimd.tensor_scalar(out=tile[:, n, :], in0=src, scalar1=1.0, scalar2=0.0, op0=MULT, op1=ADD)

        def b_quant(c, n=WHOLE):
            quantise(bq[c][:, n], bqs[c][:, n], bg[c, n.start][:, n, :].rearrange("p n t -> p (n t)"))

        def w_cast(v):
            c, g = divmod(v, PASSES)
            cast[v] = staged([P, 4, CW], "cast")
            codes = wb_first[g][:] if c == 0 else wb_later[g][:, c - 1]
            nc.scalar.copy(
                out=cast[v][:].rearrange("p t n -> p (t n)"), in_=codes.rearrange("p t n -> p (t n)").bitcast(E4M3)
            )

        def w_inter(v, engine, blocks=slice(0, 4)):
            c, g = divmod(v, PASSES)
            if v not in wg:
                wg[v] = staged([P, CW, 4], "wg")
            for e in range(blocks.start, blocks.stop):
                dst, src = in_runs(wg[v][:, 128 * e : 128 * (e + 1), :], cast[v][:, :, 128 * e : 128 * (e + 1)])
                scale = ws[:, g, 4 * c + e : 4 * c + e + 1]
                if engine == "vector":
                    nc.vector.tensor_scalar(out=dst, in0=src, scalar1=scale, scalar2=None, op0=MULT)
                else:
                    nc.scalar.activation(out=dst, in_=src, func=COPY, scale=scale)

        def w_quant(v):
            wq[v] = keep.tile([P, CW], U32, name=f"wq{v}", tag="wq", bufs=2 * PASSES, align_bytes=64)
            wqs[v] = keep.tile([P, CW], U8, name=f"wqs{v}", tag="wqs", bufs=2 * PASSES, align_bytes=64)
            quantise(wq[v][:], wqs[v][:], wg[v][:].rearrange("p n t -> p (n t)"))

        acc, done, res = {}, {}, {}

        def y_pass(c, g, i, part, n):
            key = (c, i, part.start)
            if key not in acc:
                acc[key] = bank(n, [P, part.stop - part.start])
                done[key] = 0
            if g == UPDATE:
                lhs, lhs_s = hq[:, P * i : P * (i + 1)], hqs[:, P * i : P * (i + 1)]
                rhs, rhs_s = bq[c], bqs[c]
            else:
                rows = slice(P * (i % 4), P * (i % 4 + 1))
                lhs, lhs_s = xq[:, i // 4, g, rows], xqs[:, i // 4, g, rows]
                rhs, rhs_s = wq[PASSES * c + g], wqs[PASSES * c + g]
            nc.tensor.matmul_mx(
                out=acc[key][:],
                lhsT=lhs.bitcast(MX),
                lhsT_scale=lhs_s,
                rhs=rhs[:, part].bitcast(MX),
                rhs_scale=rhs_s[:, part],
                start=(done[key] == 0),
                stop=(done[key] == PASSES),
            )
            done[key] = done[key] + 1

        def y_mm(c, g, tiles):
            for i in tiles:
                y_pass(c, g, i, LAST_PARTS[0] if (c, i) == (CHUNKS - 1, TILES - 1) else WHOLE, Y_BANK[i // 4] + i % 4)

        def y_scale(c, i, part):
            if (c, i // 2) not in res:
                res[c, i // 2] = staged([P, 2, CW], "res", F32)
            cols = slice(CW * c + part.start, CW * c + part.stop)
            nc.vector.tensor_tensor(
                out=res[c, i // 2][:, i % 2, part], in0=acc[c, i, part.start][:], in1=gain[:, cols], op=MULT
            )

        def y_out(c, tiles):
            for i in tiles:
                y_scale(c, i, WHOLE)
                if i % 2 == 1:
                    nc.sync.dma_start(out=out_view[:, i - 1 : i + 1, CW * c : CW * (c + 1)], in_=res[c, i // 2][:])

        group_a, group_b = [0, 1, 2, 3], [4, 5, 6, 7]
        first, second, both = slice(0, 1), slice(1, 2), slice(0, 2)
        later = slice(CW, N)

        def y_by_turns(c, g_a, g_b):
            for i, j in zip(group_a, group_b):
                y_mm(c, g_a, [i])
                y_mm(c, g_b, [j])

        with tc.manual_schedule(
            engines={mybir.EngineType.PE, mybir.EngineType.DVE, mybir.EngineType.Activation, mybir.EngineType.SP}
        ):
            nc.scalar.dma_start(out=xs[:], in_=x_scale.rearrange("(p i) k -> p i k", i=TILES))
            load_x(0, slice(0, 2))
            load_x(0, slice(2, 4))
            nc.scalar.dma_start(
                out=lam_rows[0:4, :].rearrange("t (q i) -> t q i", i=8),
                in_=lam.rearrange("(q t i) -> t q i", t=4, i=8),
            )
            nc.scalar.activation(out=ident_bf[:], in_=ident[:], func=COPY)
            load_x(1, slice(0, 2))
            load_a(0)
            load_x(1, slice(2, 4))
            load_x(2, slice(0, 2))
            load_a(1)
            load_x(2, slice(2, 4))
            load_a(2)
            load_x(3, slice(0, 4))
            load_a(3)
            nc.sync.dma_start(out=norm_sb[:], in_=norm.rearrange("(p j) -> p j", p=64))
            nc.sync.dma_start(out=mag_sb[:], in_=mag.rearrange("(p j) -> p j", p=64))
            load_w(wb_first, 0, WHOLE)
            load_w(wb_first, 1, WHOLE)
            load_w(wb_first, 2, WHOLE)
            ws_view = w_scale.rearrange("(g q) n -> q g n", q=4)
            for q in range(4):
                nc.sync.dma_start(out=ws[32 * q : 32 * (q + 1), :, 0 : N // 128], in_=ws_view[q].partition_broadcast(32))
            load_w(wb_first, 3, WHOLE)
            load_b(braw_first, WHOLE)

            x_widen(2, "scalar")
            x_widen(0)
            x_turn(0, 0)
            x_turn(2, 1)
            x_out(0)
            x_out(2)
            x_widen(1)
            x_turn(1, 2)
            x_out(1)
            x_widen(3)
            x_turn(3, 3)
            x_widen(4)
            x_turn(4, 4)
            x_widen(6)
            x_turn(6, 5)
            x_widen(5)
            x_turn(5, 6)
            x_widen(7)
            x_turn(7, 7)
            a_turn(1, 0, 0)
            a_turn(1, 1, 1)
            lam_turned = bank(2, [P, P], BF16)
            nc.tensor.transpose(lam_turned[:], lam_rows[:], ident_bf[:])
            x_widen(8)
            x_widen(10)
            x_quant(0, 0)
            x_widen(9)
            a_inter(0, 0, "scalar")
            x_out(3)
            x_turn(8, 3)
            a_inter(0, 1, "scalar")
            x_out(4)
            x_turn(10, 4)
            x_out(6)
            x_turn(9, 5)
            x_out(5)
            x_out(7)
            a_out(1, 0)
            a_out(1, 1)
            nc.scalar.copy(out=lam_cols[:], in_=lam_turned[:, 0:4])
            x_out(8)
            x_out(10)
            a_quant(0, both)
            x_widen(11)
            x_turn(11, 6)
            h_mm(0, 0)
            x_widen(12)
            x_turn(12, 7)
            x_quant(0, 1)
            x_widen(14)
            x_turn(14, 4)
            a_quant(1, both)
            h_mm(0, 1)
            a_inter(2, 1, "vector")
            nc.vector.reciprocal(out=inv_norm[:], in_=norm_sb[:])
            x_widen(13)
            nc.vector.tensor_tensor(out=gain_rows[:], in0=mag_sb[:], in1=inv_norm[:], op=MULT)
            nc.sync.dma_start(out=out[0].rearrange("(p j) -> p j", p=64), in_=gain_rows[:])
            load_w_later(4)
            load_w_later(5)
            load_w_later(6)
            nc.sync.dma_start(out=gain[:], in_=out[0].partition_broadcast(P))
            load_b(braw_later, later)
            for v in range(7, W_UNITS):
                load_w_later(v)
            x_quant(0, 2)
            x_widen(15)
            a_inter(2, 0, "scalar")
            x_out(9)
            x_turn(13, 5)
            x_out(11)
            x_turn(15, 6)
            x_out(12)
            x_out(14)
            x_out(13)
            x_out(15)
            a_quant(2, both)
            h_mm(0, 2)
            a_inter(3, 0, "vector")
            x_quant(1, 0)
            h_mm(1, 0, (3, 0, 1, 2))
            a_inter(3, 1, "vector")
            x_quant(1, 1)
            h_mm(1, 1)
            a_quant(3, both)
            x_quant(0, 3)
            h_mm(0, 3)
            x_quant(1, 2)
            h_mm(1, 2)
            w_cast(0)
            w_inter(0, "vector", slice(0, 2))
            x_quant(1, 3)
            h_mm(1, 3)
            w_inter(0, "vector", slice(2, 4))
            w_cast(1)
            w_inter(1, "vector", slice(0, 1))
            w_quant(0)
            w_inter(1, "vector", slice(1, 4))
            w_cast(2)
            w_inter(2, "vector", slice(0, 1))
            w_quant(1)
            w_inter(2, "vector", slice(1, 4))
            b_inter(0, 0, "vector")
            w_quant(2)
            h_out(0)
            h_out(1, (0, 1))
            y_mm(0, 0, [0, 1, 2, 3, 4, 5])
            y_mm(0, 1, group_a)
            w_cast(3)
            w_inter(3, "vector")
            b_inter(0, 1, "vector")
            w_quant(3)
            h_out(1, (2, 3))
            y_mm(0, 0, [6, 7])
            y_mm(0, 1, group_b)
            y_mm(0, 2, group_a + group_b)
            y_mm(0, 3, group_a)
            h_inter(0, 0, "scalar")
            h_inter(0, 1, "scalar")
            h_quant(0)
            b_quant(0)
            y_mm(0, UPDATE, [0])
            y_mm(0, 3, [4])
            y_mm(0, UPDATE, [1])
            y_mm(0, 3, [5])
            y_mm(0, UPDATE, [2])
            y_mm(0, 3, [6])
            y_mm(0, UPDATE, [3])
            y_mm(0, 3, [7])
            w_cast(4)
            w_inter(4, "vector")
            h_inter(1, 0, "scalar")
            h_inter(1, 1, "scalar")
            h_quant(1)
            y_mm(0, UPDATE, group_b)
            w_quant(4)
            b_later(1, wg[4])
            y_out(0, [0, 1, 2, 3, 4, 5])
            y_mm(1, 0, [0, 1, 2, 3, 4, 5])
            w_cast(5)
            w_cast(6)
            w_inter(5, "scalar")
            w_quant(5)
            y_mm(1, 1, group_a)
            y_out(0, [6, 7])
            y_mm(1, 0, [6, 7])
            y_mm(1, 1, group_b)
            w_inter(6, "vector", slice(0, 2))
            w_cast(7)
            w_inter(7, "vector", slice(0, 1))
            w_inter(6, "scalar", slice(2, 4))
            w_quant(6)
            y_mm(1, 2, group_a + group_b)
            w_inter(7, "vector", slice(1, 4))
            b_quant(1)
            w_quant(7)
            y_mm(1, 3, group_a)
            y_mm(1, UPDATE, [0])
            y_mm(1, 3, [4])
            y_mm(1, UPDATE, [1])
            y_mm(1, 3, [5])
            y_mm(1, UPDATE, [2])
            y_mm(1, 3, [6])
            y_mm(1, UPDATE, [3])
            y_mm(1, 3, [7])
            y_mm(1, UPDATE, group_b)
            w_cast(8)
            w_inter(8, "vector")
            w_cast(9)
            w_inter(9, "scalar")
            w_quant(9)
            w_quant(8)
            b_later(2, wg[8])
            y_out(1, [0, 1, 2, 3, 4, 5, 6, 7])
            y_mm(2, 0, group_a)
            y_mm(2, 1, group_a)
            y_mm(2, 0, group_b)
            y_mm(2, 1, group_b)
            b_quant(2)
            w_cast(10)
            w_cast(11)
            w_inter(11, "vector", slice(0, 2))
            w_inter(10, "scalar")
            w_quant(10)
            w_inter(11, "scalar", slice(2, 4))
            w_quant(11)
            c = CHUNKS - 1
            pieces = [(i, WHOLE, Y_BANK[i // 4] + i % 4, LAST_PASSES) for i in range(TILES - 1)]
            pieces.append((TILES - 1, LAST_PARTS[0], Y_BANK[1] + 3, LAST_PASSES))
            pieces.extend((TILES - 1, part, Y_BANK[0] + n, range(PASSES + 1)) for n, part in enumerate(LAST_PARTS[1:]))
            for i, part, n, passes in pieces:
                for g in passes:
                    y_pass(c, g, i, part, n)
                y_scale(c, i, part)
                nc.sync.dma_start(
                    out=out_view[:, i, CW * c + part.start : CW * c + part.stop], in_=res[c, i // 2][:, i % 2, part]
                )
